import numpy as np
import ml_dtypes


def mxq(x, axis, fmt="e4m3"):
    dtype, down = {"e4m3": (ml_dtypes.float8_e4m3fn, 7), "e5m2": (ml_dtypes.float8_e5m2, 14)}[fmt]
    v = np.moveaxis(np.asarray(x, np.float32).astype(ml_dtypes.bfloat16).astype(np.float64), axis, -1)
    blocks = v.reshape(v.shape[:-1] + (-1, 32))
    amax = np.abs(blocks).max(-1, keepdims=True)
    byte = np.maximum(np.where(amax > 0, np.frexp(amax)[1] - 1 + 127, 0) - down, 1)
    scale = np.exp2(byte - 127.0)
    codes = (blocks / scale).astype(np.float32).astype(dtype).astype(np.float64)
    return np.moveaxis((codes * scale).reshape(v.shape), -1, axis)


WIDE = False


def mx_kscale(k):
    if not WIDE:
        return np.ones(k)
    levels = np.array([10, -10, 5, -5, 0])
    if k % 512:
        return np.exp2(np.random.permutation(np.resize(levels, k // 32))).repeat(32)
    a = np.empty((k // 512, 16))
    for p in range(k // 512):
        a[p, :8] = np.random.permutation(np.resize(levels, 8))
        for g in range(8):
            far = levels[np.abs(levels - a[p, g]) >= 10]
            a[p, g + 8] = far[np.random.randint(len(far))]
    return np.exp2(a.ravel()).repeat(32)


def f64(x):
    return np.asarray(x).astype(np.float64)


def striped(idx):
    return np.tile(idx.reshape(-1, 16).T, (8, 1)).astype(np.uint16)


def unstriped(offs):
    return offs[:16].T.reshape(-1).astype(np.int64)


E2M1 = np.array([0.0, 0.5, 1.0, 1.5, 2.0, 3.0, 4.0, 6.0, -0.0, -0.5, -1.0, -1.5, -2.0, -3.0, -4.0, -6.0])


def pack_weight(w, fmt):
    k, n = w.shape
    w = f64(np.asarray(w, np.float32).astype(ml_dtypes.bfloat16)).reshape(k // 32, 32, n)
    amax = np.abs(w).max(1)
    if fmt == "e4m3":
        byte = np.frexp(amax)[1] - 1 + 127 - 7
    else:
        mant, ex = np.frexp(amax / 6.0)
        byte = np.where(mant > 0.5, ex, ex - 1) + 127
    byte = np.clip(np.where(amax > 0, byte, 1), 1, 254)
    scaled = (w * np.exp2(127.0 - byte)[:, None, :]).reshape(k, n).astype(np.float32)
    by_word = np.ascontiguousarray(scaled.reshape(k // 512, 128, 4, n).transpose(0, 1, 3, 2))
    if fmt == "e4m3":
        words = by_word.astype(ml_dtypes.float8_e4m3fn).view(np.uint8)
    else:
        c = by_word.astype(ml_dtypes.float4_e2m1fn).view(np.uint8) & 0xF
        words = (c[..., 0::2] | (c[..., 1::2] << 4)).reshape(k // 512, 128, 2 * n)
    return np.ascontiguousarray(words), np.ascontiguousarray(byte.astype(np.uint8).reshape(k // 512, 16, n))


def unpack_weight(words, scales, fmt):
    g, _, n = scales.shape
    words = np.ascontiguousarray(words).reshape(g, 128, n, -1)
    if fmt == "e4m3":
        vals = words.view(ml_dtypes.float8_e4m3fn).astype(np.float64)
    else:
        nib = np.empty((g, 128, n, 4), np.uint8)
        nib[..., 0::2] = words & 0xF
        nib[..., 1::2] = words >> 4
        vals = E2M1[nib]
    vals = vals * np.repeat(np.exp2(scales.astype(np.float64) - 127.0), 8, axis=1)[..., None]
    return vals.transpose(0, 1, 3, 2).reshape(g * 512, n)


def gelu(v):
    return 0.5 * v * (1.0 + np.tanh(np.sqrt(2.0 / np.pi) * (v + 0.044715 * v**3)))


K, T, S, H, P, N, P2 = 1024, 2048, 1024, 1024, 512, 512, 256

def setup_inputs():
    n = np.random.standard_normal
    s = mx_kscale(K)[:, None]
    u = mx_kscale(H)[:, None]
    tab_words, tab_scales = pack_weight(n((K, T)) * s, "e4m3")
    w4_words, w4_scales = pack_weight(n((H, N)) / np.sqrt(H) / u, "e2m1")
    return {
        "tab_words": tab_words, "tab_scales": tab_scales,
        "offs": striped(np.random.permutation(T)[:S]),
        "w1": (n((K, H)) / np.sqrt(K) / s * u.T).astype(np.float32),
        "b1": (0.5 * n(H) * u[:, 0]).astype(np.float32),
        "pos1": striped(np.random.permutation(S)[:P]),
        "pos2": striped(np.random.permutation(S)[:P]),
        "w4_words": w4_words, "w4_scales": w4_scales,
        "pos3": striped(np.random.permutation(P)[:P2]),
        "pos4": striped(np.random.permutation(P)[:P2]),
        "gn": np.random.uniform(0.3, 1.0, N).astype(np.float32),
    }

def reference(tab_words, tab_scales, offs, w1, b1, pos1, pos2, w4_words, w4_scales, pos3, pos4, gn):
    v = unpack_weight(tab_words, tab_scales, "e4m3")[:, unstriped(offs)]
    h = (mxq(f64(w1), 0, "e4m3").T @ v) + f64(b1)[:, None]
    left = h[:, unstriped(pos1)]
    right = h[:, unstriped(pos2)]
    z = left - np.maximum(right, 0.0)
    w4 = unpack_weight(w4_words, w4_scales, "e2m1")
    y = w4.T @ mxq(z, 0, "e4m3")
    both = y[:, unstriped(pos3)] * y[:, unstriped(pos4)]
    return np.tanh(f64(gn)[:, None] * both)

@@ -1,0 +1,261 @@
+from contextlib import ExitStack
+
+import concourse.mybir as mybir
+
+K, T, S, H, PAIRS, N, LINES = 1024, 2048, 1024, 1024, 512, 512, 256
+FLOPS = 2 * K * H * S + 2 * H * N * PAIRS
+
+F32 = mybir.dt.float32
+BF16 = mybir.dt.bfloat16
+I32 = mybir.dt.int32
+U32 = mybir.dt.uint32
+U16 = mybir.dt.uint16
+U8 = mybir.dt.uint8
+FP8X4 = mybir.dt.float8_e4m3fn_x4
+FP4X4 = mybir.dt.float4_e2m1fn_x4
+ACT = mybir.ActivationFunctionType
+ALU = mybir.AluOpType
+
+P = 128
+PACK = 4
+PASS = P * PACK
+BANK = 512
+
+
+def tile_list_precedent_ladder_kernel(
+    tc, tab_words, tab_scales, offs, w1, b1, pos1, pos2, w4_words, w4_scales, pos3, pos4, gn, out
+):
+    nc = tc.nc
+    with ExitStack() as ctx:
+        lists = ctx.enter_context(tc.tile_pool(name="lists", bufs=1))
+        keep = ctx.enter_context(tc.tile_pool(name="keep", bufs=1))
+        ring = ctx.enter_context(tc.tile_pool(name="ring", bufs=3))
+        h_psum = ctx.enter_context(tc.psum_pool(name="h_psum", bufs=4))
+        y_psum = ctx.enter_context(tc.psum_pool(name="y_psum", bufs=1))
+
+        def load_list(src, name):
+            t = lists.tile(list(src.shape), U16, name=name)
+            nc.sync.dma_start(t[:], src)
+            return t
+
+        def load_w1(b, a, c0, width):
+            raw = keep.tile([P, PACK, width], F32, name=f"w1_raw_{b}_{a}_{c0}")
+            rows = w1[a * PASS : (a + 1) * PASS, b * PASS + c0 : b * PASS + c0 + width]
+            nc.sync.dma_start(raw[:], rows.rearrange("(p j) c -> p j c", j=PACK))
+            return raw
+
+        def load_table(a):
+            t = keep.tile([P, T], I32, name=f"tab_w{a}")
+            nc.sync.dma_start(t[:], tab_words[a].rearrange("p t i -> p (t i)").bitcast(I32))
+            return t
+
+        tab_s = keep.tile([P, T], U8, name="tab_s")
+        w4_s = keep.tile([P, 2, N], U8, name="w4_s", align_bytes=64)
+        nc.vector.memset(tab_s[:].bitcast(I32), 0)
+        nc.vector.memset(w4_s[:].bitcast(I32), 0)
+        for q in range(4):
+            nc.scalar.dma_start(
+                tab_s[32 * q : 32 * q + 8, :].bitcast(I32), tab_scales[:, 4 * q : 4 * q + 4, :].bitcast(I32)
+            )
+        tab_w = [load_table(0)]
+        idx = load_list(offs, "idx")
+        raw00 = load_w1(0, 0, 0, PASS)
+        tab_w.append(load_table(1))
+        raw01 = [load_w1(0, 1, 0, PASS // 2), load_w1(0, 1, PASS // 2, PASS // 2)]
+        bias = keep.tile([P, 2, PACK], F32, name="bias")
+        nc.sync.dma_start(bias[:], b1.rearrange("(b p t) -> p b t", b=2, t=PACK))
+        p2 = load_list(pos2, "p2")
+        p1 = load_list(pos1, "p1")
+        raw1 = [load_w1(1, 0, 0, PASS), load_w1(1, 1, 0, PASS)]
+        w4_w = keep.tile([P, 2, 2 * N], U8, name="w4_w", align_bytes=64)
+        nc.sync.dma_start(w4_w[:].bitcast(I32), w4_words.rearrange("a p c -> p a c").bitcast(I32))
+        for q in range(4):
+            nc.sync.dma_start(
+                w4_s[32 * q : 32 * q + 4, :, :].bitcast(I32),
+                w4_scales[:, 4 * q : 4 * q + 4, :].rearrange("a r c -> r a c").bitcast(I32),
+            )
+        p3 = load_list(pos3, "p3")
+        p4 = load_list(pos4, "p4")
+        gain = keep.tile([P, N // P], F32, name="gain")
+        with nc.allow_non_contiguous_dma(reason="one gain a partition"):
+            nc.sync.dma_start(gain[:], gn.rearrange("(i p) -> p i", p=P))
+
+        v_w = [keep.tile([P, S], U32, name=f"v_w{a}", align_bytes=64) for a in range(2)]
+        v_s = keep.tile([P, S], U8, name="v_s", align_bytes=64)
+
+        w_bf = {}
+        w_code = {}
+        w_scale = {}
+        for b in range(2):
+            for a in range(2):
+                w_bf[b, a] = keep.tile([P, PACK, P, PACK], BF16, name=f"w_bf{b}{a}", align_bytes=64)
+                w_code[b, a] = keep.tile([P, PASS], U32, name=f"w_code{b}{a}", align_bytes=64)
+                w_scale[b, a] = keep.tile([P, PASS], U8, name=f"w_scale{b}{a}", align_bytes=64)
+
+        def round_w1(copy, b, a, raw, m0, t0, t1):
+            m1 = m0 + raw.shape[2] // PACK
+            copy(
+                out=w_bf[b, a][:, t0:t1, m0:m1, :].rearrange("p t m j -> p m j t"),
+                in_=raw[:].rearrange("p j (m t) -> p m j t", t=PACK)[:, :, :, t0:t1],
+            )
+
+        def quantize_w1(b, a, t0, t1):
+            nc.vector.quantize_mx(
+                out=w_code[b, a][:, t0 * P : t1 * P].bitcast(FP8X4),
+                scales=w_scale[b, a][:, t0 * P : t1 * P],
+                in_=w_bf[b, a][:, t0:t1, :, :].rearrange("p t m j -> p (t m j)"),
+            )
+
+        h = {}
+
+        def make_h(b, t, split):
+            banks = [h_psum.tile([P, BANK], F32, name="h_bank") for half in range(2)]
+            for a in range(2):
+                for half in range(2):
+                    cols = slice(half * BANK, (half + 1) * BANK)
+                    nc.tensor.matmul_mx(
+                        out=banks[half][:],
+                        lhsT=w_code[b, a][:, t * P : (t + 1) * P].bitcast(FP8X4),
+                        lhsT_scale=w_scale[b, a][:, t * P : (t + 1) * P],
+                        rhs=v_w[a][:, cols].bitcast(FP8X4),
+                        rhs_scale=v_s[4 * a : P, cols],
+                        start=(a == 0),
+                        stop=(a == 1),
+                    )
+            h[b, t] = keep.tile([P, S], F32, name=f"h{b}{t}")
+            nc.scalar.activation(h[b, t][:, 0:BANK], banks[0][:], ACT.Identity, bias=bias[:, b, t : t + 1])
+            if split:
+                nc.vector.tensor_scalar(
+                    h[b, t][:, BANK:S], banks[1][:], bias[:, b, t : t + 1], None, op0=ALU.add
+                )
+            else:
+                nc.scalar.activation(h[b, t][:, BANK:S], banks[1][:], ACT.Identity, bias=bias[:, b, t : t + 1])
+
+        right = {}
+
+        def gather_right(b, t):
+            picked = ring.tile([P, PAIRS], F32, name="picked")
+            nc.vector.tensor_copy(picked[:], h[b, t][:].indirect(p2[:]))
+            right[b, t] = keep.tile([P, PAIRS], F32, name=f"right{b}{t}")
+            nc.scalar.activation(right[b, t][:], picked[:], ACT.Relu)
+
+        z32 = {}
+
+        def gather_left(b, t, c0, c1):
+            if (b, c0) not in z32:
+                z32[b, c0] = keep.tile([P, PACK, c1 - c0], F32, name=f"z32_{b}_{c0}")
+            nc.vector.tensor_tensor(
+                z32[b, c0][:, t, :],
+                h[b, t][:].indirect(p1[:, c0 // 16 : c1 // 16]),
+                right[b, t][:, c0:c1],
+                ALU.subtract,
+            )
+
+        z_bf = {}
+
+        def round_z(copy, b, c0):
+            width = z32[b, c0].shape[2]
+            z_bf[b, c0] = keep.tile([P, width * PACK], BF16, name=f"z_bf{b}_{c0}", align_bytes=64)
+            copy(
+                out=z_bf[b, c0][:].rearrange("p (c i t) -> p c t i", i=4, t=PACK),
+                in_=z32[b, c0][:].rearrange("p t (c i) -> p c t i", i=4),
+            )
+
+        y_banks = [y_psum.tile([P, PAIRS], F32, name=f"y_bank{i}") for i in range(N // P)]
+
+        def multiply_z(b, c0):
+            width = z32[b, c0].shape[2]
+            codes = keep.tile([P, width], U32, name=f"z_code{b}_{c0}", align_bytes=64)
+            scales = keep.tile([P, width], U8, name=f"z_scale{b}_{c0}", align_bytes=64)
+            nc.vector.quantize_mx(out=codes[:].bitcast(FP8X4), scales=scales[:], in_=z_bf[b, c0][:])
+            n = width if width == BANK else P
+            for i in range(N // P):
+                for c in range(0, width, n):
+                    nc.tensor.matmul_mx(
+                        out=y_banks[i][:, c0 + c : c0 + c + n],
+                        lhsT=w4_w[:, b, 2 * P * i : 2 * P * (i + 1)].bitcast(FP4X4),
+                        lhsT_scale=w4_s[:, b, P * i : P * (i + 1)],
+                        rhs=codes[:, c : c + n].bitcast(FP8X4),
+                        rhs_scale=scales[:, c : c + n],
+                        start=(b == 0),
+                        stop=(b == 1 and c0 + c + n == PAIRS),
+                    )
+
+        nc.vector.tensor_copy(v_w[0][:], tab_w[0][:].bitcast(U32).indirect(idx[:]))
+        round_w1(nc.scalar.copy, 0, 0, raw00, 0, 0, PACK)
+        nc.vector.tensor_copy(v_s[:], tab_s[:].indirect(idx[:]))
+        nc.vector.tensor_copy(v_w[1][:], tab_w[1][:].bitcast(U32).indirect(idx[:]))
+        round_w1(nc.scalar.copy, 0, 1, raw01[0], 0, 0, PACK)
+        quantize_w1(0, 0, 0, 1)
+        round_w1(nc.vector.tensor_copy, 0, 1, raw01[1], P // 2, 0, 2)
+        round_w1(nc.scalar.copy, 0, 1, raw01[1], P // 2, 2, PACK)
+        quantize_w1(0, 0, 1, 2)
+        quantize_w1(0, 1, 0, 1)
+        quantize_w1(0, 1, 1, 2)
+        quantize_w1(0, 0, 2, PACK)
+        quantize_w1(0, 1, 2, PACK)
+
+        make_h(0, 0, True)
+        make_h(0, 1, False)
+        gather_right(0, 0)
+        make_h(0, 2, False)
+        gather_right(0, 1)
+        round_w1(nc.scalar.copy, 1, 0, raw1[0], 0, 0, PACK)
+        gather_left(0, 0, 0, PAIRS)
+        gather_right(0, 2)
+        make_h(0, 3, False)
+        gather_left(0, 1, 0, PAIRS)
+        round_w1(nc.scalar.copy, 1, 1, raw1[1], 0, 0, PACK)
+        quantize_w1(1, 0, 0, PACK)
+        gather_right(0, 3)
+        gather_left(0, 2, 0, PAIRS)
+        quantize_w1(1, 1, 0, PACK)
+        gather_left(0, 3, 0, PAIRS)
+        make_h(1, 0, False)
+        make_h(1, 1, False)
+        gather_right(1, 0)
+        make_h(1, 2, False)
+        gather_right(1, 1)
+        make_h(1, 3, False)
+        half, quarter = PAIRS // 2, PAIRS // 4
+        gather_left(1, 0, 0, half)
+        gather_right(1, 2)
+        round_z(nc.scalar.copy, 0, 0)
+        gather_left(1, 1, 0, half)
+        gather_right(1, 3)
+        gather_left(1, 2, 0, half)
+        multiply_z(0, 0)
+        gather_left(1, 3, 0, half)
+        round_z(nc.scalar.copy, 1, 0)
+        for t in range(PACK):
+            gather_left(1, t, half, half + quarter)
+        round_z(nc.scalar.copy, 1, half)
+        multiply_z(1, 0)
+        for t in range(PACK):
+            gather_left(1, t, half + quarter, PAIRS)
+        multiply_z(1, half)
+        round_z(nc.vector.tensor_copy, 1, half + quarter)
+        multiply_z(1, half + quarter)
+
+        y = []
+        for i in range(N // P):
+            y.append(keep.tile([P, PAIRS], F32, name=f"y{i}"))
+            nc.scalar.copy(y[i][:], y_banks[i][:])
+        first = {}
+
+        def gather_first(i):
+            first[i] = keep.tile([P, LINES], F32, name=f"first{i}")
+            nc.vector.tensor_copy(first[i][:], y[i][:].indirect(p3[:]))
+
+        def finish(i):
+            both = keep.tile([P, LINES], F32, name=f"both{i}")
+            nc.vector.tensor_tensor(both[:], y[i][:].indirect(p4[:]), first[i][:], ALU.mult)
+            result = keep.tile([P, LINES], F32, name=f"result{i}")
+            nc.scalar.activation(result[:], both[:], ACT.Tanh, scale=gain[:, i : i + 1])
+            nc.sync.dma_start(out[i * P : (i + 1) * P, :], result[:])
+
+        gather_first(0)
+        for i in range(1, N // P):
+            gather_first(i)
+            finish(i - 1)
+        finish(N // P - 1)

@@ -20,6 +20,7 @@ P = 128
 PACK = 4
 PASS = P * PACK
 BANK = 512
+F32_MAX = 3.4028234663852886e38
 
 
 def tile_list_precedent_ladder_kernel(
@@ -29,9 +30,7 @@ def tile_list_precedent_ladder_kernel(
     with ExitStack() as ctx:
         lists = ctx.enter_context(tc.tile_pool(name="lists", bufs=1))
         keep = ctx.enter_context(tc.tile_pool(name="keep", bufs=1))
-        ring = ctx.enter_context(tc.tile_pool(name="ring", bufs=3))
-        h_psum = ctx.enter_context(tc.psum_pool(name="h_psum", bufs=4))
-        y_psum = ctx.enter_context(tc.psum_pool(name="y_psum", bufs=1))
+        psum = ctx.enter_context(tc.psum_pool(name="psum", bufs=1))
 
         def load_list(src, name):
             t = lists.tile(list(src.shape), U16, name=name)
@@ -52,18 +51,17 @@ def tile_list_precedent_ladder_kernel(
         tab_s = keep.tile([P, T], U8, name="tab_s")
         w4_s = keep.tile([P, 2, N], U8, name="w4_s", align_bytes=64)
         nc.vector.memset(tab_s[:].bitcast(I32), 0)
-        nc.vector.memset(w4_s[:].bitcast(I32), 0)
         for q in range(4):
-            nc.scalar.dma_start(
+            nc.sync.dma_start(
                 tab_s[32 * q : 32 * q + 8, :].bitcast(I32), tab_scales[:, 4 * q : 4 * q + 4, :].bitcast(I32)
             )
         tab_w = [load_table(0)]
         idx = load_list(offs, "idx")
         raw00 = load_w1(0, 0, 0, PASS)
-        tab_w.append(load_table(1))
-        raw01 = [load_w1(0, 1, 0, PASS // 2), load_w1(0, 1, PASS // 2, PASS // 2)]
         bias = keep.tile([P, 2, PACK], F32, name="bias")
         nc.sync.dma_start(bias[:], b1.rearrange("(b p t) -> p b t", b=2, t=PACK))
+        tab_w.append(load_table(1))
+        raw01 = [load_w1(0, 1, 0, PASS // 2), load_w1(0, 1, PASS // 2, PASS // 2)]
         p2 = load_list(pos2, "p2")
         p1 = load_list(pos1, "p1")
         raw1 = [load_w1(1, 0, 0, PASS), load_w1(1, 1, 0, PASS)]
@@ -87,36 +85,41 @@ def tile_list_precedent_ladder_kernel(
         w_code = {}
         w_scale = {}
         for b in range(2):
-            for a in range(2):
-                w_bf[b, a] = keep.tile([P, PACK, P, PACK], BF16, name=f"w_bf{b}{a}", align_bytes=64)
-                w_code[b, a] = keep.tile([P, PASS], U32, name=f"w_code{b}{a}", align_bytes=64)
-                w_scale[b, a] = keep.tile([P, PASS], U8, name=f"w_scale{b}{a}", align_bytes=64)
+            for u in range(2):
+                w_code[b, u] = keep.tile([P, 4 * P], U32, name=f"w_code{b}{u}", align_bytes=64)
+                w_scale[b, u] = keep.tile([P, 4 * P], U8, name=f"w_scale{b}{u}", align_bytes=64)
 
-        def round_w1(copy, b, a, raw, m0, t0, t1):
-            m1 = m0 + raw.shape[2] // PACK
+        def round_w1(copy, b, u, a, raw, m0, c0=0, width=None):
+            width = width or raw.shape[2]
+            if (b, u) not in w_bf:
+                tag = f"picked0{u}" if b == 1 else f"w_bf{b}{u}"
+                w_bf[b, u] = keep.tile([P, 2, 2, P, PACK], BF16, name=f"w_bf{b}{u}", tag=tag, align_bytes=64)
+            m1 = m0 + width // PACK
             copy(
-                out=w_bf[b, a][:, t0:t1, m0:m1, :].rearrange("p t m j -> p m j t"),
-                in_=raw[:].rearrange("p j (m t) -> p m j t", t=PACK)[:, :, :, t0:t1],
+                out=w_bf[b, u][:, a, :, m0:m1, :].rearrange("p t m j -> p m j t"),
+                in_=raw[:, :, c0 : c0 + width].rearrange("p j (m t) -> p m j t", t=PACK)[:, :, :, 2 * u : 2 * u + 2],
             )
 
-        def quantize_w1(b, a, t0, t1):
+        def quantize_w1(b, u, s0, s1):
             nc.vector.quantize_mx(
-                out=w_code[b, a][:, t0 * P : t1 * P].bitcast(FP8X4),
-                scales=w_scale[b, a][:, t0 * P : t1 * P],
-                in_=w_bf[b, a][:, t0:t1, :, :].rearrange("p t m j -> p (t m j)"),
+                out=w_code[b, u][:, s0 * P : s1 * P].bitcast(FP8X4),
+                scales=w_scale[b, u][:, s0 * P : s1 * P],
+                in_=w_bf[b, u][:].rearrange("p a t m j -> p (a t m j)")[:, s0 * PASS : s1 * PASS],
             )
 
         h = {}
 
         def make_h(b, t, split):
-            banks = [h_psum.tile([P, BANK], F32, name="h_bank") for half in range(2)]
+            first_bank = 2 * t
+            banks = [psum.tile([P, BANK], F32, name=f"bank{first_bank + half}") for half in range(2)]
             for a in range(2):
+                w_cols = slice((2 * a + t % 2) * P, (2 * a + t % 2 + 1) * P)
                 for half in range(2):
                     cols = slice(half * BANK, (half + 1) * BANK)
                     nc.tensor.matmul_mx(
                         out=banks[half][:],
-                        lhsT=w_code[b, a][:, t * P : (t + 1) * P].bitcast(FP8X4),
-                        lhsT_scale=w_scale[b, a][:, t * P : (t + 1) * P],
+                        lhsT=w_code[b, t // 2][:, w_cols].bitcast(FP8X4),
+                        lhsT_scale=w_scale[b, t // 2][:, w_cols],
                         rhs=v_w[a][:, cols].bitcast(FP8X4),
                         rhs_scale=v_s[4 * a : P, cols],
                         start=(a == 0),
@@ -132,18 +135,25 @@ def tile_list_precedent_ladder_kernel(
                 nc.scalar.activation(h[b, t][:, BANK:S], banks[1][:], ACT.Identity, bias=bias[:, b, t : t + 1])
 
         right = {}
+        picked = {}
 
         def gather_right(b, t):
-            picked = ring.tile([P, PAIRS], F32, name="picked")
-            nc.vector.tensor_copy(picked[:], h[b, t][:].indirect(p2[:]))
+            picked[b, t] = keep.tile([P, PAIRS], F32, name=f"picked{b}{t}", tag=f"picked{b}{t}", align_bytes=64)
+            nc.vector.tensor_copy(picked[b, t][:], h[b, t][:].indirect(p2[:]))
+
+        def positive_part(b, t, on_scalar=False):
             right[b, t] = keep.tile([P, PAIRS], F32, name=f"right{b}{t}")
-            nc.scalar.activation(right[b, t][:], picked[:], ACT.Relu)
+            if on_scalar:
+                nc.scalar.activation(right[b, t][:], picked[b, t][:], ACT.Relu)
+            else:
+                nc.gpsimd.tensor_scalar(right[b, t][:], picked[b, t][:], F32_MAX, 0.0, op0=ALU.min, op1=ALU.max)
 
         z32 = {}
 
         def gather_left(b, t, c0, c1):
             if (b, c0) not in z32:
-                z32[b, c0] = keep.tile([P, PACK, c1 - c0], F32, name=f"z32_{b}_{c0}")
+                tag = TAGS.get((b, c0), f"z32_{b}_{c0}")
+                z32[b, c0] = keep.tile([P, PACK, c1 - c0], F32, name=f"z32_{b}_{c0}", tag=tag, align_bytes=64)
             nc.vector.tensor_tensor(
                 z32[b, c0][:, t, :],
                 h[b, t][:].indirect(p1[:, c0 // 16 : c1 // 16]),
@@ -155,92 +165,110 @@ def tile_list_precedent_ladder_kernel(
 
         def round_z(copy, b, c0):
             width = z32[b, c0].shape[2]
-            z_bf[b, c0] = keep.tile([P, width * PACK], BF16, name=f"z_bf{b}_{c0}", align_bytes=64)
+            if b == 1:
+                z_bf[b, c0] = keep.tile([P, width * PACK], BF16, name=f"z_bf{b}_{c0}", align_bytes=64)
+                dst = z_bf[b, c0][:]
+            else:
+                if c0 == 0:
+                    z_bf[b, 0] = keep.tile([P, PAIRS * PACK], BF16, name="z_bf0", tag=ZTAG, align_bytes=64)
+                dst = z_bf[b, 0][:, c0 * PACK : (c0 + width) * PACK]
             copy(
-                out=z_bf[b, c0][:].rearrange("p (c i t) -> p c t i", i=4, t=PACK),
+                out=dst.rearrange("p (c i t) -> p c t i", i=4, t=PACK),
                 in_=z32[b, c0][:].rearrange("p t (c i) -> p c t i", i=4),
             )
 
-        y_banks = [y_psum.tile([P, PAIRS], F32, name=f"y_bank{i}") for i in range(N // P)]
+        y_banks = []
+        y_last = []
 
         def multiply_z(b, c0):
-            width = z32[b, c0].shape[2]
+            width = z_bf[b, c0].shape[1] // PACK
             codes = keep.tile([P, width], U32, name=f"z_code{b}_{c0}", align_bytes=64)
             scales = keep.tile([P, width], U8, name=f"z_scale{b}_{c0}", align_bytes=64)
             nc.vector.quantize_mx(out=codes[:].bitcast(FP8X4), scales=scales[:], in_=z_bf[b, c0][:])
-            n = width if width == BANK else P
+            if b == 0:
+                y_banks.extend(psum.tile([P, PAIRS - P], F32, name=f"bank{i}") for i in range(N // P))
+                y_last.extend(psum.tile([P, P], F32, name=f"bank{4 + i}") for i in range(N // P))
             for i in range(N // P):
-                for c in range(0, width, n):
+                for c in range(0, width, P):
+                    last = c0 + c == PAIRS - P
                     nc.tensor.matmul_mx(
-                        out=y_banks[i][:, c0 + c : c0 + c + n],
+                        out=y_last[i][:] if last else y_banks[i][:, c0 + c : c0 + c + P],
                         lhsT=w4_w[:, b, 2 * P * i : 2 * P * (i + 1)].bitcast(FP4X4),
                         lhsT_scale=w4_s[:, b, P * i : P * (i + 1)],
-                        rhs=codes[:, c : c + n].bitcast(FP8X4),
-                        rhs_scale=scales[:, c : c + n],
-                        start=(b == 0),
-                        stop=(b == 1 and c0 + c + n == PAIRS),
+                        rhs=codes[:, c : c + P].bitcast(FP8X4),
+                        rhs_scale=scales[:, c : c + P],
+                        start=(b == 0 and (last or c == 0)),
+                        stop=(b == 1 and c0 + c >= PAIRS - 2 * P),
                     )
 
         nc.vector.tensor_copy(v_w[0][:], tab_w[0][:].bitcast(U32).indirect(idx[:]))
-        round_w1(nc.scalar.copy, 0, 0, raw00, 0, 0, PACK)
+        round_w1(nc.scalar.copy, 0, 0, 0, raw00, 0)
         nc.vector.tensor_copy(v_s[:], tab_s[:].indirect(idx[:]))
+        quantize_w1(0, 0, 0, 2)
         nc.vector.tensor_copy(v_w[1][:], tab_w[1][:].bitcast(U32).indirect(idx[:]))
-        round_w1(nc.scalar.copy, 0, 1, raw01[0], 0, 0, PACK)
-        quantize_w1(0, 0, 0, 1)
-        round_w1(nc.vector.tensor_copy, 0, 1, raw01[1], P // 2, 0, 2)
-        round_w1(nc.scalar.copy, 0, 1, raw01[1], P // 2, 2, PACK)
-        quantize_w1(0, 0, 1, 2)
-        quantize_w1(0, 1, 0, 1)
-        quantize_w1(0, 1, 1, 2)
-        quantize_w1(0, 0, 2, PACK)
-        quantize_w1(0, 1, 2, PACK)
+        round_w1(nc.scalar.copy, 0, 0, 1, raw01[0], 0)
+        round_w1(nc.scalar.copy, 0, 0, 1, raw01[1], P // 2)
+        quantize_w1(0, 0, 2, 3)
+        quantize_w1(0, 0, 3, 4)
+        round_w1(nc.scalar.copy, 0, 1, 0, raw00, 0)
+        round_w1(nc.scalar.copy, 0, 1, 1, raw01[0], 0)
+        round_w1(nc.scalar.copy, 0, 1, 1, raw01[1], P // 2)
+        quantize_w1(0, 1, 0, 4)
 
-        make_h(0, 0, True)
-        make_h(0, 1, False)
-        gather_right(0, 0)
-        make_h(0, 2, False)
-        gather_right(0, 1)
-        round_w1(nc.scalar.copy, 1, 0, raw1[0], 0, 0, PACK)
-        gather_left(0, 0, 0, PAIRS)
-        gather_right(0, 2)
-        make_h(0, 3, False)
-        gather_left(0, 1, 0, PAIRS)
-        round_w1(nc.scalar.copy, 1, 1, raw1[1], 0, 0, PACK)
-        quantize_w1(1, 0, 0, PACK)
-        gather_right(0, 3)
-        gather_left(0, 2, 0, PAIRS)
-        quantize_w1(1, 1, 0, PACK)
-        gather_left(0, 3, 0, PAIRS)
+        half, quarter = PAIRS // 2, PAIRS // 4
+        TAGS = {(0, 0): "picked02", (0, 256): "picked01", (1, 0): "picked12", (1, 256): "picked13", (1, 384): "picked12"}
+        ZTAG = "z_bf0"
+        for t in range(PACK):
+            make_h(0, t, t == 0)
+        for t in range(PACK):
+            gather_right(0, t)
+            positive_part(0, t, t == 3)
+        for t in range(PACK):
+            gather_left(0, t, 0, half)
+        round_w1(nc.scalar.copy, 1, 0, 0, raw1[0], 0, 0, 256)
+        round_w1(nc.scalar.copy, 1, 0, 0, raw1[0], 64, 256, 256)
+        quantize_w1(1, 0, 0, 2)
+        round_w1(nc.scalar.copy, 1, 0, 1, raw1[1], 0, 0, 256)
+        round_w1(nc.scalar.copy, 1, 0, 1, raw1[1], 64, 256, 256)
+        quantize_w1(1, 0, 2, 4)
+        round_w1(nc.scalar.copy, 1, 1, 0, raw1[0], 0, 0, 256)
+        round_w1(nc.scalar.copy, 1, 1, 0, raw1[0], 64, 256, 256)
+        quantize_w1(1, 1, 0, 2)
+        round_w1(nc.scalar.copy, 1, 1, 1, raw1[1], 0, 0, 256)
+        round_w1(nc.scalar.copy, 1, 1, 1, raw1[1], 64, 256, 256)
+        quantize_w1(1, 1, 2, 4)
+        for t in range(PACK):
+            gather_left(0, t, half, PAIRS)
+        round_z(nc.scalar.copy, 0, 0)
         make_h(1, 0, False)
         make_h(1, 1, False)
-        gather_right(1, 0)
         make_h(1, 2, False)
-        gather_right(1, 1)
         make_h(1, 3, False)
-        half, quarter = PAIRS // 2, PAIRS // 4
-        gather_left(1, 0, 0, half)
-        gather_right(1, 2)
-        round_z(nc.scalar.copy, 0, 0)
-        gather_left(1, 1, 0, half)
-        gather_right(1, 3)
-        gather_left(1, 2, 0, half)
+        round_z(nc.scalar.copy, 0, half)
         multiply_z(0, 0)
-        gather_left(1, 3, 0, half)
+        for t in range(PACK):
+            gather_right(1, t)
+            positive_part(1, t, t == 3)
+        for t in range(PACK):
+            gather_left(1, t, 0, half)
         round_z(nc.scalar.copy, 1, 0)
         for t in range(PACK):
             gather_left(1, t, half, half + quarter)
         round_z(nc.scalar.copy, 1, half)
         multiply_z(1, 0)
+        multiply_z(1, half)
         for t in range(PACK):
             gather_left(1, t, half + quarter, PAIRS)
-        multiply_z(1, half)
         round_z(nc.vector.tensor_copy, 1, half + quarter)
         multiply_z(1, half + quarter)
 
         y = []
         for i in range(N // P):
             y.append(keep.tile([P, PAIRS], F32, name=f"y{i}"))
-            nc.scalar.copy(y[i][:], y_banks[i][:])
+            nc.scalar.copy(y[i][:, 0 : PAIRS - P], y_banks[i][:])
+        nc.vector.tensor_copy(y[0][:, PAIRS - P : PAIRS], y_last[0][:])
+        for i in range(1, N // P):
+            nc.scalar.copy(y[i][:, PAIRS - P : PAIRS], y_last[i][:])
         first = {}
 
         def gather_first(i):

@@ -20,7 +20,13 @@ P = 128
 PACK = 4
 PASS = P * PACK
 BANK = 512
+QUADS = 4
+PER_COLUMN = 16
+LINE = 4
+Y_TILES = N // P
 F32_MAX = 3.4028234663852886e38
+HALF, QUARTER = PAIRS // 2, PAIRS // 4
+LAST = PAIRS - QUARTER
 
 
 def tile_list_precedent_ladder_kernel(
@@ -33,152 +39,156 @@ def tile_list_precedent_ladder_kernel(
         psum = ctx.enter_context(tc.psum_pool(name="psum", bufs=1))
 
         def load_list(src, name):
-            t = lists.tile(list(src.shape), U16, name=name)
-            nc.sync.dma_start(t[:], src)
-            return t
+            tile = lists.tile(list(src.shape), U16, name=name)
+            nc.sync.dma_start(tile[:], src)
+            return tile
+
+        def load_table_words(a):
+            tile = keep.tile([P, T], I32, name=f"tab_w{a}", align_bytes=256)
+            nc.sync.dma_start(tile[:], tab_words[a].rearrange("p t i -> p (t i)").bitcast(I32))
+            return tile
 
         def load_w1(b, a, c0, width):
-            raw = keep.tile([P, PACK, width], F32, name=f"w1_raw_{b}_{a}_{c0}")
+            raw = keep.tile([P, PACK, width], F32, name=f"w1_raw_{b}_{a}_{c0}", align_bytes=256)
             rows = w1[a * PASS : (a + 1) * PASS, b * PASS + c0 : b * PASS + c0 + width]
             nc.sync.dma_start(raw[:], rows.rearrange("(p j) c -> p j c", j=PACK))
             return raw
 
-        def load_table(a):
-            t = keep.tile([P, T], I32, name=f"tab_w{a}")
-            nc.sync.dma_start(t[:], tab_words[a].rearrange("p t i -> p (t i)").bitcast(I32))
-            return t
-
-        tab_s = keep.tile([P, T], U8, name="tab_s")
+        tab_s = keep.tile([P, T], U8, name="tab_s", align_bytes=256)
         w4_s = keep.tile([P, 2, N], U8, name="w4_s", align_bytes=64)
         nc.vector.memset(tab_s[:].bitcast(I32), 0)
-        for q in range(4):
+        for q in range(QUADS):
             nc.sync.dma_start(
                 tab_s[32 * q : 32 * q + 8, :].bitcast(I32), tab_scales[:, 4 * q : 4 * q + 4, :].bitcast(I32)
             )
-        tab_w = [load_table(0)]
+        tab_w = [load_table_words(0)]
         idx = load_list(offs, "idx")
-        raw00 = load_w1(0, 0, 0, PASS)
+        raw_00 = load_w1(0, 0, 0, PASS)
         bias = keep.tile([P, 2, PACK], F32, name="bias")
-        nc.sync.dma_start(bias[:], b1.rearrange("(b p t) -> p b t", b=2, t=PACK))
-        tab_w.append(load_table(1))
-        raw01 = [load_w1(0, 1, 0, PASS // 2), load_w1(0, 1, PASS // 2, PASS // 2)]
+        nc.gpsimd.dma_start(bias[:], b1.rearrange("(b p t) -> p b t", b=2, t=PACK))
         p2 = load_list(pos2, "p2")
+        tab_w.append(load_table_words(1))
+        raw_01 = [load_w1(0, 1, c0, PASS // 2) for c0 in (0, PASS // 2)]
         p1 = load_list(pos1, "p1")
-        raw1 = [load_w1(1, 0, 0, PASS), load_w1(1, 1, 0, PASS)]
+        raw_1 = [load_w1(1, a, 0, PASS) for a in range(2)]
         w4_w = keep.tile([P, 2, 2 * N], U8, name="w4_w", align_bytes=64)
         nc.sync.dma_start(w4_w[:].bitcast(I32), w4_words.rearrange("a p c -> p a c").bitcast(I32))
-        for q in range(4):
+        for q in range(QUADS):
             nc.sync.dma_start(
                 w4_s[32 * q : 32 * q + 4, :, :].bitcast(I32),
                 w4_scales[:, 4 * q : 4 * q + 4, :].rearrange("a r c -> r a c").bitcast(I32),
             )
         p3 = load_list(pos3, "p3")
         p4 = load_list(pos4, "p4")
-        gain = keep.tile([P, N // P], F32, name="gain")
+        gain = keep.tile([P, Y_TILES], F32, name="gain")
         with nc.allow_non_contiguous_dma(reason="one gain a partition"):
             nc.sync.dma_start(gain[:], gn.rearrange("(i p) -> p i", p=P))
+
+        def picked_slot(b, t):
+            return f"picked{b}{t}"
+
+        w_bf_slot = {
+            (0, 0): "w_bf00",
+            (0, 1): "w_bf01",
+            (1, 0): picked_slot(0, 1),
+            (1, 1): picked_slot(0, 3),
+        }
+        z32_slot = {
+            (0, 0): picked_slot(0, 2),
+            (0, HALF): picked_slot(0, 1),
+            (1, 0): picked_slot(1, 2),
+            (1, HALF): picked_slot(1, 3),
+            (1, LAST): picked_slot(1, 2),
+        }
 
         v_w = [keep.tile([P, S], U32, name=f"v_w{a}", align_bytes=64) for a in range(2)]
         v_s = keep.tile([P, S], U8, name="v_s", align_bytes=64)
 
-        w_bf = {}
-        w_code = {}
-        w_scale = {}
+        w_bf, w_code, w_scale = {}, {}, {}
         for b in range(2):
             for u in range(2):
                 w_code[b, u] = keep.tile([P, 4 * P], U32, name=f"w_code{b}{u}", align_bytes=64)
                 w_scale[b, u] = keep.tile([P, 4 * P], U8, name=f"w_scale{b}{u}", align_bytes=64)
 
-        def round_w1(copy, b, u, a, raw, m0, c0=0, width=None):
-            width = width or raw.shape[2]
+        def round_w1(b, u, a, raw, m0):
             if (b, u) not in w_bf:
-                tag = f"picked0{u}" if b == 1 else f"w_bf{b}{u}"
-                w_bf[b, u] = keep.tile([P, 2, 2, P, PACK], BF16, name=f"w_bf{b}{u}", tag=tag, align_bytes=64)
-            m1 = m0 + width // PACK
-            copy(
+                w_bf[b, u] = keep.tile(
+                    [P, 2, 2, P, PACK], BF16, name=f"w_bf{b}{u}", tag=w_bf_slot[b, u], align_bytes=64
+                )
+            m1 = m0 + raw.shape[2] // PACK
+            nc.scalar.copy(
                 out=w_bf[b, u][:, a, :, m0:m1, :].rearrange("p t m j -> p m j t"),
-                in_=raw[:, :, c0 : c0 + width].rearrange("p j (m t) -> p m j t", t=PACK)[:, :, :, 2 * u : 2 * u + 2],
+                in_=raw[:].rearrange("p j (m t) -> p m j t", t=PACK)[:, :, :, 2 * u : 2 * u + 2],
             )
 
-        def quantize_w1(b, u, s0, s1):
+        def quantize_w1(b, u, first_operand, end_operand):
+            words = slice(first_operand * P, end_operand * P)
             nc.vector.quantize_mx(
-                out=w_code[b, u][:, s0 * P : s1 * P].bitcast(FP8X4),
-                scales=w_scale[b, u][:, s0 * P : s1 * P],
-                in_=w_bf[b, u][:].rearrange("p a t m j -> p (a t m j)")[:, s0 * PASS : s1 * PASS],
+                out=w_code[b, u][:, words].bitcast(FP8X4),
+                scales=w_scale[b, u][:, words],
+                in_=w_bf[b, u][:].rearrange("p a t m j -> p (a t m j)")[:, first_operand * PASS : end_operand * PASS],
             )
 
         h = {}
 
-        def make_h(b, t, split):
-            first_bank = 2 * t
-            banks = [psum.tile([P, BANK], F32, name=f"bank{first_bank + half}") for half in range(2)]
+        def make_h(b, t):
+            banks = [psum.tile([P, BANK], F32, name=f"bank{2 * t + side}") for side in range(2)]
             for a in range(2):
-                w_cols = slice((2 * a + t % 2) * P, (2 * a + t % 2 + 1) * P)
-                for half in range(2):
-                    cols = slice(half * BANK, (half + 1) * BANK)
+                operand = 2 * a + t % 2
+                words = slice(operand * P, (operand + 1) * P)
+                for side in range(2):
+                    entries = slice(side * BANK, (side + 1) * BANK)
                     nc.tensor.matmul_mx(
-                        out=banks[half][:],
-                        lhsT=w_code[b, t // 2][:, w_cols].bitcast(FP8X4),
-                        lhsT_scale=w_scale[b, t // 2][:, w_cols],
-                        rhs=v_w[a][:, cols].bitcast(FP8X4),
-                        rhs_scale=v_s[4 * a : P, cols],
+                        out=banks[side][:],
+                        lhsT=w_code[b, t // 2][:, words].bitcast(FP8X4),
+                        lhsT_scale=w_scale[b, t // 2][:, words],
+                        rhs=v_w[a][:, entries].bitcast(FP8X4),
+                        rhs_scale=v_s[4 * a : P, entries],
                         start=(a == 0),
                         stop=(a == 1),
                     )
             h[b, t] = keep.tile([P, S], F32, name=f"h{b}{t}")
-            nc.scalar.activation(h[b, t][:, 0:BANK], banks[0][:], ACT.Identity, bias=bias[:, b, t : t + 1])
-            if split:
-                nc.vector.tensor_scalar(
-                    h[b, t][:, BANK:S], banks[1][:], bias[:, b, t : t + 1], None, op0=ALU.add
-                )
+            row_bias = bias[:, b, t : t + 1]
+            nc.scalar.activation(h[b, t][:, 0:BANK], banks[0][:], ACT.Identity, bias=row_bias)
+            if (b, t) == (0, 0):
+                nc.vector.tensor_scalar(h[b, t][:, BANK:S], banks[1][:], row_bias, None, op0=ALU.add)
             else:
-                nc.scalar.activation(h[b, t][:, BANK:S], banks[1][:], ACT.Identity, bias=bias[:, b, t : t + 1])
+                nc.scalar.activation(h[b, t][:, BANK:S], banks[1][:], ACT.Identity, bias=row_bias)
 
-        right = {}
-        picked = {}
+        right, z32, z_bf = {}, {}, {}
 
         def gather_right(b, t):
-            picked[b, t] = keep.tile([P, PAIRS], F32, name=f"picked{b}{t}", tag=f"picked{b}{t}", align_bytes=64)
-            nc.vector.tensor_copy(picked[b, t][:], h[b, t][:].indirect(p2[:]))
-
-        def positive_part(b, t, on_scalar=False):
+            picked = keep.tile([P, PAIRS], F32, name=f"picked{b}{t}", tag=picked_slot(b, t), align_bytes=64)
+            nc.vector.tensor_copy(picked[:], h[b, t][:].indirect(p2[:]))
             right[b, t] = keep.tile([P, PAIRS], F32, name=f"right{b}{t}")
-            if on_scalar:
-                nc.scalar.activation(right[b, t][:], picked[b, t][:], ACT.Relu)
+            if t < PACK - 1:
+                nc.gpsimd.tensor_scalar(right[b, t][:], picked[:], F32_MAX, 0.0, op0=ALU.min, op1=ALU.max)
             else:
-                nc.gpsimd.tensor_scalar(right[b, t][:], picked[b, t][:], F32_MAX, 0.0, op0=ALU.min, op1=ALU.max)
+                nc.scalar.activation(right[b, t][:], picked[:], ACT.Relu)
 
-        z32 = {}
-
-        def gather_left(b, t, c0, c1):
-            if (b, c0) not in z32:
-                tag = TAGS.get((b, c0), f"z32_{b}_{c0}")
-                z32[b, c0] = keep.tile([P, PACK, c1 - c0], F32, name=f"z32_{b}_{c0}", tag=tag, align_bytes=64)
-            nc.vector.tensor_tensor(
-                z32[b, c0][:, t, :],
-                h[b, t][:].indirect(p1[:, c0 // 16 : c1 // 16]),
-                right[b, t][:, c0:c1],
-                ALU.subtract,
+        def gather_left(b, c0, c1):
+            z32[b, c0] = keep.tile(
+                [P, PACK, c1 - c0], F32, name=f"z32_{b}_{c0}", tag=z32_slot[b, c0], align_bytes=64
             )
+            for t in range(PACK):
+                nc.vector.tensor_tensor(
+                    z32[b, c0][:, t, :],
+                    h[b, t][:].indirect(p1[:, c0 // PER_COLUMN : c1 // PER_COLUMN]),
+                    right[b, t][:, c0:c1],
+                    ALU.subtract,
+                )
 
-        z_bf = {}
-
-        def round_z(copy, b, c0):
-            width = z32[b, c0].shape[2]
-            if b == 1:
-                z_bf[b, c0] = keep.tile([P, width * PACK], BF16, name=f"z_bf{b}_{c0}", align_bytes=64)
-                dst = z_bf[b, c0][:]
-            else:
-                if c0 == 0:
-                    z_bf[b, 0] = keep.tile([P, PAIRS * PACK], BF16, name="z_bf0", tag=ZTAG, align_bytes=64)
-                dst = z_bf[b, 0][:, c0 * PACK : (c0 + width) * PACK]
+        def round_z(copy, b, c0, rounded):
             copy(
-                out=dst.rearrange("p (c i t) -> p c t i", i=4, t=PACK),
-                in_=z32[b, c0][:].rearrange("p t (c i) -> p c t i", i=4),
+                out=rounded.rearrange("p (c i t) -> p c t i", i=LINE, t=PACK),
+                in_=z32[b, c0][:].rearrange("p t (c i) -> p c t i", i=LINE),
             )
 
-        y_banks = []
-        y_last = []
+        def z_bf_tile(b, c0, width):
+            z_bf[b, c0] = keep.tile([P, width * PACK], BF16, name=f"z_bf{b}_{c0}", align_bytes=64)
+            return z_bf[b, c0]
+
+        y_main, y_last = [], []
 
         def multiply_z(b, c0):
             width = z_bf[b, c0].shape[1] // PACK
@@ -186,104 +196,89 @@ def tile_list_precedent_ladder_kernel(
             scales = keep.tile([P, width], U8, name=f"z_scale{b}_{c0}", align_bytes=64)
             nc.vector.quantize_mx(out=codes[:].bitcast(FP8X4), scales=scales[:], in_=z_bf[b, c0][:])
             if b == 0:
-                y_banks.extend(psum.tile([P, PAIRS - P], F32, name=f"bank{i}") for i in range(N // P))
-                y_last.extend(psum.tile([P, P], F32, name=f"bank{4 + i}") for i in range(N // P))
-            for i in range(N // P):
-                for c in range(0, width, P):
-                    last = c0 + c == PAIRS - P
+                y_main.extend(psum.tile([P, LAST], F32, name=f"bank{i}") for i in range(Y_TILES))
+                y_last.extend(psum.tile([P, QUARTER], F32, name=f"bank{Y_TILES + i}") for i in range(Y_TILES))
+            for i in range(Y_TILES):
+                for c in range(0, width, QUARTER):
+                    column = c0 + c
                     nc.tensor.matmul_mx(
-                        out=y_last[i][:] if last else y_banks[i][:, c0 + c : c0 + c + P],
+                        out=y_last[i][:] if column == LAST else y_main[i][:, column : column + QUARTER],
                         lhsT=w4_w[:, b, 2 * P * i : 2 * P * (i + 1)].bitcast(FP4X4),
                         lhsT_scale=w4_s[:, b, P * i : P * (i + 1)],
-                        rhs=codes[:, c : c + P].bitcast(FP8X4),
-                        rhs_scale=scales[:, c : c + P],
-                        start=(b == 0 and (last or c == 0)),
-                        stop=(b == 1 and c0 + c >= PAIRS - 2 * P),
+                        rhs=codes[:, c : c + QUARTER].bitcast(FP8X4),
+                        rhs_scale=scales[:, c : c + QUARTER],
+                        start=(b == 0 and column in (0, LAST)),
+                        stop=(b == 1 and column in (HALF, LAST)),
                     )
 
         nc.vector.tensor_copy(v_w[0][:], tab_w[0][:].bitcast(U32).indirect(idx[:]))
-        round_w1(nc.scalar.copy, 0, 0, 0, raw00, 0)
+        round_w1(0, 0, 0, raw_00, 0)
         nc.vector.tensor_copy(v_s[:], tab_s[:].indirect(idx[:]))
         quantize_w1(0, 0, 0, 2)
         nc.vector.tensor_copy(v_w[1][:], tab_w[1][:].bitcast(U32).indirect(idx[:]))
-        round_w1(nc.scalar.copy, 0, 0, 1, raw01[0], 0)
-        round_w1(nc.scalar.copy, 0, 0, 1, raw01[1], P // 2)
+        round_w1(0, 0, 1, raw_01[0], 0)
+        round_w1(0, 0, 1, raw_01[1], P // 2)
         quantize_w1(0, 0, 2, 3)
         quantize_w1(0, 0, 3, 4)
-        round_w1(nc.scalar.copy, 0, 1, 0, raw00, 0)
-        round_w1(nc.scalar.copy, 0, 1, 1, raw01[0], 0)
-        round_w1(nc.scalar.copy, 0, 1, 1, raw01[1], P // 2)
+        round_w1(0, 1, 0, raw_00, 0)
+        round_w1(0, 1, 1, raw_01[0], 0)
+        round_w1(0, 1, 1, raw_01[1], P // 2)
         quantize_w1(0, 1, 0, 4)
 
-        half, quarter = PAIRS // 2, PAIRS // 4
-        TAGS = {(0, 0): "picked02", (0, 256): "picked01", (1, 0): "picked12", (1, 256): "picked13", (1, 384): "picked12"}
-        ZTAG = "z_bf0"
         for t in range(PACK):
-            make_h(0, t, t == 0)
+            make_h(0, t)
         for t in range(PACK):
             gather_right(0, t)
-            positive_part(0, t, t == 3)
+        gather_left(0, 0, HALF)
+        for u in range(2):
+            for a in range(2):
+                round_w1(1, u, a, raw_1[a], 0)
+                quantize_w1(1, u, 2 * a, 2 * a + 2)
+        gather_left(0, HALF, PAIRS)
+        z_bf_0 = z_bf_tile(0, 0, PAIRS)
+        round_z(nc.scalar.copy, 0, 0, z_bf_0[:, 0 : HALF * PACK])
+
         for t in range(PACK):
-            gather_left(0, t, 0, half)
-        round_w1(nc.scalar.copy, 1, 0, 0, raw1[0], 0, 0, 256)
-        round_w1(nc.scalar.copy, 1, 0, 0, raw1[0], 64, 256, 256)
-        quantize_w1(1, 0, 0, 2)
-        round_w1(nc.scalar.copy, 1, 0, 1, raw1[1], 0, 0, 256)
-        round_w1(nc.scalar.copy, 1, 0, 1, raw1[1], 64, 256, 256)
-        quantize_w1(1, 0, 2, 4)
-        round_w1(nc.scalar.copy, 1, 1, 0, raw1[0], 0, 0, 256)
-        round_w1(nc.scalar.copy, 1, 1, 0, raw1[0], 64, 256, 256)
-        quantize_w1(1, 1, 0, 2)
-        round_w1(nc.scalar.copy, 1, 1, 1, raw1[1], 0, 0, 256)
-        round_w1(nc.scalar.copy, 1, 1, 1, raw1[1], 64, 256, 256)
-        quantize_w1(1, 1, 2, 4)
-        for t in range(PACK):
-            gather_left(0, t, half, PAIRS)
-        round_z(nc.scalar.copy, 0, 0)
-        make_h(1, 0, False)
-        make_h(1, 1, False)
-        make_h(1, 2, False)
-        make_h(1, 3, False)
-        round_z(nc.scalar.copy, 0, half)
+            make_h(1, t)
+        round_z(nc.scalar.copy, 0, HALF, z_bf_0[:, HALF * PACK : PAIRS * PACK])
         multiply_z(0, 0)
         for t in range(PACK):
             gather_right(1, t)
-            positive_part(1, t, t == 3)
-        for t in range(PACK):
-            gather_left(1, t, 0, half)
-        round_z(nc.scalar.copy, 1, 0)
-        for t in range(PACK):
-            gather_left(1, t, half, half + quarter)
-        round_z(nc.scalar.copy, 1, half)
+        gather_left(1, 0, HALF)
+        round_z(nc.scalar.copy, 1, 0, z_bf_tile(1, 0, HALF)[:])
+        gather_left(1, HALF, LAST)
+        round_z(nc.scalar.copy, 1, HALF, z_bf_tile(1, HALF, QUARTER)[:])
         multiply_z(1, 0)
-        multiply_z(1, half)
-        for t in range(PACK):
-            gather_left(1, t, half + quarter, PAIRS)
-        round_z(nc.vector.tensor_copy, 1, half + quarter)
-        multiply_z(1, half + quarter)
+        multiply_z(1, HALF)
+        gather_left(1, LAST, PAIRS)
+        round_z(nc.vector.tensor_copy, 1, LAST, z_bf_tile(1, LAST, QUARTER)[:])
+        multiply_z(1, LAST)
 
         y = []
-        for i in range(N // P):
+        for i in range(Y_TILES):
             y.append(keep.tile([P, PAIRS], F32, name=f"y{i}"))
-            nc.scalar.copy(y[i][:, 0 : PAIRS - P], y_banks[i][:])
-        nc.vector.tensor_copy(y[0][:, PAIRS - P : PAIRS], y_last[0][:])
-        for i in range(1, N // P):
-            nc.scalar.copy(y[i][:, PAIRS - P : PAIRS], y_last[i][:])
-        first = {}
+            nc.scalar.copy(y[i][:, 0:LAST], y_main[i][:])
+        nc.vector.tensor_copy(y[0][:, LAST:PAIRS], y_last[0][:])
+        for i in range(1, Y_TILES):
+            nc.scalar.copy(y[i][:, LAST:PAIRS], y_last[i][:])
 
-        def gather_first(i):
-            first[i] = keep.tile([P, LINES], F32, name=f"first{i}")
-            nc.vector.tensor_copy(first[i][:], y[i][:].indirect(p3[:]))
+        first_line = {}
 
-        def finish(i):
-            both = keep.tile([P, LINES], F32, name=f"both{i}")
-            nc.vector.tensor_tensor(both[:], y[i][:].indirect(p4[:]), first[i][:], ALU.mult)
-            result = keep.tile([P, LINES], F32, name=f"result{i}")
+        def gather_first_line(i):
+            first_line[i] = keep.tile([P, LINES], F32, name=f"first_line{i}")
+            nc.vector.tensor_copy(first_line[i][:], y[i][:].indirect(p3[:]))
+
+        def finish(i, c0, c1):
+            both = keep.tile([P, c1 - c0], F32, name=f"both{i}_{c0}")
+            second_line = y[i][:].indirect(p4[:, c0 // PER_COLUMN : c1 // PER_COLUMN])
+            nc.vector.tensor_tensor(both[:], second_line, first_line[i][:, c0:c1], ALU.mult)
+            result = keep.tile([P, c1 - c0], F32, name=f"result{i}_{c0}")
             nc.scalar.activation(result[:], both[:], ACT.Tanh, scale=gain[:, i : i + 1])
-            nc.sync.dma_start(out[i * P : (i + 1) * P, :], result[:])
+            nc.sync.dma_start(out[i * P : (i + 1) * P, c0:c1], result[:])
 
-        gather_first(0)
-        for i in range(1, N // P):
-            gather_first(i)
-            finish(i - 1)
-        finish(N // P - 1)
+        gather_first_line(0)
+        for i in range(1, Y_TILES):
+            gather_first_line(i)
+            finish(i - 1, 0, LINES)
+        finish(Y_TILES - 1, 0, LINES // 2)
+        finish(Y_TILES - 1, LINES // 2, LINES)

@@ -26,6 +26,7 @@ LINE = 4
 Y_TILES = N // P
 F32_MAX = 3.4028234663852886e38
 HALF, QUARTER = PAIRS // 2, PAIRS // 4
+HELD = ((1, 0, "w_bf100"), (2, 0, "w_bf101"), (3, 0, "w_bf110"), (4, 0, "w_bf111"), (7, 0, "z_bf0_0"))
 LAST = PAIRS - QUARTER
 
 
@@ -84,22 +85,12 @@ def tile_list_precedent_ladder_kernel(
         with nc.allow_non_contiguous_dma(reason="one gain a partition"):
             nc.sync.dma_start(gain[:], gn.rearrange("(i p) -> p i", p=P))
 
-        def picked_slot(b, t):
-            return f"picked{b}{t}"
-
-        w_bf_slot = {
-            (0, 0): "w_bf00",
-            (0, 1): "w_bf01",
-            (1, 0): picked_slot(0, 1),
-            (1, 1): picked_slot(0, 3),
-        }
-        z32_slot = {
-            (0, 0): picked_slot(0, 2),
-            (0, HALF): picked_slot(0, 1),
-            (1, 0): picked_slot(1, 2),
-            (1, HALF): picked_slot(1, 3),
-            (1, LAST): picked_slot(1, 2),
-        }
+        bias_src = [bias[:, n // PACK, n % PACK : n % PACK + 1] for n in range(8)]
+        row_bias = [[src, src] for src in bias_src]
+        for n, side, slot in HELD:
+            held = keep.tile([P, 1], F32, name=f"held{n}{side}", tag=slot, align_bytes=64)
+            nc.scalar.copy(held[:], bias_src[n])
+            row_bias[n][side] = held[:]
 
         v_w = [keep.tile([P, S], U32, name=f"v_w{a}", align_bytes=64) for a in range(2)]
         v_s = keep.tile([P, S], U8, name="v_s", align_bytes=64)
@@ -110,14 +101,17 @@ def tile_list_precedent_ladder_kernel(
                 w_code[b, u] = keep.tile([P, 4 * P], U32, name=f"w_code{b}{u}", align_bytes=64)
                 w_scale[b, u] = keep.tile([P, 4 * P], U8, name=f"w_scale{b}{u}", align_bytes=64)
 
-        def round_w1(b, u, a, raw, m0):
-            if (b, u) not in w_bf:
-                w_bf[b, u] = keep.tile(
-                    [P, 2, 2, P, PACK], BF16, name=f"w_bf{b}{u}", tag=w_bf_slot[b, u], align_bytes=64
-                )
+        pair01 = keep.tile([P, 2, 2, P, PACK], BF16, name="w_bf01", align_bytes=64)
+        w_bf[0, 1, 0] = pair01[:, 0, :, :, :]
+        w_bf[0, 0, 1] = w_bf[0, 1, 1] = pair01[:, 1, :, :, :]
+
+        def round_w1(b, u, a, raw, m0, copy=nc.scalar.copy):
+            if (b, u, a) not in w_bf:
+                tile = keep.tile([P, 2, P, PACK], BF16, name=f"w_bf{b}{u}{a}", align_bytes=64)
+                w_bf[b, u, a] = tile[:]
             m1 = m0 + raw.shape[2] // PACK
-            nc.scalar.copy(
-                out=w_bf[b, u][:, a, :, m0:m1, :].rearrange("p t m j -> p m j t"),
+            copy(
+                out=w_bf[b, u, a][:, :, m0:m1, :].rearrange("p t m j -> p m j t"),
                 in_=raw[:].rearrange("p j (m t) -> p m j t", t=PACK)[:, :, :, 2 * u : 2 * u + 2],
             )
 
@@ -126,62 +120,67 @@ def tile_list_precedent_ladder_kernel(
             nc.vector.quantize_mx(
                 out=w_code[b, u][:, words].bitcast(FP8X4),
                 scales=w_scale[b, u][:, words],
-                in_=w_bf[b, u][:].rearrange("p a t m j -> p (a t m j)")[:, first_operand * PASS : end_operand * PASS],
+                in_=w_bf[b, u, first_operand // 2].rearrange("p t m j -> p (t m j)")[
+                    :, first_operand % 2 * PASS : (end_operand - first_operand // 2 * 2) * PASS
+                ],
             )
 
-        h = {}
+        h, banks = {}, {}
 
-        def make_h(b, t):
-            banks = [psum.tile([P, BANK], F32, name=f"bank{2 * t + side}") for side in range(2)]
-            for a in range(2):
-                operand = 2 * a + t % 2
-                words = slice(operand * P, (operand + 1) * P)
-                for side in range(2):
-                    entries = slice(side * BANK, (side + 1) * BANK)
-                    nc.tensor.matmul_mx(
-                        out=banks[side][:],
-                        lhsT=w_code[b, t // 2][:, words].bitcast(FP8X4),
-                        lhsT_scale=w_scale[b, t // 2][:, words],
-                        rhs=v_w[a][:, entries].bitcast(FP8X4),
-                        rhs_scale=v_s[4 * a : P, entries],
-                        start=(a == 0),
-                        stop=(a == 1),
-                    )
-            h[b, t] = keep.tile([P, S], F32, name=f"h{b}{t}")
-            row_bias = bias[:, b, t : t + 1]
-            nc.scalar.activation(h[b, t][:, 0:BANK], banks[0][:], ACT.Identity, bias=row_bias)
-            if (b, t) == (0, 0):
-                nc.vector.tensor_scalar(h[b, t][:, BANK:S], banks[1][:], row_bias, None, op0=ALU.add)
+        def multiply_w(n, a):
+            b, t = divmod(n, PACK)
+            if a == 0:
+                banks[n] = [psum.tile([P, BANK], F32, name=f"bank{2 * t + side}") for side in range(2)]
+            operand = 2 * a + t % 2
+            words = slice(operand * P, (operand + 1) * P)
+            for side in range(2):
+                entries = slice(side * BANK, (side + 1) * BANK)
+                nc.tensor.matmul_mx(
+                    out=banks[n][side][:],
+                    lhsT=w_code[b, t // 2][:, words].bitcast(FP8X4),
+                    lhsT_scale=w_scale[b, t // 2][:, words],
+                    rhs=v_w[a][:, entries].bitcast(FP8X4),
+                    rhs_scale=v_s[4 * a : P, entries],
+                    start=(a == 0),
+                    stop=(a == 1),
+                )
+
+        def empty_h(n):
+            h[n] = keep.tile([P, S], F32, name=f"h{n}")
+            nc.scalar.activation(h[n][:, 0:BANK], banks[n][0][:], ACT.Identity, bias=row_bias[n][0])
+            if n == 0:
+                nc.vector.tensor_scalar(h[n][:, BANK:S], banks[n][1][:], row_bias[n][1], None, op0=ALU.add)
             else:
-                nc.scalar.activation(h[b, t][:, BANK:S], banks[1][:], ACT.Identity, bias=row_bias)
+                nc.scalar.activation(h[n][:, BANK:S], banks[n][1][:], ACT.Identity, bias=row_bias[n][1])
 
-        right, z32, z_bf = {}, {}, {}
+        picked, right, z32, z_bf = {}, {}, {}, {}
+        z32[0, 0] = keep.tile([P, PACK, PAIRS], F32, name="z32_0", align_bytes=64)
 
-        def gather_right(b, t):
-            picked = keep.tile([P, PAIRS], F32, name=f"picked{b}{t}", tag=picked_slot(b, t), align_bytes=64)
-            nc.vector.tensor_copy(picked[:], h[b, t][:].indirect(p2[:]))
-            right[b, t] = keep.tile([P, PAIRS], F32, name=f"right{b}{t}")
-            if t < PACK - 1:
-                nc.gpsimd.tensor_scalar(right[b, t][:], picked[:], F32_MAX, 0.0, op0=ALU.min, op1=ALU.max)
-            else:
-                nc.scalar.activation(right[b, t][:], picked[:], ACT.Relu)
+        def gather_right(n):
+            picked[n] = keep.tile([P, PAIRS], F32, name=f"picked{n}", align_bytes=64)
+            nc.vector.tensor_copy(picked[n][:], h[n][:].indirect(p2[:]))
 
-        def gather_left(b, c0, c1):
-            z32[b, c0] = keep.tile(
-                [P, PACK, c1 - c0], F32, name=f"z32_{b}_{c0}", tag=z32_slot[b, c0], align_bytes=64
-            )
+        def positive(n):
+            right[n] = keep.tile([P, PAIRS], F32, name=f"right{n}", align_bytes=64)
+            nc.scalar.activation(right[n][:], picked[n][:], ACT.Relu)
+
+        def gather_left0(n):
+            nc.vector.tensor_tensor(z32[0, 0][:, n, :], h[n][:].indirect(p1[:]), right[n][:], ALU.subtract)
+
+        def gather_left1(c0, c1, slot):
+            z32[1, c0] = keep.tile([P, PACK, c1 - c0], F32, name=f"z32_1_{c0}", tag=slot, align_bytes=64)
             for t in range(PACK):
                 nc.vector.tensor_tensor(
-                    z32[b, c0][:, t, :],
-                    h[b, t][:].indirect(p1[:, c0 // PER_COLUMN : c1 // PER_COLUMN]),
-                    right[b, t][:, c0:c1],
+                    z32[1, c0][:, t, :],
+                    h[4 + t][:].indirect(p1[:, c0 // PER_COLUMN : c1 // PER_COLUMN]),
+                    right[4 + t][:, c0:c1],
                     ALU.subtract,
                 )
 
-        def round_z(copy, b, c0, rounded):
+        def round_z(copy, b, c0, width):
             copy(
-                out=rounded.rearrange("p (c i t) -> p c t i", i=LINE, t=PACK),
-                in_=z32[b, c0][:].rearrange("p t (c i) -> p c t i", i=LINE),
+                out=z_bf_tile(b, c0, width)[:].rearrange("p (c i t) -> p c t i", i=LINE, t=PACK),
+                in_=(z32[1, c0][:] if b else z32[0, 0][:, :, c0 : c0 + width]).rearrange("p t (c i) -> p c t i", i=LINE),
             )
 
         def z_bf_tile(b, c0, width):
@@ -195,7 +194,7 @@ def tile_list_precedent_ladder_kernel(
             codes = keep.tile([P, width], U32, name=f"z_code{b}_{c0}", align_bytes=64)
             scales = keep.tile([P, width], U8, name=f"z_scale{b}_{c0}", align_bytes=64)
             nc.vector.quantize_mx(out=codes[:].bitcast(FP8X4), scales=scales[:], in_=z_bf[b, c0][:])
-            if b == 0:
+            if (b, c0) == (0, 0):
                 y_main.extend(psum.tile([P, LAST], F32, name=f"bank{i}") for i in range(Y_TILES))
                 y_last.extend(psum.tile([P, QUARTER], F32, name=f"bank{Y_TILES + i}") for i in range(Y_TILES))
             for i in range(Y_TILES):
@@ -215,43 +214,55 @@ def tile_list_precedent_ladder_kernel(
         round_w1(0, 0, 0, raw_00, 0)
         nc.vector.tensor_copy(v_s[:], tab_s[:].indirect(idx[:]))
         quantize_w1(0, 0, 0, 2)
+        multiply_w(0, 0)
+        multiply_w(1, 0)
         nc.vector.tensor_copy(v_w[1][:], tab_w[1][:].bitcast(U32).indirect(idx[:]))
+        round_w1(0, 1, 0, raw_00, 0)
         round_w1(0, 0, 1, raw_01[0], 0)
         round_w1(0, 0, 1, raw_01[1], P // 2)
         quantize_w1(0, 0, 2, 3)
+        multiply_w(0, 1)
         quantize_w1(0, 0, 3, 4)
-        round_w1(0, 1, 0, raw_00, 0)
-        round_w1(0, 1, 1, raw_01[0], 0)
-        round_w1(0, 1, 1, raw_01[1], P // 2)
-        quantize_w1(0, 1, 0, 4)
-
-        for t in range(PACK):
-            make_h(0, t)
-        for t in range(PACK):
-            gather_right(0, t)
-        gather_left(0, 0, HALF)
-        for u in range(2):
-            for a in range(2):
-                round_w1(1, u, a, raw_1[a], 0)
-                quantize_w1(1, u, 2 * a, 2 * a + 2)
-        gather_left(0, HALF, PAIRS)
-        z_bf_0 = z_bf_tile(0, 0, PAIRS)
-        round_z(nc.scalar.copy, 0, 0, z_bf_0[:, 0 : HALF * PACK])
-
-        for t in range(PACK):
-            make_h(1, t)
-        round_z(nc.scalar.copy, 0, HALF, z_bf_0[:, HALF * PACK : PAIRS * PACK])
+        multiply_w(1, 1)
+        round_w1(0, 1, 1, raw_01[0], 0, nc.vector.tensor_copy)
+        round_w1(0, 1, 1, raw_01[1], P // 2, nc.vector.tensor_copy)
+        nc.vector.quantize_mx(
+            out=w_code[0, 1][:].bitcast(FP8X4),
+            scales=w_scale[0, 1][:],
+            in_=pair01[:].rearrange("p a t m j -> p (a t m j)"),
+        )
+        empty_h(0)
+        gather_right(0)
+        for n in (2, 3):
+            multiply_w(n, 0)
+            multiply_w(n, 1)
+        for n in range(1, 5):
+            u, a = divmod(n - 1, 2)
+            empty_h(n)
+            gather_right(n)
+            round_w1(1, u, a, raw_1[a], 0)
+            positive(n - 1)
+            quantize_w1(1, u, 2 * a, 2 * a + 2)
+            gather_left0(n - 1)
+            multiply_w(4 + 2 * u, a)
+            multiply_w(5 + 2 * u, a)
+        for n in (5, 6, 7):
+            empty_h(n)
+            gather_right(n)
+        for n in (4, 5, 6, 7):
+            positive(n)
+        round_z(nc.scalar.copy, 0, 0, HALF)
+        round_z(nc.scalar.copy, 0, HALF, HALF)
+        gather_left1(0, HALF, "picked6")
         multiply_z(0, 0)
-        for t in range(PACK):
-            gather_right(1, t)
-        gather_left(1, 0, HALF)
-        round_z(nc.scalar.copy, 1, 0, z_bf_tile(1, 0, HALF)[:])
-        gather_left(1, HALF, LAST)
-        round_z(nc.scalar.copy, 1, HALF, z_bf_tile(1, HALF, QUARTER)[:])
+        round_z(nc.scalar.copy, 1, 0, HALF)
+        gather_left1(HALF, LAST, "picked7")
+        multiply_z(0, HALF)
+        round_z(nc.scalar.copy, 1, HALF, QUARTER)
         multiply_z(1, 0)
+        gather_left1(LAST, PAIRS, "z_bf0_256")
         multiply_z(1, HALF)
-        gather_left(1, LAST, PAIRS)
-        round_z(nc.vector.tensor_copy, 1, LAST, z_bf_tile(1, LAST, QUARTER)[:])
+        round_z(nc.vector.tensor_copy, 1, LAST, QUARTER)
         multiply_z(1, LAST)
 
         y = []

@@ -26,7 +26,8 @@ LINE = 4
 Y_TILES = N // P
 F32_MAX = 3.4028234663852886e38
 HALF, QUARTER = PAIRS // 2, PAIRS // 4
-HELD = ((1, 0, "w_bf100"), (2, 0, "w_bf101"), (3, 0, "w_bf110"), (4, 0, "w_bf111"), (7, 0, "z_bf0_0"))
+HELD = ((1, 0, "w_bf100"), (2, 0, "w_bf101"), (3, 0, "w_bf110"), (7, 0, "z_bf0_0"), (7, 1, "z_bf0_256"),
+        (1, 1, "right0"), (2, 1, "right1"), (3, 1, "right2"), (4, 1, "right3"))
 LAST = PAIRS - QUARTER
 
 
@@ -103,7 +104,7 @@ def tile_list_precedent_ladder_kernel(
 
         pair01 = keep.tile([P, 2, 2, P, PACK], BF16, name="w_bf01", align_bytes=64)
         w_bf[0, 1, 0] = pair01[:, 0, :, :, :]
-        w_bf[0, 0, 1] = w_bf[0, 1, 1] = pair01[:, 1, :, :, :]
+        w_bf[0, 1, 1] = pair01[:, 1, :, :, :]
 
         def round_w1(b, u, a, raw, m0, copy=nc.scalar.copy):
             if (b, u, a) not in w_bf:
@@ -162,7 +163,10 @@ def tile_list_precedent_ladder_kernel(
 
         def positive(n):
             right[n] = keep.tile([P, PAIRS], F32, name=f"right{n}", align_bytes=64)
-            nc.scalar.activation(right[n][:], picked[n][:], ACT.Relu)
+            if n < 7:
+                nc.gpsimd.tensor_scalar(right[n][:], picked[n][:], F32_MAX, 0.0, op0=ALU.min, op1=ALU.max)
+            else:
+                nc.scalar.activation(right[n][:], picked[n][:], ACT.Relu)
 
         def gather_left0(n):
             nc.vector.tensor_tensor(z32[0, 0][:, n, :], h[n][:].indirect(p1[:]), right[n][:], ALU.subtract)
@@ -224,8 +228,8 @@ def tile_list_precedent_ladder_kernel(
         multiply_w(0, 1)
         quantize_w1(0, 0, 3, 4)
         multiply_w(1, 1)
-        round_w1(0, 1, 1, raw_01[0], 0, nc.vector.tensor_copy)
-        round_w1(0, 1, 1, raw_01[1], P // 2, nc.vector.tensor_copy)
+        round_w1(0, 1, 1, raw_01[0], 0)
+        round_w1(0, 1, 1, raw_01[1], P // 2)
         nc.vector.quantize_mx(
             out=w_code[0, 1][:].bitcast(FP8X4),
             scales=w_scale[0, 1][:],
@@ -237,21 +241,34 @@ def tile_list_precedent_ladder_kernel(
             multiply_w(n, 0)
             multiply_w(n, 1)
         for n in range(1, 5):
-            u, a = divmod(n - 1, 2)
             empty_h(n)
             gather_right(n)
-            round_w1(1, u, a, raw_1[a], 0)
             positive(n - 1)
-            quantize_w1(1, u, 2 * a, 2 * a + 2)
             gather_left0(n - 1)
-            multiply_w(4 + 2 * u, a)
-            multiply_w(5 + 2 * u, a)
+            for u, a in {1: [(0, 0)], 2: [(0, 1)], 3: [], 4: []}[n]:
+                round_w1(1, u, a, raw_1[a], 0)
+                quantize_w1(1, u, 2 * a, 2 * a + 2)
+                multiply_w(4 + 2 * u, a)
+                multiply_w(5 + 2 * u, a)
+            if n == 3:
+                pair11 = keep.tile([P, 2, 2, P, PACK], BF16, name="w_bf110", align_bytes=64)
+                for a in range(2):
+                    w_bf[1, 1, a] = pair11[:, a, :, :, :]
+                    round_w1(1, 1, a, raw_1[a], 0)
+                nc.vector.quantize_mx(
+                    out=w_code[1, 1][:].bitcast(FP8X4),
+                    scales=w_scale[1, 1][:],
+                    in_=pair11[:].rearrange("p a t m j -> p (a t m j)"),
+                )
+                for m in (6, 7):
+                    multiply_w(m, 0)
+                    multiply_w(m, 1)
         for n in (5, 6, 7):
             empty_h(n)
             gather_right(n)
-        for n in (4, 5, 6, 7):
-            positive(n)
+            positive(n - 1)
         round_z(nc.scalar.copy, 0, 0, HALF)
+        positive(7)
         round_z(nc.scalar.copy, 0, HALF, HALF)
         gather_left1(0, HALF, "picked6")
         multiply_z(0, 0)
@@ -260,7 +277,7 @@ def tile_list_precedent_ladder_kernel(
         multiply_z(0, HALF)
         round_z(nc.scalar.copy, 1, HALF, QUARTER)
         multiply_z(1, 0)
-        gather_left1(LAST, PAIRS, "z_bf0_256")
+        gather_left1(LAST, PAIRS, "picked6")
         multiply_z(1, HALF)
         round_z(nc.vector.tensor_copy, 1, LAST, QUARTER)
         multiply_z(1, LAST)

@@ -26,9 +26,19 @@ LINE = 4
 Y_TILES = N // P
 F32_MAX = 3.4028234663852886e38
 HALF, QUARTER = PAIRS // 2, PAIRS // 4
-HELD = ((1, 0, "w_bf100"), (2, 0, "w_bf101"), (3, 0, "w_bf110"), (7, 0, "z_bf0_0"), (7, 1, "z_bf0_256"),
-        (1, 1, "right0"), (2, 1, "right1"), (3, 1, "right2"), (4, 1, "right3"))
 LAST = PAIRS - QUARTER
+H_TILES = H // P
+BIAS_SLOTS = (
+    (1, 0, "w_bf100"),
+    (2, 0, "w_bf101"),
+    (3, 0, "w_bf110"),
+    (7, 0, "z_bf0_0"),
+    (7, 1, "z_bf0_256"),
+    (1, 1, "right0"),
+    (2, 1, "right1"),
+    (3, 1, "right2"),
+    (4, 1, "right3"),
+)
 
 
 def tile_list_precedent_ladder_kernel(
@@ -86,12 +96,15 @@ def tile_list_precedent_ladder_kernel(
         with nc.allow_non_contiguous_dma(reason="one gain a partition"):
             nc.sync.dma_start(gain[:], gn.rearrange("(i p) -> p i", p=P))
 
-        bias_src = [bias[:, n // PACK, n % PACK : n % PACK + 1] for n in range(8)]
-        row_bias = [[src, src] for src in bias_src]
-        for n, side, slot in HELD:
-            held = keep.tile([P, 1], F32, name=f"held{n}{side}", tag=slot, align_bytes=64)
-            nc.scalar.copy(held[:], bias_src[n])
-            row_bias[n][side] = held[:]
+        row_bias = {}
+        for ht in range(H_TILES):
+            b, t = divmod(ht, PACK)
+            row_bias[ht, 0] = row_bias[ht, 1] = bias[:, b, t : t + 1]
+        for ht, side, slot in BIAS_SLOTS:
+            b, t = divmod(ht, PACK)
+            held = keep.tile([P, 1], F32, name=f"bias{ht}{side}", tag=slot, align_bytes=64)
+            nc.scalar.copy(held[:], bias[:, b, t : t + 1])
+            row_bias[ht, side] = held[:]
 
         v_w = [keep.tile([P, S], U32, name=f"v_w{a}", align_bytes=64) for a in range(2)]
         v_s = keep.tile([P, S], U8, name="v_s", align_bytes=64)
@@ -102,42 +115,45 @@ def tile_list_precedent_ladder_kernel(
                 w_code[b, u] = keep.tile([P, 4 * P], U32, name=f"w_code{b}{u}", align_bytes=64)
                 w_scale[b, u] = keep.tile([P, 4 * P], U8, name=f"w_scale{b}{u}", align_bytes=64)
 
-        pair01 = keep.tile([P, 2, 2, P, PACK], BF16, name="w_bf01", align_bytes=64)
-        w_bf[0, 1, 0] = pair01[:, 0, :, :, :]
-        w_bf[0, 1, 1] = pair01[:, 1, :, :, :]
+        def w_bf_tile(b, u, passes):
+            name = f"w_bf{b}{u}{passes[0]}"
+            tile = keep.tile([P, len(passes), 2, P, PACK], BF16, name=name, align_bytes=64)
+            for i, a in enumerate(passes):
+                w_bf[b, u, a] = (tile, i)
 
-        def round_w1(b, u, a, raw, m0, copy=nc.scalar.copy):
-            if (b, u, a) not in w_bf:
-                tile = keep.tile([P, 2, P, PACK], BF16, name=f"w_bf{b}{u}{a}", align_bytes=64)
-                w_bf[b, u, a] = tile[:]
+        def round_w1(b, u, a, raw, m0):
+            tile, i = w_bf[b, u, a]
             m1 = m0 + raw.shape[2] // PACK
-            copy(
-                out=w_bf[b, u, a][:, :, m0:m1, :].rearrange("p t m j -> p m j t"),
+            nc.scalar.copy(
+                out=tile[:, i, :, m0:m1, :].rearrange("p t m j -> p m j t"),
                 in_=raw[:].rearrange("p j (m t) -> p m j t", t=PACK)[:, :, :, 2 * u : 2 * u + 2],
             )
 
         def quantize_w1(b, u, first_operand, end_operand):
+            tile, i = w_bf[b, u, first_operand // 2]
+            first_value = (2 * i + first_operand % 2) * PASS
+            values = slice(first_value, first_value + (end_operand - first_operand) * PASS)
             words = slice(first_operand * P, end_operand * P)
             nc.vector.quantize_mx(
                 out=w_code[b, u][:, words].bitcast(FP8X4),
                 scales=w_scale[b, u][:, words],
-                in_=w_bf[b, u, first_operand // 2].rearrange("p t m j -> p (t m j)")[
-                    :, first_operand % 2 * PASS : (end_operand - first_operand // 2 * 2) * PASS
-                ],
+                in_=tile[:].rearrange("p a t m j -> p (a t m j)")[:, values],
             )
+
+        w_bf_tile(0, 1, (0, 1))
 
         h, banks = {}, {}
 
-        def multiply_w(n, a):
-            b, t = divmod(n, PACK)
+        def multiply_w(ht, a):
+            b, t = divmod(ht, PACK)
             if a == 0:
-                banks[n] = [psum.tile([P, BANK], F32, name=f"bank{2 * t + side}") for side in range(2)]
+                banks[ht] = [psum.tile([P, BANK], F32, name=f"bank{2 * t + side}") for side in range(2)]
             operand = 2 * a + t % 2
             words = slice(operand * P, (operand + 1) * P)
             for side in range(2):
                 entries = slice(side * BANK, (side + 1) * BANK)
                 nc.tensor.matmul_mx(
-                    out=banks[n][side][:],
+                    out=banks[ht][side][:],
                     lhsT=w_code[b, t // 2][:, words].bitcast(FP8X4),
                     lhsT_scale=w_scale[b, t // 2][:, words],
                     rhs=v_w[a][:, entries].bitcast(FP8X4),
@@ -146,50 +162,47 @@ def tile_list_precedent_ladder_kernel(
                     stop=(a == 1),
                 )
 
-        def empty_h(n):
-            h[n] = keep.tile([P, S], F32, name=f"h{n}")
-            nc.scalar.activation(h[n][:, 0:BANK], banks[n][0][:], ACT.Identity, bias=row_bias[n][0])
-            if n == 0:
-                nc.vector.tensor_scalar(h[n][:, BANK:S], banks[n][1][:], row_bias[n][1], None, op0=ALU.add)
+        def empty_h(ht):
+            h[ht] = keep.tile([P, S], F32, name=f"h{ht}")
+            nc.scalar.activation(h[ht][:, 0:BANK], banks[ht][0][:], ACT.Identity, bias=row_bias[ht, 0])
+            if ht == 0:
+                nc.vector.tensor_scalar(h[ht][:, BANK:S], banks[ht][1][:], row_bias[ht, 1], None, op0=ALU.add)
             else:
-                nc.scalar.activation(h[n][:, BANK:S], banks[n][1][:], ACT.Identity, bias=row_bias[n][1])
+                nc.scalar.activation(h[ht][:, BANK:S], banks[ht][1][:], ACT.Identity, bias=row_bias[ht, 1])
 
-        picked, right, z32, z_bf = {}, {}, {}, {}
-        z32[0, 0] = keep.tile([P, PACK, PAIRS], F32, name="z32_0", align_bytes=64)
+        picked, right, z32_piece, z_bf = {}, {}, {}, {}
+        z32_whole = keep.tile([P, PACK, PAIRS], F32, name="z32_0", align_bytes=64)
 
-        def gather_right(n):
-            picked[n] = keep.tile([P, PAIRS], F32, name=f"picked{n}", align_bytes=64)
-            nc.vector.tensor_copy(picked[n][:], h[n][:].indirect(p2[:]))
+        def gather_right(ht):
+            picked[ht] = keep.tile([P, PAIRS], F32, name=f"picked{ht}", align_bytes=64)
+            nc.vector.tensor_copy(picked[ht][:], h[ht][:].indirect(p2[:]))
 
-        def positive(n):
-            right[n] = keep.tile([P, PAIRS], F32, name=f"right{n}", align_bytes=64)
-            if n < 7:
-                nc.gpsimd.tensor_scalar(right[n][:], picked[n][:], F32_MAX, 0.0, op0=ALU.min, op1=ALU.max)
+        def positive_part(ht):
+            right[ht] = keep.tile([P, PAIRS], F32, name=f"right{ht}", align_bytes=64)
+            if ht < PACK:
+                nc.gpsimd.tensor_scalar(right[ht][:], picked[ht][:], F32_MAX, 0.0, op0=ALU.min, op1=ALU.max)
             else:
-                nc.scalar.activation(right[n][:], picked[n][:], ACT.Relu)
+                nc.scalar.activation(right[ht][:], picked[ht][:], ACT.Relu)
 
-        def gather_left0(n):
-            nc.vector.tensor_tensor(z32[0, 0][:, n, :], h[n][:].indirect(p1[:]), right[n][:], ALU.subtract)
+        def gather_left_tile(ht):
+            nc.vector.tensor_tensor(z32_whole[:, ht, :], h[ht][:].indirect(p1[:]), right[ht][:], ALU.subtract)
 
-        def gather_left1(c0, c1, slot):
-            z32[1, c0] = keep.tile([P, PACK, c1 - c0], F32, name=f"z32_1_{c0}", tag=slot, align_bytes=64)
+        def gather_left_piece(c0, c1, slot):
+            z32_piece[c0] = keep.tile([P, PACK, c1 - c0], F32, name=f"z32_1_{c0}", tag=slot, align_bytes=64)
             for t in range(PACK):
                 nc.vector.tensor_tensor(
-                    z32[1, c0][:, t, :],
-                    h[4 + t][:].indirect(p1[:, c0 // PER_COLUMN : c1 // PER_COLUMN]),
-                    right[4 + t][:, c0:c1],
+                    z32_piece[c0][:, t, :],
+                    h[PACK + t][:].indirect(p1[:, c0 // PER_COLUMN : c1 // PER_COLUMN]),
+                    right[PACK + t][:, c0:c1],
                     ALU.subtract,
                 )
 
-        def round_z(copy, b, c0, width):
+        def round_z(copy, b, c0, values):
+            z_bf[b, c0] = keep.tile([P, values.shape[2] * PACK], BF16, name=f"z_bf{b}_{c0}", align_bytes=64)
             copy(
-                out=z_bf_tile(b, c0, width)[:].rearrange("p (c i t) -> p c t i", i=LINE, t=PACK),
-                in_=(z32[1, c0][:] if b else z32[0, 0][:, :, c0 : c0 + width]).rearrange("p t (c i) -> p c t i", i=LINE),
+                out=z_bf[b, c0][:].rearrange("p (c i t) -> p c t i", i=LINE, t=PACK),
+                in_=values.rearrange("p t (c i) -> p c t i", i=LINE),
             )
-
-        def z_bf_tile(b, c0, width):
-            z_bf[b, c0] = keep.tile([P, width * PACK], BF16, name=f"z_bf{b}_{c0}", align_bytes=64)
-            return z_bf[b, c0]
 
         y_main, y_last = [], []
 
@@ -215,6 +228,7 @@ def tile_list_precedent_ladder_kernel(
                     )
 
         nc.vector.tensor_copy(v_w[0][:], tab_w[0][:].bitcast(U32).indirect(idx[:]))
+        w_bf_tile(0, 0, (0,))
         round_w1(0, 0, 0, raw_00, 0)
         nc.vector.tensor_copy(v_s[:], tab_s[:].indirect(idx[:]))
         quantize_w1(0, 0, 0, 2)
@@ -222,6 +236,7 @@ def tile_list_precedent_ladder_kernel(
         multiply_w(1, 0)
         nc.vector.tensor_copy(v_w[1][:], tab_w[1][:].bitcast(U32).indirect(idx[:]))
         round_w1(0, 1, 0, raw_00, 0)
+        w_bf_tile(0, 0, (1,))
         round_w1(0, 0, 1, raw_01[0], 0)
         round_w1(0, 0, 1, raw_01[1], P // 2)
         quantize_w1(0, 0, 2, 3)
@@ -230,56 +245,54 @@ def tile_list_precedent_ladder_kernel(
         multiply_w(1, 1)
         round_w1(0, 1, 1, raw_01[0], 0)
         round_w1(0, 1, 1, raw_01[1], P // 2)
-        nc.vector.quantize_mx(
-            out=w_code[0, 1][:].bitcast(FP8X4),
-            scales=w_scale[0, 1][:],
-            in_=pair01[:].rearrange("p a t m j -> p (a t m j)"),
-        )
+        quantize_w1(0, 1, 0, 4)
         empty_h(0)
         gather_right(0)
-        for n in (2, 3):
-            multiply_w(n, 0)
-            multiply_w(n, 1)
-        for n in range(1, 5):
-            empty_h(n)
-            gather_right(n)
-            positive(n - 1)
-            gather_left0(n - 1)
-            for u, a in {1: [(0, 0)], 2: [(0, 1)], 3: [], 4: []}[n]:
-                round_w1(1, u, a, raw_1[a], 0)
-                quantize_w1(1, u, 2 * a, 2 * a + 2)
-                multiply_w(4 + 2 * u, a)
-                multiply_w(5 + 2 * u, a)
-            if n == 3:
-                pair11 = keep.tile([P, 2, 2, P, PACK], BF16, name="w_bf110", align_bytes=64)
-                for a in range(2):
-                    w_bf[1, 1, a] = pair11[:, a, :, :, :]
-                    round_w1(1, 1, a, raw_1[a], 0)
-                nc.vector.quantize_mx(
-                    out=w_code[1, 1][:].bitcast(FP8X4),
-                    scales=w_scale[1, 1][:],
-                    in_=pair11[:].rearrange("p a t m j -> p (a t m j)"),
-                )
-                for m in (6, 7):
-                    multiply_w(m, 0)
-                    multiply_w(m, 1)
-        for n in (5, 6, 7):
-            empty_h(n)
-            gather_right(n)
-            positive(n - 1)
-        round_z(nc.scalar.copy, 0, 0, HALF)
-        positive(7)
-        round_z(nc.scalar.copy, 0, HALF, HALF)
-        gather_left1(0, HALF, "picked6")
+        for ht in (2, 3):
+            multiply_w(ht, 0)
+            multiply_w(ht, 1)
+
+        def step(ht):
+            empty_h(ht)
+            gather_right(ht)
+            positive_part(ht - 1)
+            gather_left_tile(ht - 1)
+
+        for a in range(2):
+            step(1 + a)
+            w_bf_tile(1, 0, (a,))
+            round_w1(1, 0, a, raw_1[a], 0)
+            quantize_w1(1, 0, 2 * a, 2 * a + 2)
+            multiply_w(4, a)
+            multiply_w(5, a)
+        step(3)
+        w_bf_tile(1, 1, (0, 1))
+        for a in range(2):
+            round_w1(1, 1, a, raw_1[a], 0)
+        quantize_w1(1, 1, 0, 4)
+        for ht in (6, 7):
+            multiply_w(ht, 0)
+            multiply_w(ht, 1)
+        step(4)
+
+        for ht in (5, 6, 7):
+            empty_h(ht)
+            gather_right(ht)
+        for ht in (4, 5, 6):
+            positive_part(ht)
+        round_z(nc.scalar.copy, 0, 0, z32_whole[:, :, 0:HALF])
+        positive_part(7)
+        round_z(nc.scalar.copy, 0, HALF, z32_whole[:, :, HALF:PAIRS])
+        gather_left_piece(0, HALF, "picked6")
         multiply_z(0, 0)
-        round_z(nc.scalar.copy, 1, 0, HALF)
-        gather_left1(HALF, LAST, "picked7")
+        round_z(nc.scalar.copy, 1, 0, z32_piece[0][:])
+        gather_left_piece(HALF, LAST, "picked7")
         multiply_z(0, HALF)
-        round_z(nc.scalar.copy, 1, HALF, QUARTER)
+        round_z(nc.scalar.copy, 1, HALF, z32_piece[HALF][:])
         multiply_z(1, 0)
-        gather_left1(LAST, PAIRS, "picked6")
+        gather_left_piece(LAST, PAIRS, "picked6")
         multiply_z(1, HALF)
-        round_z(nc.vector.tensor_copy, 1, LAST, QUARTER)
+        round_z(nc.vector.tensor_copy, 1, LAST, z32_piece[LAST][:])
         multiply_z(1, LAST)
 
         y = []

@@ -17,6 +17,7 @@ ACT = mybir.ActivationFunctionType
 ALU = mybir.AluOpType
 
 P = 128
+HALF_P = P // 2
 PACK = 4
 PASS = P * PACK
 BANK = 512
@@ -24,20 +25,22 @@ QUADS = 4
 PER_COLUMN = 16
 LINE = 4
 Y_TILES = N // P
+H_TILES = H // P
 F32_MAX = 3.4028234663852886e38
 HALF, QUARTER = PAIRS // 2, PAIRS // 4
-LAST = PAIRS - QUARTER
-H_TILES = H // P
 BIAS_SLOTS = (
-    (1, 0, "w_bf100"),
-    (2, 0, "w_bf101"),
-    (3, 0, "w_bf110"),
-    (7, 0, "z_bf0_0"),
-    (7, 1, "z_bf0_256"),
+    (0, 0, "w_bf_2_1"),
+    (0, 2, "w_code_2_0"),
     (1, 1, "right0"),
+    (2, 0, "w_bf_4_0"),
     (2, 1, "right1"),
     (3, 1, "right2"),
+    (4, 0, "w_bf_6_1"),
     (4, 1, "right3"),
+    (5, 1, "right4"),
+    (6, 1, "right5"),
+    (7, 0, "z_bf0"),
+    (7, 1, "right6"),
 )
 
 
@@ -60,9 +63,9 @@ def tile_list_precedent_ladder_kernel(
             nc.sync.dma_start(tile[:], tab_words[a].rearrange("p t i -> p (t i)").bitcast(I32))
             return tile
 
-        def load_w1(b, a, c0, width):
-            raw = keep.tile([P, PACK, width], F32, name=f"w1_raw_{b}_{a}_{c0}", align_bytes=256)
-            rows = w1[a * PASS : (a + 1) * PASS, b * PASS + c0 : b * PASS + c0 + width]
+        def load_w1(a, c0, width):
+            raw = keep.tile([P, PACK, width], F32, name=f"w1_raw_{a}_{c0}", align_bytes=256)
+            rows = w1[a * PASS : (a + 1) * PASS, c0 : c0 + width]
             nc.sync.dma_start(raw[:], rows.rearrange("(p j) c -> p j c", j=PACK))
             return raw
 
@@ -75,14 +78,31 @@ def tile_list_precedent_ladder_kernel(
             )
         tab_w = [load_table_words(0)]
         idx = load_list(offs, "idx")
-        raw_00 = load_w1(0, 0, 0, PASS)
-        bias = keep.tile([P, 2, PACK], F32, name="bias")
-        nc.gpsimd.dma_start(bias[:], b1.rearrange("(b p t) -> p b t", b=2, t=PACK))
+        raw = {(0, 0): load_w1(0, 0, HALF)}
         p2 = load_list(pos2, "p2")
+        raw[0, 1] = load_w1(1, 0, HALF)
         tab_w.append(load_table_words(1))
-        raw_01 = [load_w1(0, 1, c0, PASS // 2) for c0 in (0, PASS // 2)]
+        dealt = b1[0:PASS].rearrange("(u m t) -> t m u", u=2, t=PACK)
+        row_bias = {}
+
+        def load_bias(v, u0, u1, slot):
+            tile = keep.tile([P, u1 - u0], F32, name=f"bias_low{v}{u0}", tag=slot, align_bytes=64)
+            with nc.allow_non_contiguous_dma(reason="single values of the bias"):
+                for s in range(2):
+                    nc.sync.dma_start(tile[s * HALF_P : (s + 1) * HALF_P, :], dealt[2 * v + s, :, u0:u1])
+            for u in range(u0, u1):
+                row_bias[2 * u + v] = tile[:, u - u0 : u - u0 + 1]
+
+        raw[1, 0] = load_w1(0, HALF, HALF)
+        load_bias(0, 0, 2, "bias_low")
+        raw[1, 1] = load_w1(1, HALF, HALF)
+        load_bias(1, 0, 1, "w_bf_3_1")
         p1 = load_list(pos1, "p1")
-        raw_1 = [load_w1(1, a, 0, PASS) for a in range(2)]
+        for a in range(2):
+            raw[2, a] = raw[3, a] = load_w1(a, PASS, PASS)
+        load_bias(1, 1, 2, "w_bf_6_0")
+        bias_high = keep.tile([P, PACK], F32, name="bias_high")
+        nc.gpsimd.dma_start(bias_high[:], b1[PASS:H].rearrange("(p t) -> p t", t=PACK))
         w4_w = keep.tile([P, 2, 2 * N], U8, name="w4_w", align_bytes=64)
         nc.sync.dma_start(w4_w[:].bitcast(I32), w4_words.rearrange("a p c -> p a c").bitcast(I32))
         for q in range(QUADS):
@@ -96,212 +116,204 @@ def tile_list_precedent_ladder_kernel(
         with nc.allow_non_contiguous_dma(reason="one gain a partition"):
             nc.sync.dma_start(gain[:], gn.rearrange("(i p) -> p i", p=P))
 
-        row_bias = {}
+        for t in range(PACK):
+            row_bias[PACK + t] = bias_high[:, t : t + 1]
         for ht in range(H_TILES):
-            b, t = divmod(ht, PACK)
-            row_bias[ht, 0] = row_bias[ht, 1] = bias[:, b, t : t + 1]
+            for side in range(3 if ht == 0 else 2):
+                row_bias[ht, side] = row_bias[ht]
         for ht, side, slot in BIAS_SLOTS:
-            b, t = divmod(ht, PACK)
             held = keep.tile([P, 1], F32, name=f"bias{ht}{side}", tag=slot, align_bytes=64)
-            nc.scalar.copy(held[:], bias[:, b, t : t + 1])
+            copy = nc.scalar.copy if ht in (1, 3) else nc.gpsimd.tensor_copy
+            copy(held[:], row_bias[ht, side])
             row_bias[ht, side] = held[:]
 
         v_w = [keep.tile([P, S], U32, name=f"v_w{a}", align_bytes=64) for a in range(2)]
         v_s = keep.tile([P, S], U8, name="v_s", align_bytes=64)
 
-        w_bf, w_code, w_scale = {}, {}, {}
-        for b in range(2):
-            for u in range(2):
-                w_code[b, u] = keep.tile([P, 4 * P], U32, name=f"w_code{b}{u}", align_bytes=64)
-                w_scale[b, u] = keep.tile([P, 4 * P], U8, name=f"w_scale{b}{u}", align_bytes=64)
+        operand = {}
 
-        def w_bf_tile(b, u, passes):
-            name = f"w_bf{b}{u}{passes[0]}"
-            tile = keep.tile([P, len(passes), 2, P, PACK], BF16, name=name, align_bytes=64)
+        def round_w1(tiles, passes):
+            first = tiles[0]
+            name = f"w_bf_{first}_{passes[0]}"
+            rounded = keep.tile([P, len(passes), len(tiles) * PASS], BF16, name=name, align_bytes=64)
+            t0, t1 = (2 * (first % 2), 2 * (tiles[-1] % 2) + 2) if first < PACK else (first - PACK, tiles[-1] - PACK + 1)
             for i, a in enumerate(passes):
-                w_bf[b, u, a] = (tile, i)
+                nc.scalar.copy(
+                    out=rounded[:, i, :].rearrange("p (t m j) -> p m j t", t=t1 - t0, j=PACK),
+                    in_=raw[first // 2, a][:].rearrange("p j (m t) -> p m j t", t=PACK)[:, :, :, t0:t1],
+                )
+            return rounded
 
-        def round_w1(b, u, a, raw, m0):
-            tile, i = w_bf[b, u, a]
-            m1 = m0 + raw.shape[2] // PACK
-            nc.scalar.copy(
-                out=tile[:, i, :, m0:m1, :].rearrange("p t m j -> p m j t"),
-                in_=raw[:].rearrange("p j (m t) -> p m j t", t=PACK)[:, :, :, 2 * u : 2 * u + 2],
-            )
-
-        def quantize_w1(b, u, first_operand, end_operand):
-            tile, i = w_bf[b, u, first_operand // 2]
-            first_value = (2 * i + first_operand % 2) * PASS
-            values = slice(first_value, first_value + (end_operand - first_operand) * PASS)
-            words = slice(first_operand * P, end_operand * P)
+        def quantize_w1(tiles, passes, rounded, slot=None):
+            words = len(tiles) * len(passes) * P
+            name = f"w_code_{tiles[0]}_{passes[0]}"
+            codes = keep.tile([P, words], U32, name=name, tag=slot or name, align_bytes=64)
+            scales = keep.tile([P, words], U8, name=f"w_scale_{tiles[0]}_{passes[0]}", align_bytes=64)
             nc.vector.quantize_mx(
-                out=w_code[b, u][:, words].bitcast(FP8X4),
-                scales=w_scale[b, u][:, words],
-                in_=tile[:].rearrange("p a t m j -> p (a t m j)")[:, values],
+                out=codes[:].bitcast(FP8X4), scales=scales[:], in_=rounded[:].rearrange("p a c -> p (a c)")
             )
+            for i, a in enumerate(passes):
+                for n, ht in enumerate(tiles):
+                    columns = slice((i * len(tiles) + n) * P, (i * len(tiles) + n + 1) * P)
+                    operand[ht, a] = (codes[:, columns], scales[:, columns])
 
-        w_bf_tile(0, 1, (0, 1))
+        def prepare_w1(tiles, passes, slot=None):
+            quantize_w1(tiles, passes, round_w1(tiles, passes), slot)
+            for ht in tiles:
+                multiply_w(ht, *passes)
 
         h, banks = {}, {}
 
-        def multiply_w(ht, a):
-            b, t = divmod(ht, PACK)
-            if a == 0:
-                banks[ht] = [psum.tile([P, BANK], F32, name=f"bank{2 * t + side}") for side in range(2)]
-            operand = 2 * a + t % 2
-            words = slice(operand * P, (operand + 1) * P)
-            for side in range(2):
-                entries = slice(side * BANK, (side + 1) * BANK)
-                nc.tensor.matmul_mx(
-                    out=banks[ht][side][:],
-                    lhsT=w_code[b, t // 2][:, words].bitcast(FP8X4),
-                    lhsT_scale=w_scale[b, t // 2][:, words],
-                    rhs=v_w[a][:, entries].bitcast(FP8X4),
-                    rhs_scale=v_s[4 * a : P, entries],
-                    start=(a == 0),
-                    stop=(a == 1),
-                )
+        def spans(ht):
+            if ht == 0:
+                return [(0, 0, BANK), (1, BANK, BANK + HALF), (7, BANK + HALF, S)]
+            return [(2 * (ht % PACK), 0, BANK), (2 * (ht % PACK) + 1, BANK, S)]
 
-        def empty_h(ht):
+        def multiply_w(ht, *passes):
+            if passes[0] == 0:
+                banks[ht] = [psum.tile([P, e1 - e0], F32, name=f"bank{n}") for n, e0, e1 in spans(ht)]
+            for a in passes:
+                for bank, (n, e0, e1) in zip(banks[ht], spans(ht)):
+                    nc.tensor.matmul_mx(
+                        out=bank[:],
+                        lhsT=operand[ht, a][0].bitcast(FP8X4),
+                        lhsT_scale=operand[ht, a][1],
+                        rhs=v_w[a][:, e0:e1].bitcast(FP8X4),
+                        rhs_scale=v_s[4 * a : P, e0:e1],
+                        start=(a == 0),
+                        stop=(a == 1),
+                    )
+
+        def empty_h(ht, slot=""):
             h[ht] = keep.tile([P, S], F32, name=f"h{ht}")
             nc.scalar.activation(h[ht][:, 0:BANK], banks[ht][0][:], ACT.Identity, bias=row_bias[ht, 0])
             if ht == 0:
-                nc.vector.tensor_scalar(h[ht][:, BANK:S], banks[ht][1][:], row_bias[ht, 1], None, op0=ALU.add)
+                for side in (1, 2):
+                    n, e0, e1 = spans(ht)[side]
+                    nc.vector.tensor_scalar(h[ht][:, e0:e1], banks[ht][side][:], row_bias[ht, side], None, op0=ALU.add)
             else:
                 nc.scalar.activation(h[ht][:, BANK:S], banks[ht][1][:], ACT.Identity, bias=row_bias[ht, 1])
 
-        picked, right, z32_piece, z_bf = {}, {}, {}, {}
-        z32_whole = keep.tile([P, PACK, PAIRS], F32, name="z32_0", align_bytes=64)
+        picked, right, z_bf, z_words = {}, {}, {}, {}
+        z32 = [keep.tile([P, PACK, PAIRS], F32, name=f"z32_{b}", align_bytes=64) for b in range(2)]
 
-        def gather_right(ht):
-            picked[ht] = keep.tile([P, PAIRS], F32, name=f"picked{ht}", align_bytes=64)
+        def gather_right(ht, slot=None):
+            name = f"picked{ht}"
+            picked[ht] = keep.tile([P, PAIRS], F32, name=name, tag=slot or name, align_bytes=256)
             nc.vector.tensor_copy(picked[ht][:], h[ht][:].indirect(p2[:]))
 
         def positive_part(ht):
-            right[ht] = keep.tile([P, PAIRS], F32, name=f"right{ht}", align_bytes=64)
-            if ht < PACK:
+            slot = f"right{ht}" if ht < H_TILES - 1 else "z32_0"
+            right[ht] = keep.tile([P, PAIRS], F32, name=f"right{ht}", tag=slot, align_bytes=64)
+            if ht < H_TILES - 1:
                 nc.gpsimd.tensor_scalar(right[ht][:], picked[ht][:], F32_MAX, 0.0, op0=ALU.min, op1=ALU.max)
             else:
                 nc.scalar.activation(right[ht][:], picked[ht][:], ACT.Relu)
 
-        def gather_left_tile(ht):
-            nc.vector.tensor_tensor(z32_whole[:, ht, :], h[ht][:].indirect(p1[:]), right[ht][:], ALU.subtract)
+        def gather_left(ht, c0=0, c1=PAIRS):
+            entries = p1[:, c0 // PER_COLUMN : c1 // PER_COLUMN]
+            if ht in (2, 3):
+                spare = keep.tile([P, PAIRS], F32, name=f"spare{ht}", align_bytes=64)
+                target = spare[:]
+            elif ht < 2:
+                target = z32[0][:, 2 * ht, :]
+            else:
+                target = z32[1][:, ht - PACK, c0:c1]
+            nc.vector.tensor_tensor(target, h[ht][:].indirect(entries), right[ht][:, c0:c1], ALU.subtract)
+            if ht < 2:
+                nc.sync.dma_start(z32[0][0:HALF_P, 2 * ht + 1, :], target[HALF_P:P, :])
+            elif ht < PACK:
+                t = 2 * (ht - 2)
+                nc.sync.dma_start(z32[0][HALF_P:P, t, :], target[0:HALF_P, :])
+                nc.sync.dma_start(z32[0][HALF_P:P, t + 1, :], target[HALF_P:P, :])
 
-        def gather_left_piece(c0, c1, slot):
-            z32_piece[c0] = keep.tile([P, PACK, c1 - c0], F32, name=f"z32_1_{c0}", tag=slot, align_bytes=64)
-            for t in range(PACK):
-                nc.vector.tensor_tensor(
-                    z32_piece[c0][:, t, :],
-                    h[PACK + t][:].indirect(p1[:, c0 // PER_COLUMN : c1 // PER_COLUMN]),
-                    right[PACK + t][:, c0:c1],
-                    ALU.subtract,
-                )
-
-        def round_z(copy, b, c0, values):
-            z_bf[b, c0] = keep.tile([P, values.shape[2] * PACK], BF16, name=f"z_bf{b}_{c0}", align_bytes=64)
+        def round_z(copy, b, c0, c1):
+            if c0 == 0:
+                z_words[b] = keep.tile([P, PAIRS * PACK], BF16, name=f"z_bf{b}", align_bytes=64)
+            z_bf[b, c0] = z_words[b][:, c0 * PACK : c1 * PACK]
             copy(
-                out=z_bf[b, c0][:].rearrange("p (c i t) -> p c t i", i=LINE, t=PACK),
-                in_=values.rearrange("p t (c i) -> p c t i", i=LINE),
+                out=z_bf[b, c0].rearrange("p (c i t) -> p c t i", i=LINE, t=PACK),
+                in_=z32[b][:, :, c0:c1].rearrange("p t (c i) -> p c t i", i=LINE),
             )
 
-        y_main, y_last = [], []
+        y_banks = {}
 
-        def multiply_z(b, c0):
+        def multiply_z(b, c0, last=()):
             width = z_bf[b, c0].shape[1] // PACK
             codes = keep.tile([P, width], U32, name=f"z_code{b}_{c0}", align_bytes=64)
             scales = keep.tile([P, width], U8, name=f"z_scale{b}_{c0}", align_bytes=64)
-            nc.vector.quantize_mx(out=codes[:].bitcast(FP8X4), scales=scales[:], in_=z_bf[b, c0][:])
-            if (b, c0) == (0, 0):
-                y_main.extend(psum.tile([P, LAST], F32, name=f"bank{i}") for i in range(Y_TILES))
-                y_last.extend(psum.tile([P, QUARTER], F32, name=f"bank{Y_TILES + i}") for i in range(Y_TILES))
+            nc.vector.quantize_mx(out=codes[:].bitcast(FP8X4), scales=scales[:], in_=z_bf[b, c0])
+            side = c0 // HALF
             for i in range(Y_TILES):
+                if b == 0:
+                    y_banks[i, side] = psum.tile([P, HALF], F32, name=f"bank{2 * i + side}")
                 for c in range(0, width, QUARTER):
-                    column = c0 + c
+                    column = (c0 + c) % HALF
                     nc.tensor.matmul_mx(
-                        out=y_last[i][:] if column == LAST else y_main[i][:, column : column + QUARTER],
+                        out=y_banks[i, side][:, column : column + QUARTER],
                         lhsT=w4_w[:, b, 2 * P * i : 2 * P * (i + 1)].bitcast(FP4X4),
                         lhsT_scale=w4_s[:, b, P * i : P * (i + 1)],
                         rhs=codes[:, c : c + QUARTER].bitcast(FP8X4),
                         rhs_scale=scales[:, c : c + QUARTER],
-                        start=(b == 0 and column in (0, LAST)),
-                        stop=(b == 1 and column in (HALF, LAST)),
+                        start=(b == 0 and column == 0),
+                        stop=(b == 1 and column == QUARTER),
                     )
 
         nc.vector.tensor_copy(v_w[0][:], tab_w[0][:].bitcast(U32).indirect(idx[:]))
-        w_bf_tile(0, 0, (0,))
-        round_w1(0, 0, 0, raw_00, 0)
         nc.vector.tensor_copy(v_s[:], tab_s[:].indirect(idx[:]))
-        quantize_w1(0, 0, 0, 2)
+        for a in range(2):
+            quantize_w1((0, 1), (a,), round_w1((0, 1), (a,)))
         multiply_w(0, 0)
         multiply_w(1, 0)
-        nc.vector.tensor_copy(v_w[1][:], tab_w[1][:].bitcast(U32).indirect(idx[:]))
-        round_w1(0, 1, 0, raw_00, 0)
-        w_bf_tile(0, 0, (1,))
-        round_w1(0, 0, 1, raw_01[0], 0)
-        round_w1(0, 0, 1, raw_01[1], P // 2)
-        quantize_w1(0, 0, 2, 3)
+        for n, e0, e1 in spans(0):
+            entries = idx[:, e0 // PER_COLUMN : e1 // PER_COLUMN]
+            nc.vector.tensor_copy(v_w[1][:, e0:e1], tab_w[1][:].bitcast(U32).indirect(entries))
         multiply_w(0, 1)
-        quantize_w1(0, 0, 3, 4)
         multiply_w(1, 1)
-        round_w1(0, 1, 1, raw_01[0], 0)
-        round_w1(0, 1, 1, raw_01[1], P // 2)
-        quantize_w1(0, 1, 0, 4)
+        rounded = round_w1((2, 3), (0,))
         empty_h(0)
+        quantize_w1((2, 3), (0,), rounded)
+        multiply_w(2, 0)
+        multiply_w(3, 0)
         gather_right(0)
-        for ht in (2, 3):
-            multiply_w(ht, 0)
-            multiply_w(ht, 1)
+        prepare_w1((2,), (1,), "w_bf_2_0")
 
         def step(ht):
             empty_h(ht)
             gather_right(ht)
             positive_part(ht - 1)
-            gather_left_tile(ht - 1)
+            gather_left(ht - 1)
 
-        for a in range(2):
-            step(1 + a)
-            w_bf_tile(1, 0, (a,))
-            round_w1(1, 0, a, raw_1[a], 0)
-            quantize_w1(1, 0, 2 * a, 2 * a + 2)
-            multiply_w(4, a)
-            multiply_w(5, a)
+        step(1)
+        prepare_w1((3,), (1,))
+        step(2)
+        prepare_w1((4, 5), (0, 1))
         step(3)
-        w_bf_tile(1, 1, (0, 1))
-        for a in range(2):
-            round_w1(1, 1, a, raw_1[a], 0)
-        quantize_w1(1, 1, 0, 4)
-        for ht in (6, 7):
-            multiply_w(ht, 0)
-            multiply_w(ht, 1)
+        prepare_w1((6, 7), (0,))
         step(4)
-
-        for ht in (5, 6, 7):
-            empty_h(ht)
-            gather_right(ht)
-        for ht in (4, 5, 6):
-            positive_part(ht)
-        round_z(nc.scalar.copy, 0, 0, z32_whole[:, :, 0:HALF])
-        positive_part(7)
-        round_z(nc.scalar.copy, 0, HALF, z32_whole[:, :, HALF:PAIRS])
-        gather_left_piece(0, HALF, "picked6")
+        prepare_w1((6, 7), (1,))
+        for ht in range(5, H_TILES):
+            step(ht)
+        round_z(nc.scalar.copy, 0, 0, HALF)
+        round_z(nc.scalar.copy, 0, HALF, PAIRS)
+        positive_part(H_TILES - 1)
         multiply_z(0, 0)
-        round_z(nc.scalar.copy, 1, 0, z32_piece[0][:])
-        gather_left_piece(HALF, LAST, "picked7")
         multiply_z(0, HALF)
-        round_z(nc.scalar.copy, 1, HALF, z32_piece[HALF][:])
+        pieces = ((0, QUARTER), (HALF, PAIRS), (QUARTER, HALF))
+        for c0, c1 in pieces:
+            gather_left(H_TILES - 1, c0, c1)
+        round_z(nc.scalar.copy, 1, 0, QUARTER)
+        round_z(nc.scalar.copy, 1, HALF, PAIRS)
+        round_z(nc.vector.tensor_copy, 1, QUARTER, HALF)
         multiply_z(1, 0)
-        gather_left_piece(LAST, PAIRS, "picked6")
+        multiply_z(1, QUARTER)
         multiply_z(1, HALF)
-        round_z(nc.vector.tensor_copy, 1, LAST, z32_piece[LAST][:])
-        multiply_z(1, LAST)
 
-        y = []
+        y = [keep.tile([P, PAIRS], F32, name=f"y{i}") for i in range(Y_TILES)]
         for i in range(Y_TILES):
-            y.append(keep.tile([P, PAIRS], F32, name=f"y{i}"))
-            nc.scalar.copy(y[i][:, 0:LAST], y_main[i][:])
-        nc.vector.tensor_copy(y[0][:, LAST:PAIRS], y_last[0][:])
-        for i in range(1, Y_TILES):
-            nc.scalar.copy(y[i][:, LAST:PAIRS], y_last[i][:])
+            nc.scalar.copy(y[i][:, 0:HALF], y_banks[i, 0][:])
+            copy = nc.vector.tensor_copy if i == 0 else nc.scalar.copy
+            copy(y[i][:, HALF:PAIRS], y_banks[i, 1][:])
 
         first_line = {}
 

@@ -28,18 +28,17 @@ Y_TILES = N // P
 H_TILES = H // P
 F32_MAX = 3.4028234663852886e38
 HALF, QUARTER = PAIRS // 2, PAIRS // 4
+LAST = PAIRS - QUARTER
 BIAS_SLOTS = (
-    (0, 0, "w_bf_2_1"),
-    (0, 2, "w_code_2_0"),
+    (1, 0, "w_bf_4_0"),
     (1, 1, "right0"),
-    (2, 0, "w_bf_4_0"),
     (2, 1, "right1"),
     (3, 1, "right2"),
     (4, 0, "w_bf_6_1"),
     (4, 1, "right3"),
     (5, 1, "right4"),
     (6, 1, "right5"),
-    (7, 0, "z_bf0"),
+    (7, 0, "z_bf0_0"),
     (7, 1, "right6"),
 )
 
@@ -70,7 +69,7 @@ def tile_list_precedent_ladder_kernel(
             return raw
 
         tab_s = keep.tile([P, T], U8, name="tab_s", align_bytes=256)
-        w4_s = keep.tile([P, 2, N], U8, name="w4_s", align_bytes=64)
+        w4_s = keep.tile([P, 2, N], U8, name="w4_s", align_bytes=256)
         nc.vector.memset(tab_s[:].bitcast(I32), 0)
         for q in range(QUADS):
             nc.sync.dma_start(
@@ -78,32 +77,28 @@ def tile_list_precedent_ladder_kernel(
             )
         tab_w = [load_table_words(0)]
         idx = load_list(offs, "idx")
-        raw = {(0, 0): load_w1(0, 0, HALF)}
-        p2 = load_list(pos2, "p2")
-        raw[0, 1] = load_w1(1, 0, HALF)
-        tab_w.append(load_table_words(1))
-        dealt = b1[0:PASS].rearrange("(u m t) -> t m u", u=2, t=PACK)
+        raw = {(0, 0): [load_w1(0, 0, PASS)]}
+        dealt_bias = b1.rearrange("(b p t) -> b p t", b=2, t=PACK)
         row_bias = {}
 
-        def load_bias(v, u0, u1, slot):
-            tile = keep.tile([P, u1 - u0], F32, name=f"bias_low{v}{u0}", tag=slot, align_bytes=64)
-            with nc.allow_non_contiguous_dma(reason="single values of the bias"):
-                for s in range(2):
-                    nc.sync.dma_start(tile[s * HALF_P : (s + 1) * HALF_P, :], dealt[2 * v + s, :, u0:u1])
-            for u in range(u0, u1):
-                row_bias[2 * u + v] = tile[:, u - u0 : u - u0 + 1]
+        def load_bias(queue, ht0, ht1, slot):
+            b, t = divmod(ht0, PACK)
+            tile = keep.tile([P, ht1 - ht0], F32, name=f"bias_from{ht0}", tag=slot, align_bytes=256)
+            with nc.allow_non_contiguous_dma(reason="a few values of the bias a partition"):
+                queue.dma_start(tile[:], dealt_bias[b, :, t : t + ht1 - ht0])
+            for ht in range(ht0, ht1):
+                row_bias[ht] = tile[:, ht - ht0 : ht - ht0 + 1]
 
-        raw[1, 0] = load_w1(0, HALF, HALF)
-        load_bias(0, 0, 2, "bias_low")
-        raw[1, 1] = load_w1(1, HALF, HALF)
-        load_bias(1, 0, 1, "w_bf_3_1")
+        load_bias(nc.gpsimd, 0, 2, "bias_first")
+        load_bias(nc.gpsimd, 4, 8, "bias_second")
+        p2 = load_list(pos2, "p2")
+        tab_w.append(load_table_words(1))
+        raw[0, 1] = [load_w1(1, c0, HALF) for c0 in (0, HALF)]
         p1 = load_list(pos1, "p1")
-        for a in range(2):
-            raw[2, a] = raw[3, a] = load_w1(a, PASS, PASS)
-        load_bias(1, 1, 2, "w_bf_6_0")
-        bias_high = keep.tile([P, PACK], F32, name="bias_high")
-        nc.gpsimd.dma_start(bias_high[:], b1[PASS:H].rearrange("(p t) -> p t", t=PACK))
-        w4_w = keep.tile([P, 2, 2 * N], U8, name="w4_w", align_bytes=64)
+        for a, slot in enumerate(("w_bf_4_1", "w_bf_6_0")):
+            raw[1, a] = [load_w1(a, PASS, PASS)]
+            load_bias(nc.sync, 2 + a, 3 + a, slot)
+        w4_w = keep.tile([P, 2, 2 * N], U8, name="w4_w", align_bytes=256)
         nc.sync.dma_start(w4_w[:].bitcast(I32), w4_words.rearrange("a p c -> p a c").bitcast(I32))
         for q in range(QUADS):
             nc.sync.dma_start(
@@ -116,57 +111,52 @@ def tile_list_precedent_ladder_kernel(
         with nc.allow_non_contiguous_dma(reason="one gain a partition"):
             nc.sync.dma_start(gain[:], gn.rearrange("(i p) -> p i", p=P))
 
-        for t in range(PACK):
-            row_bias[PACK + t] = bias_high[:, t : t + 1]
         for ht in range(H_TILES):
-            for side in range(3 if ht == 0 else 2):
+            for side in range(2):
                 row_bias[ht, side] = row_bias[ht]
         for ht, side, slot in BIAS_SLOTS:
-            held = keep.tile([P, 1], F32, name=f"bias{ht}{side}", tag=slot, align_bytes=64)
-            copy = nc.scalar.copy if ht in (1, 3) else nc.gpsimd.tensor_copy
+            held = keep.tile([P, 1], F32, name=f"bias{ht}{side}", tag=slot, align_bytes=256)
+            copy = nc.scalar.copy if ht in (2, 3) else nc.gpsimd.tensor_copy
             copy(held[:], row_bias[ht, side])
             row_bias[ht, side] = held[:]
 
-        v_w = [keep.tile([P, S], U32, name=f"v_w{a}", align_bytes=64) for a in range(2)]
-        v_s = keep.tile([P, S], U8, name="v_s", align_bytes=64)
+        v_w = [keep.tile([P, S], U32, name=f"v_w{a}", align_bytes=256) for a in range(2)]
+        v_s = keep.tile([P, S], U8, name="v_s", align_bytes=256)
 
         operand = {}
 
-        def round_w1(tiles, passes):
-            first = tiles[0]
-            name = f"w_bf_{first}_{passes[0]}"
-            rounded = keep.tile([P, len(passes), len(tiles) * PASS], BF16, name=name, align_bytes=64)
-            t0, t1 = (2 * (first % 2), 2 * (tiles[-1] % 2) + 2) if first < PACK else (first - PACK, tiles[-1] - PACK + 1)
-            for i, a in enumerate(passes):
-                nc.scalar.copy(
-                    out=rounded[:, i, :].rearrange("p (t m j) -> p m j t", t=t1 - t0, j=PACK),
-                    in_=raw[first // 2, a][:].rearrange("p j (m t) -> p m j t", t=PACK)[:, :, :, t0:t1],
-                )
-            return rounded
+        def rounded_tile(pair, a):
+            return keep.tile([P, 2, P, PACK], BF16, name=f"w_bf_{2 * pair}_{a}", align_bytes=256)
 
-        def quantize_w1(tiles, passes, rounded, slot=None):
-            words = len(tiles) * len(passes) * P
-            name = f"w_code_{tiles[0]}_{passes[0]}"
-            codes = keep.tile([P, words], U32, name=name, tag=slot or name, align_bytes=64)
-            scales = keep.tile([P, words], U8, name=f"w_scale_{tiles[0]}_{passes[0]}", align_bytes=64)
-            nc.vector.quantize_mx(
-                out=codes[:].bitcast(FP8X4), scales=scales[:], in_=rounded[:].rearrange("p a c -> p (a c)")
+        def round_w1(pair, a, rounded, part=0):
+            b, u = divmod(pair, 2)
+            source = raw[b, a][part]
+            count = source.shape[2] // PACK
+            nc.scalar.copy(
+                out=rounded[:, :, part * count : (part + 1) * count, :].rearrange("p t m j -> p m j t"),
+                in_=source[:].rearrange("p j (m t) -> p m j t", t=PACK)[:, :, :, 2 * u : 2 * u + 2],
             )
-            for i, a in enumerate(passes):
-                for n, ht in enumerate(tiles):
-                    columns = slice((i * len(tiles) + n) * P, (i * len(tiles) + n + 1) * P)
-                    operand[ht, a] = (codes[:, columns], scales[:, columns])
 
-        def prepare_w1(tiles, passes, slot=None):
-            quantize_w1(tiles, passes, round_w1(tiles, passes), slot)
-            for ht in tiles:
-                multiply_w(ht, *passes)
+        def quantize_w1(pair, a, rounded, t0=0, t1=2):
+            name = f"{2 * pair + t0}_{a}"
+            slot = "w_bf_0_1" if name == "2_0" else f"w_code_{name}"
+            codes = keep.tile([P, (t1 - t0) * P], U32, name=f"w_code_{name}", tag=slot, align_bytes=256)
+            scales = keep.tile([P, (t1 - t0) * P], U8, name=f"w_scale_{name}", align_bytes=256)
+            values = rounded[:, t0:t1, :, :].rearrange("p t m j -> p (t m j)")
+            nc.vector.quantize_mx(out=codes[:].bitcast(FP8X4), scales=scales[:], in_=values)
+            for t in range(t0, t1):
+                columns = slice((t - t0) * P, (t - t0 + 1) * P)
+                operand[2 * pair + t, a] = (codes[:, columns], scales[:, columns])
+                multiply_w(2 * pair + t, a)
+
+        def prepare_w1(pair, a):
+            rounded = rounded_tile(pair, a)
+            round_w1(pair, a, rounded)
+            quantize_w1(pair, a, rounded)
 
         h, banks = {}, {}
 
         def spans(ht):
-            if ht == 0:
-                return [(0, 0, BANK), (1, BANK, BANK + HALF), (7, BANK + HALF, S)]
             return [(2 * (ht % PACK), 0, BANK), (2 * (ht % PACK) + 1, BANK, S)]
 
         def multiply_w(ht, *passes):
@@ -188,67 +178,62 @@ def tile_list_precedent_ladder_kernel(
             h[ht] = keep.tile([P, S], F32, name=f"h{ht}")
             nc.scalar.activation(h[ht][:, 0:BANK], banks[ht][0][:], ACT.Identity, bias=row_bias[ht, 0])
             if ht == 0:
-                for side in (1, 2):
-                    n, e0, e1 = spans(ht)[side]
-                    nc.vector.tensor_scalar(h[ht][:, e0:e1], banks[ht][side][:], row_bias[ht, side], None, op0=ALU.add)
+                nc.vector.tensor_scalar(h[ht][:, BANK:S], banks[ht][1][:], row_bias[ht, 1], None, op0=ALU.add)
             else:
                 nc.scalar.activation(h[ht][:, BANK:S], banks[ht][1][:], ACT.Identity, bias=row_bias[ht, 1])
 
-        picked, right, z_bf, z_words = {}, {}, {}, {}
-        z32 = [keep.tile([P, PACK, PAIRS], F32, name=f"z32_{b}", align_bytes=64) for b in range(2)]
+        picked, right, z32, z_bf = {}, {}, {}, {}
+        z32[0, 0] = keep.tile([P, PACK, PAIRS], F32, name="z32_0", align_bytes=256)
 
-        def gather_right(ht, slot=None):
-            name = f"picked{ht}"
-            picked[ht] = keep.tile([P, PAIRS], F32, name=name, tag=slot or name, align_bytes=256)
+        def gather_right(ht):
+            picked[ht] = keep.tile([P, PAIRS], F32, name=f"picked{ht}", tag=f"picked{ht % 2}", align_bytes=256)
             nc.vector.tensor_copy(picked[ht][:], h[ht][:].indirect(p2[:]))
 
-        def positive_part(ht):
-            slot = f"right{ht}" if ht < H_TILES - 1 else "z32_0"
-            right[ht] = keep.tile([P, PAIRS], F32, name=f"right{ht}", tag=slot, align_bytes=64)
-            if ht < H_TILES - 1:
-                nc.gpsimd.tensor_scalar(right[ht][:], picked[ht][:], F32_MAX, 0.0, op0=ALU.min, op1=ALU.max)
+        def positive_part(ht, on_scalar=False, c0=0, c1=PAIRS, slot=None):
+            name = f"right{ht}" if c0 == 0 else f"right{ht}_{c0}"
+            right[ht, c0] = keep.tile([P, c1 - c0], F32, name=name, tag=slot or name, align_bytes=256)
+            if on_scalar:
+                nc.scalar.activation(right[ht, c0][:], picked[ht][:, c0:c1], ACT.Relu)
             else:
-                nc.scalar.activation(right[ht][:], picked[ht][:], ACT.Relu)
+                nc.gpsimd.tensor_scalar(right[ht, c0][:], picked[ht][:, c0:c1], F32_MAX, 0.0, op0=ALU.min, op1=ALU.max)
 
         def gather_left(ht, c0=0, c1=PAIRS):
             entries = p1[:, c0 // PER_COLUMN : c1 // PER_COLUMN]
-            if ht in (2, 3):
-                spare = keep.tile([P, PAIRS], F32, name=f"spare{ht}", align_bytes=64)
-                target = spare[:]
-            elif ht < 2:
-                target = z32[0][:, 2 * ht, :]
-            else:
-                target = z32[1][:, ht - PACK, c0:c1]
-            nc.vector.tensor_tensor(target, h[ht][:].indirect(entries), right[ht][:, c0:c1], ALU.subtract)
-            if ht < 2:
-                nc.sync.dma_start(z32[0][0:HALF_P, 2 * ht + 1, :], target[HALF_P:P, :])
-            elif ht < PACK:
-                t = 2 * (ht - 2)
-                nc.sync.dma_start(z32[0][HALF_P:P, t, :], target[0:HALF_P, :])
-                nc.sync.dma_start(z32[0][HALF_P:P, t + 1, :], target[HALF_P:P, :])
+            first = HALF if c0 >= HALF and (ht, HALF) in right else 0
+            plain = right[ht, first][:, c0 - first : c1 - first]
+            target = z32[ht // PACK, c0][:, ht % PACK, :]
+            nc.vector.tensor_tensor(target, h[ht][:].indirect(entries), plain, ALU.subtract)
 
-        def round_z(copy, b, c0, c1):
-            if c0 == 0:
-                z_words[b] = keep.tile([P, PAIRS * PACK], BF16, name=f"z_bf{b}", align_bytes=64)
-            z_bf[b, c0] = z_words[b][:, c0 * PACK : c1 * PACK]
+        def gather_piece(c0, c1, slot):
+            z32[1, c0] = keep.tile([P, PACK, c1 - c0], F32, name=f"z32_1_{c0}", tag=slot, align_bytes=256)
+            for ht in range(PACK, H_TILES):
+                gather_left(ht, c0, c1)
+
+        def round_z(copy, b, c0, values, rounded=None):
+            if rounded is None:
+                tile = keep.tile([P, values.shape[2] * PACK], BF16, name=f"z_bf{b}_{c0}", align_bytes=256)
+                rounded = tile[:]
+            z_bf[b, c0] = rounded
             copy(
                 out=z_bf[b, c0].rearrange("p (c i t) -> p c t i", i=LINE, t=PACK),
-                in_=z32[b][:, :, c0:c1].rearrange("p t (c i) -> p c t i", i=LINE),
+                in_=values.rearrange("p t (c i) -> p c t i", i=LINE),
             )
 
         y_banks = {}
 
-        def multiply_z(b, c0, last=()):
+        def multiply_z(b, c0, slot=None):
             width = z_bf[b, c0].shape[1] // PACK
-            codes = keep.tile([P, width], U32, name=f"z_code{b}_{c0}", align_bytes=64)
-            scales = keep.tile([P, width], U8, name=f"z_scale{b}_{c0}", align_bytes=64)
+            name = f"z_code{b}_{c0}"
+            codes = keep.tile([P, width], U32, name=name, tag=slot or name, align_bytes=256)
+            scales = keep.tile([P, width], U8, name=f"z_scale{b}_{c0}", align_bytes=256)
             nc.vector.quantize_mx(out=codes[:].bitcast(FP8X4), scales=scales[:], in_=z_bf[b, c0])
-            side = c0 // HALF
             for i in range(Y_TILES):
-                if b == 0:
-                    y_banks[i, side] = psum.tile([P, HALF], F32, name=f"bank{2 * i + side}")
+                if (b, c0) == (0, 0):
+                    y_banks[i, 0] = psum.tile([P, LAST], F32, name=f"bank{i}")
+                if (b, c0) == (0, HALF):
+                    y_banks[i, 1] = psum.tile([P, QUARTER], F32, name=f"bank{Y_TILES + i}")
                 for c in range(0, width, QUARTER):
-                    column = (c0 + c) % HALF
+                    side, column = divmod(c0 + c, LAST)
                     nc.tensor.matmul_mx(
                         out=y_banks[i, side][:, column : column + QUARTER],
                         lhsT=w4_w[:, b, 2 * P * i : 2 * P * (i + 1)].bitcast(FP4X4),
@@ -256,27 +241,26 @@ def tile_list_precedent_ladder_kernel(
                         rhs=codes[:, c : c + QUARTER].bitcast(FP8X4),
                         rhs_scale=scales[:, c : c + QUARTER],
                         start=(b == 0 and column == 0),
-                        stop=(b == 1 and column == QUARTER),
+                        stop=(b == 1 and c0 >= HALF),
                     )
 
         nc.vector.tensor_copy(v_w[0][:], tab_w[0][:].bitcast(U32).indirect(idx[:]))
         nc.vector.tensor_copy(v_s[:], tab_s[:].indirect(idx[:]))
-        for a in range(2):
-            quantize_w1((0, 1), (a,), round_w1((0, 1), (a,)))
-        multiply_w(0, 0)
-        multiply_w(1, 0)
-        for n, e0, e1 in spans(0):
-            entries = idx[:, e0 // PER_COLUMN : e1 // PER_COLUMN]
-            nc.vector.tensor_copy(v_w[1][:, e0:e1], tab_w[1][:].bitcast(U32).indirect(entries))
-        multiply_w(0, 1)
-        multiply_w(1, 1)
-        rounded = round_w1((2, 3), (0,))
+        prepare_w1(0, 0)
+        nc.vector.tensor_copy(v_w[1][:], tab_w[1][:].bitcast(U32).indirect(idx[:]))
+        waiting = rounded_tile(1, 0)
+        round_w1(1, 0, waiting)
+        rounded = [rounded_tile(pair, 1) for pair in range(2)]
+        for part in range(2):
+            round_w1(0, 1, rounded[0], part)
+        quantize_w1(0, 1, rounded[0], 0, 1)
+        quantize_w1(0, 1, rounded[0], 1, 2)
+        quantize_w1(1, 0, waiting)
+        for part in range(2):
+            round_w1(1, 1, rounded[1], part)
+        quantize_w1(1, 1, rounded[1])
         empty_h(0)
-        quantize_w1((2, 3), (0,), rounded)
-        multiply_w(2, 0)
-        multiply_w(3, 0)
         gather_right(0)
-        prepare_w1((2,), (1,), "w_bf_2_0")
 
         def step(ht):
             empty_h(ht)
@@ -285,35 +269,45 @@ def tile_list_precedent_ladder_kernel(
             gather_left(ht - 1)
 
         step(1)
-        prepare_w1((3,), (1,))
+        prepare_w1(2, 0)
         step(2)
-        prepare_w1((4, 5), (0, 1))
+        prepare_w1(2, 1)
         step(3)
-        prepare_w1((6, 7), (0,))
-        step(4)
-        prepare_w1((6, 7), (1,))
-        for ht in range(5, H_TILES):
-            step(ht)
-        round_z(nc.scalar.copy, 0, 0, HALF)
-        round_z(nc.scalar.copy, 0, HALF, PAIRS)
-        positive_part(H_TILES - 1)
+        prepare_w1(3, 0)
+        empty_h(4)
+        gather_right(4)
+        prepare_w1(3, 1)
+        positive_part(3, on_scalar=True)
+        gather_left(3)
+        z32[1, 0] = keep.tile([P, PACK, HALF], F32, name="z32_1_0", align_bytes=256)
+        for ht in (5, 6, 7):
+            empty_h(ht)
+            gather_right(ht)
+            positive_part(ht - 1)
+            gather_left(ht - 1, 0, HALF)
+        whole = keep.tile([P, PAIRS * PACK], BF16, name="z_bf0_0", align_bytes=256)
+        for c0 in (0, HALF):
+            round_z(nc.scalar.copy, 0, c0, z32[0, 0][:, :, c0 : c0 + HALF], whole[:, c0 * PACK : (c0 + HALF) * PACK])
         multiply_z(0, 0)
-        multiply_z(0, HALF)
-        pieces = ((0, QUARTER), (HALF, PAIRS), (QUARTER, HALF))
-        for c0, c1 in pieces:
-            gather_left(H_TILES - 1, c0, c1)
-        round_z(nc.scalar.copy, 1, 0, QUARTER)
-        round_z(nc.scalar.copy, 1, HALF, PAIRS)
-        round_z(nc.vector.tensor_copy, 1, QUARTER, HALF)
+        positive_part(7, True, 0, HALF)
+        positive_part(7, True, HALF, PAIRS)
+        gather_left(7, 0, HALF)
+        round_z(nc.scalar.copy, 1, 0, z32[1, 0][:])
+        gather_piece(HALF, LAST, "picked1")
+        multiply_z(0, HALF, "right7")
+        round_z(nc.scalar.copy, 1, HALF, z32[1, HALF][:])
         multiply_z(1, 0)
-        multiply_z(1, QUARTER)
+        gather_piece(LAST, PAIRS, "z32_1_0")
         multiply_z(1, HALF)
+        round_z(nc.vector.tensor_copy, 1, LAST, z32[1, LAST][:])
+        multiply_z(1, LAST)
 
         y = [keep.tile([P, PAIRS], F32, name=f"y{i}") for i in range(Y_TILES)]
         for i in range(Y_TILES):
-            nc.scalar.copy(y[i][:, 0:HALF], y_banks[i, 0][:])
-            copy = nc.vector.tensor_copy if i == 0 else nc.scalar.copy
-            copy(y[i][:, HALF:PAIRS], y_banks[i, 1][:])
+            nc.scalar.copy(y[i][:, 0:LAST], y_banks[i, 0][:])
+        nc.vector.tensor_copy(y[0][:, LAST:PAIRS], y_banks[0, 1][:])
+        for i in range(1, Y_TILES):
+            nc.scalar.copy(y[i][:, LAST:PAIRS], y_banks[i, 1][:])
 
         first_line = {}
 

@@ -89,15 +89,15 @@ def tile_list_precedent_ladder_kernel(
             for ht in range(ht0, ht1):
                 row_bias[ht] = tile[:, ht - ht0 : ht - ht0 + 1]
 
-        load_bias(nc.gpsimd, 0, 2, "bias_first")
-        load_bias(nc.gpsimd, 4, 8, "bias_second")
-        p2 = load_list(pos2, "p2")
+        load_bias(nc.sync, 0, 2, "bias_first")
         tab_w.append(load_table_words(1))
-        raw[0, 1] = [load_w1(1, c0, HALF) for c0 in (0, HALF)]
+        raw[0, 1] = [load_w1(1, 0, LAST), load_w1(1, LAST, QUARTER)]
+        p2 = load_list(pos2, "p2")
         p1 = load_list(pos1, "p1")
         for a, slot in enumerate(("w_bf_4_1", "w_bf_6_0")):
             raw[1, a] = [load_w1(a, PASS, PASS)]
             load_bias(nc.sync, 2 + a, 3 + a, slot)
+        load_bias(nc.sync, 4, 8, "bias_second")
         w4_w = keep.tile([P, 2, 2 * N], U8, name="w4_w", align_bytes=256)
         nc.sync.dma_start(w4_w[:].bitcast(I32), w4_words.rearrange("a p c -> p a c").bitcast(I32))
         for q in range(QUADS):
@@ -112,11 +112,11 @@ def tile_list_precedent_ladder_kernel(
             nc.sync.dma_start(gain[:], gn.rearrange("(i p) -> p i", p=P))
 
         for ht in range(H_TILES):
-            for side in range(2):
+            for side in range(PACK):
                 row_bias[ht, side] = row_bias[ht]
         for ht, side, slot in BIAS_SLOTS:
             held = keep.tile([P, 1], F32, name=f"bias{ht}{side}", tag=slot, align_bytes=256)
-            copy = nc.scalar.copy if ht in (2, 3) else nc.gpsimd.tensor_copy
+            copy = nc.scalar.copy if ht >= 2 else nc.gpsimd.tensor_copy
             copy(held[:], row_bias[ht, side])
             row_bias[ht, side] = held[:]
 
@@ -132,14 +132,15 @@ def tile_list_precedent_ladder_kernel(
             b, u = divmod(pair, 2)
             source = raw[b, a][part]
             count = source.shape[2] // PACK
+            first = P - count if part else 0
             nc.scalar.copy(
-                out=rounded[:, :, part * count : (part + 1) * count, :].rearrange("p t m j -> p m j t"),
+                out=rounded[:, :, first : first + count, :].rearrange("p t m j -> p m j t"),
                 in_=source[:].rearrange("p j (m t) -> p m j t", t=PACK)[:, :, :, 2 * u : 2 * u + 2],
             )
 
         def quantize_w1(pair, a, rounded, t0=0, t1=2):
             name = f"{2 * pair + t0}_{a}"
-            slot = "w_bf_0_1" if name == "2_0" else f"w_code_{name}"
+            slot = "tab_s" if name == "2_0" else f"w_code_{name}"
             codes = keep.tile([P, (t1 - t0) * P], U32, name=f"w_code_{name}", tag=slot, align_bytes=256)
             scales = keep.tile([P, (t1 - t0) * P], U8, name=f"w_scale_{name}", align_bytes=256)
             values = rounded[:, t0:t1, :, :].rearrange("p t m j -> p (t m j)")
@@ -157,6 +158,8 @@ def tile_list_precedent_ladder_kernel(
         h, banks = {}, {}
 
         def spans(ht):
+            if ht == 0:
+                return [(n, i * HALF, (i + 1) * HALF) for i, n in enumerate((4, 5, 6, 7))]
             return [(2 * (ht % PACK), 0, BANK), (2 * (ht % PACK) + 1, BANK, S)]
 
         def multiply_w(ht, *passes):
@@ -174,13 +177,13 @@ def tile_list_precedent_ladder_kernel(
                         stop=(a == 1),
                     )
 
-        def empty_h(ht, slot=""):
+        def empty_h(ht):
             h[ht] = keep.tile([P, S], F32, name=f"h{ht}")
-            nc.scalar.activation(h[ht][:, 0:BANK], banks[ht][0][:], ACT.Identity, bias=row_bias[ht, 0])
-            if ht == 0:
-                nc.vector.tensor_scalar(h[ht][:, BANK:S], banks[ht][1][:], row_bias[ht, 1], None, op0=ALU.add)
-            else:
-                nc.scalar.activation(h[ht][:, BANK:S], banks[ht][1][:], ACT.Identity, bias=row_bias[ht, 1])
+            for side, (n, e0, e1) in enumerate(spans(ht)):
+                if ht == 0 and side % 2:
+                    nc.vector.tensor_scalar(h[ht][:, e0:e1], banks[ht][side][:], row_bias[ht, side], None, op0=ALU.add)
+                else:
+                    nc.scalar.activation(h[ht][:, e0:e1], banks[ht][side][:], ACT.Identity, bias=row_bias[ht, side])
 
         picked, right, z32, z_bf = {}, {}, {}, {}
         z32[0, 0] = keep.tile([P, PACK, PAIRS], F32, name="z32_0", align_bytes=256)

@@ -94,12 +94,13 @@ def tile_list_precedent_ladder_kernel(
         raw[0, 1] = [load_w1(1, 0, LAST), load_w1(1, LAST, QUARTER)]
         p2 = load_list(pos2, "p2")
         p1 = load_list(pos1, "p1")
-        for a, slot in enumerate(("w_bf_4_1", "w_bf_6_0")):
-            raw[1, a] = [load_w1(a, PASS, PASS)]
-            load_bias(nc.sync, 2 + a, 3 + a, slot)
-        load_bias(nc.sync, 4, 8, "bias_second")
+        raw[1, 0] = [load_w1(0, PASS, PASS)]
+        load_bias(nc.sync, 2, 3, "w_bf_4_1")
         w4_w = keep.tile([P, 2, 2 * N], U8, name="w4_w", align_bytes=256)
         nc.sync.dma_start(w4_w[:].bitcast(I32), w4_words.rearrange("a p c -> p a c").bitcast(I32))
+        raw[1, 1] = [load_w1(1, PASS, PASS)]
+        load_bias(nc.sync, 3, 4, "w_bf_6_0")
+        load_bias(nc.sync, 4, 8, "bias_second")
         for q in range(QUADS):
             nc.sync.dma_start(
                 w4_s[32 * q : 32 * q + 4, :, :].bitcast(I32),

@@ -309,9 +309,9 @@ def tile_list_precedent_ladder_kernel(
         y = [keep.tile([P, PAIRS], F32, name=f"y{i}") for i in range(Y_TILES)]
         for i in range(Y_TILES):
             nc.scalar.copy(y[i][:, 0:LAST], y_banks[i, 0][:])
-        nc.vector.tensor_copy(y[0][:, LAST:PAIRS], y_banks[0, 1][:])
-        for i in range(1, Y_TILES):
-            nc.scalar.copy(y[i][:, LAST:PAIRS], y_banks[i, 1][:])
+        for i in range(Y_TILES):
+            copy = nc.vector.tensor_copy if i < Y_TILES - 1 else nc.scalar.copy
+            copy(y[i][:, LAST:PAIRS], y_banks[i, 1][:])
 
         first_line = {}
 

@@ -96,11 +96,11 @@ def tile_list_precedent_ladder_kernel(
         p1 = load_list(pos1, "p1")
         raw[1, 0] = [load_w1(0, PASS, PASS)]
         load_bias(nc.sync, 2, 3, "w_bf_4_1")
-        w4_w = keep.tile([P, 2, 2 * N], U8, name="w4_w", align_bytes=256)
-        nc.sync.dma_start(w4_w[:].bitcast(I32), w4_words.rearrange("a p c -> p a c").bitcast(I32))
         raw[1, 1] = [load_w1(1, PASS, PASS)]
         load_bias(nc.sync, 3, 4, "w_bf_6_0")
         load_bias(nc.sync, 4, 8, "bias_second")
+        w4_w = keep.tile([P, 2, 2 * N], U8, name="w4_w", align_bytes=256)
+        nc.sync.dma_start(w4_w[:].bitcast(I32), w4_words.rearrange("a p c -> p a c").bitcast(I32))
         for q in range(QUADS):
             nc.sync.dma_start(
                 w4_s[32 * q : 32 * q + 4, :, :].bitcast(I32),

@@ -225,28 +225,39 @@ def tile_list_precedent_ladder_kernel(
 
         y_banks = {}
 
-        def multiply_z(b, c0, slot=None):
+        z_mx = {}
+
+        def quantize_z(b, c0, slot=None):
             width = z_bf[b, c0].shape[1] // PACK
             name = f"z_code{b}_{c0}"
             codes = keep.tile([P, width], U32, name=name, tag=slot or name, align_bytes=256)
             scales = keep.tile([P, width], U8, name=f"z_scale{b}_{c0}", align_bytes=256)
             nc.vector.quantize_mx(out=codes[:].bitcast(FP8X4), scales=scales[:], in_=z_bf[b, c0])
+            z_mx[b, c0] = (codes, scales, width)
+
+        def multiply_tile(b, c0, i):
+            codes, scales, width = z_mx[b, c0]
+            if (b, c0) == (0, 0):
+                y_banks[i, 0] = psum.tile([P, LAST], F32, name=f"bank{i}")
+            if (b, c0) == (0, HALF):
+                y_banks[i, 1] = psum.tile([P, QUARTER], F32, name=f"bank{Y_TILES + i}")
+            step = HALF if c0 == 0 else QUARTER
+            for c in range(0, width, step):
+                side, column = divmod(c0 + c, LAST)
+                nc.tensor.matmul_mx(
+                    out=y_banks[i, side][:, column : column + step],
+                    lhsT=w4_w[:, b, 2 * P * i : 2 * P * (i + 1)].bitcast(FP4X4),
+                    lhsT_scale=w4_s[:, b, P * i : P * (i + 1)],
+                    rhs=codes[:, c : c + step].bitcast(FP8X4),
+                    rhs_scale=scales[:, c : c + step],
+                    start=(b == 0 and column == 0),
+                    stop=(b == 1 and c0 >= HALF),
+                )
+
+        def multiply_z(b, c0, slot=None):
+            quantize_z(b, c0, slot)
             for i in range(Y_TILES):
-                if (b, c0) == (0, 0):
-                    y_banks[i, 0] = psum.tile([P, LAST], F32, name=f"bank{i}")
-                if (b, c0) == (0, HALF):
-                    y_banks[i, 1] = psum.tile([P, QUARTER], F32, name=f"bank{Y_TILES + i}")
-                for c in range(0, width, QUARTER):
-                    side, column = divmod(c0 + c, LAST)
-                    nc.tensor.matmul_mx(
-                        out=y_banks[i, side][:, column : column + QUARTER],
-                        lhsT=w4_w[:, b, 2 * P * i : 2 * P * (i + 1)].bitcast(FP4X4),
-                        lhsT_scale=w4_s[:, b, P * i : P * (i + 1)],
-                        rhs=codes[:, c : c + QUARTER].bitcast(FP8X4),
-                        rhs_scale=scales[:, c : c + QUARTER],
-                        start=(b == 0 and column == 0),
-                        stop=(b == 1 and c0 >= HALF),
-                    )
+                multiply_tile(b, c0, i)
 
         nc.vector.tensor_copy(v_w[0][:], tab_w[0][:].bitcast(U32).indirect(idx[:]))
         nc.vector.tensor_copy(v_s[:], tab_s[:].indirect(idx[:]))
@@ -297,14 +308,23 @@ def tile_list_precedent_ladder_kernel(
         positive_part(7, True, HALF, PAIRS)
         gather_left(7, 0, HALF)
         round_z(nc.scalar.copy, 1, 0, z32[1, 0][:])
-        gather_piece(HALF, LAST, "picked1")
         multiply_z(0, HALF, "right7")
+        gather_piece(HALF, LAST, "picked1")
         round_z(nc.scalar.copy, 1, HALF, z32[1, HALF][:])
         multiply_z(1, 0)
         gather_piece(LAST, PAIRS, "z32_1_0")
-        multiply_z(1, HALF)
-        round_z(nc.vector.tensor_copy, 1, LAST, z32[1, LAST][:])
-        multiply_z(1, LAST)
+        last_bf = keep.tile([P, QUARTER, PACK], BF16, name="z_bf_last", tag="right6", align_bytes=256)
+        for t0 in (0, 2):
+            nc.vector.tensor_copy(
+                out=last_bf[:, :, t0 : t0 + 2].rearrange("p (c i) t -> p c t i", i=LINE),
+                in_=z32[1, LAST][:, t0 : t0 + 2, :].rearrange("p t (c i) -> p c t i", i=LINE),
+            )
+        z_bf[1, LAST] = last_bf[:].rearrange("p c t -> p (c t)")
+        quantize_z(1, HALF, "right7_256")
+        quantize_z(1, LAST)
+        for i in range(Y_TILES):
+            for c0 in (HALF, LAST):
+                multiply_tile(1, c0, i)
 
         y = [keep.tile([P, PAIRS], F32, name=f"y{i}") for i in range(Y_TILES)]
         for i in range(Y_TILES):

@@ -235,23 +235,28 @@ def tile_list_precedent_ladder_kernel(
             nc.vector.quantize_mx(out=codes[:].bitcast(FP8X4), scales=scales[:], in_=z_bf[b, c0])
             z_mx[b, c0] = (codes, scales, width)
 
+        def y_place(i, c):
+            if i == 0:
+                return {0: (0, HALF, 0), HALF: (4, QUARTER, 0), LAST: (5, QUARTER, 0)}[c]
+            if i == Y_TILES - 1:
+                return (i, PAIRS, c)
+            return (i, LAST, c) if c < LAST else (5 + i, QUARTER, 0)
+
         def multiply_tile(b, c0, i):
             codes, scales, width = z_mx[b, c0]
-            if (b, c0) == (0, 0):
-                y_banks[i, 0] = psum.tile([P, LAST], F32, name=f"bank{i}")
-            if (b, c0) == (0, HALF):
-                y_banks[i, 1] = psum.tile([P, QUARTER], F32, name=f"bank{Y_TILES + i}")
             step = HALF if c0 == 0 else QUARTER
             for c in range(0, width, step):
-                side, column = divmod(c0 + c, LAST)
+                n, span, column = y_place(i, c0 + c)
+                if n not in y_banks:
+                    y_banks[n] = psum.tile([P, span], F32, name=f"bank{n}")
                 nc.tensor.matmul_mx(
-                    out=y_banks[i, side][:, column : column + step],
+                    out=y_banks[n][:, column : column + step],
                     lhsT=w4_w[:, b, 2 * P * i : 2 * P * (i + 1)].bitcast(FP4X4),
                     lhsT_scale=w4_s[:, b, P * i : P * (i + 1)],
                     rhs=codes[:, c : c + step].bitcast(FP8X4),
                     rhs_scale=scales[:, c : c + step],
                     start=(b == 0 and column == 0),
-                    stop=(b == 1 and c0 >= HALF),
+                    stop=(b == 1 and column + step == span),
                 )
 
         def multiply_z(b, c0, slot=None):
@@ -327,12 +332,16 @@ def tile_list_precedent_ladder_kernel(
                 multiply_tile(1, c0, i)
 
         y = [keep.tile([P, PAIRS], F32, name=f"y{i}") for i in range(Y_TILES)]
-        for i in range(Y_TILES):
-            nc.scalar.copy(y[i][:, 0:LAST], y_banks[i, 0][:])
-        for i in range(Y_TILES):
-            copy = nc.vector.tensor_copy if i < Y_TILES - 1 else nc.scalar.copy
-            copy(y[i][:, LAST:PAIRS], y_banks[i, 1][:])
+        nc.scalar.copy(y[0][:, 0:HALF], y_banks[0][:])
+        nc.scalar.copy(y[0][:, HALF:LAST], y_banks[4][:])
+        for i in range(1, Y_TILES):
+            nc.scalar.copy(y[i][:, 0 : y_place(i, 0)[1]], y_banks[i][:])
 
+        def empty_last(i):
+            nc.vector.tensor_copy(y[i][:, LAST:PAIRS], y_banks[5 + i][:])
+
+        empty_last(0)
+        empty_last(1)
         first_line = {}
 
         def gather_first_line(i):
@@ -348,6 +357,7 @@ def tile_list_precedent_ladder_kernel(
             nc.sync.dma_start(out[i * P : (i + 1) * P, c0:c1], result[:])
 
         gather_first_line(0)
+        empty_last(2)
         for i in range(1, Y_TILES):
             gather_first_line(i)
             finish(i - 1, 0, LINES)

@@ -1,6 +1,7 @@
 from contextlib import ExitStack
 
 import concourse.mybir as mybir
+from concourse.masks import make_identity
 
 K, T, S, H, PAIRS, N, LINES = 1024, 2048, 1024, 1024, 512, 512, 256
 FLOPS = 2 * K * H * S + 2 * H * N * PAIRS
@@ -17,11 +18,11 @@ ACT = mybir.ActivationFunctionType
 ALU = mybir.AluOpType
 
 P = 128
-HALF_P = P // 2
 PACK = 4
 PASS = P * PACK
 BANK = 512
 QUADS = 4
+QUAD = P // QUADS
 PER_COLUMN = 16
 LINE = 4
 Y_TILES = N // P
@@ -29,18 +30,60 @@ H_TILES = H // P
 F32_MAX = 3.4028234663852886e38
 HALF, QUARTER = PAIRS // 2, PAIRS // 4
 LAST = PAIRS - QUARTER
-BIAS_SLOTS = (
-    (1, 0, "w_bf_4_0"),
-    (1, 1, "right0"),
-    (2, 1, "right1"),
-    (3, 1, "right2"),
-    (4, 0, "w_bf_6_1"),
-    (4, 1, "right3"),
-    (5, 1, "right4"),
-    (6, 1, "right5"),
-    (7, 0, "z_bf0_0"),
-    (7, 1, "right6"),
-)
+KB = 1024
+
+PLACE = {
+    "tab_w0": 1 * KB,
+    "raw1_1": 0,
+    "picked0_0": 0,
+    "raw2_0": 2 * KB,
+    "raw2_1": 4 * KB,
+    "h1": 1 * KB,
+    "z0_0": 5 * KB,
+    "raw3": 6 * KB,
+    "z0_256": 6 * KB,
+    "h2": 7 * KB,
+    "tab_w1": 21 * KB,
+    "wide0": 13 * KB + 256,
+    "w4_w": 23 * KB + 256,
+    "w4_s": 25 * KB + 256,
+    "wide1": 26 * KB + 256,
+    "gain": 26 * KB + 256,
+    "z32_1_0": 70 * KB,
+    "z32_1_384": 70 * KB,
+    "picked3_0": 74 * KB,
+    "rounded4_0": 75 * KB,
+    "right2_0": 76 * KB,
+    "raw0_0": 78 * KB,
+    "v_w1_1": 78 * KB,
+    "bias1_0": 35 * KB,
+    "rounded3": 35 * KB,
+    "bias1_1": 37 * KB,
+    "right0_256": 37 * KB,
+    "bias2_1": 38 * KB,
+    "right1_0": 38 * KB,
+    "rounded4_1": 42 * KB,
+    "z2_0": 42 * KB,
+    "right3_0": 28 * KB,
+    "bias4_0": 46 * KB,
+    "rounded6_0": 46 * KB,
+    "bias5_1": 50 * KB,
+    "right4_0": 50 * KB,
+    "bias6_1": 52 * KB,
+    "right5_0": 52 * KB,
+    "bias7_1": 54 * KB,
+    "right6_0": 54 * KB,
+    "z_bf_last": 54 * KB,
+    "bias7_0": 56 * KB,
+    "z_bf0": 56 * KB,
+    "picked7_0": 60 * KB,
+    "z32_1_256": 60 * KB,
+    "z32_0": 62 * KB,
+    "right7_0": 62 * KB,
+    "z_code0_256": 62 * KB,
+    "right7_256": 63 * KB,
+    "z_code1_256": 63 * KB,
+}
 
 
 def tile_list_precedent_ladder_kernel(
@@ -50,7 +93,13 @@ def tile_list_precedent_ladder_kernel(
     with ExitStack() as ctx:
         lists = ctx.enter_context(tc.tile_pool(name="lists", bufs=1))
         keep = ctx.enter_context(tc.tile_pool(name="keep", bufs=1))
+        reused = ctx.enter_context(tc.tile_pool(name="reused", bufs=1))
         psum = ctx.enter_context(tc.psum_pool(name="psum", bufs=1))
+
+        def sbuf(name, shape, dtype):
+            if name in PLACE:
+                return reused.tile(shape, dtype, name=name, align_bytes=256, offset=PLACE[name])
+            return keep.tile(shape, dtype, name=name, align_bytes=256)
 
         def load_list(src, name):
             tile = lists.tile(list(src.shape), U16, name=name)
@@ -58,180 +107,185 @@ def tile_list_precedent_ladder_kernel(
             return tile
 
         def load_table_words(a):
-            tile = keep.tile([P, T], I32, name=f"tab_w{a}", align_bytes=256)
+            tile = sbuf(f"tab_w{a}", [P, T], I32)
             nc.sync.dma_start(tile[:], tab_words[a].rearrange("p t i -> p (t i)").bitcast(I32))
             return tile
 
-        def load_w1(a, c0, width):
-            raw = keep.tile([P, PACK, width], F32, name=f"w1_raw_{a}_{c0}", align_bytes=256)
+        def load_w1(target, a, c0, width):
             rows = w1[a * PASS : (a + 1) * PASS, c0 : c0 + width]
-            nc.sync.dma_start(raw[:], rows.rearrange("(p j) c -> p j c", j=PACK))
+            nc.sync.dma_start(target, rows.rearrange("(p j) c -> p j c", j=PACK))
+
+        def new_raw(name, a, c0, width):
+            raw = sbuf(name, [P, PACK, width], F32)
+            load_w1(raw[:], a, c0, width)
             return raw
 
-        tab_s = keep.tile([P, T], U8, name="tab_s", align_bytes=256)
-        w4_s = keep.tile([P, 2, N], U8, name="w4_s", align_bytes=256)
-        nc.vector.memset(tab_s[:].bitcast(I32), 0)
-        for q in range(QUADS):
+        bias_rows = sbuf("bias_rows", [P, PASS], F32)
+        tab_s = sbuf("tab_s", [P, T], U8)
+        nc.vector.memset(bias_rows[:], 0.0)
+        nc.vector.memset(tab_s[QUAD : 2 * QUAD, :].bitcast(I32), 0)
+        nc.vector.memset(tab_s[2 * QUAD : P, :].bitcast(I32), 0)
+        identity = sbuf("identity", [P, P], F32)
+        make_identity(nc, identity[:])
+        nc.gpsimd.dma_start(bias_rows[0:2, :], b1.rearrange("(b c) -> b c", b=2))
+
+        for a in range(2):
             nc.sync.dma_start(
-                tab_s[32 * q : 32 * q + 8, :].bitcast(I32), tab_scales[:, 4 * q : 4 * q + 4, :].bitcast(I32)
+                tab_s[16 * a : 16 * (a + 1), :].bitcast(I32),
+                tab_scales[a].rearrange("(q r) c -> r q c", r=4).bitcast(I32),
             )
-        tab_w = [load_table_words(0)]
         idx = load_list(offs, "idx")
-        raw = {(0, 0): [load_w1(0, 0, PASS)]}
-        dealt_bias = b1.rearrange("(b p t) -> b p t", b=2, t=PACK)
-        row_bias = {}
-
-        def load_bias(queue, ht0, ht1, slot):
-            b, t = divmod(ht0, PACK)
-            tile = keep.tile([P, ht1 - ht0], F32, name=f"bias_from{ht0}", tag=slot, align_bytes=256)
-            with nc.allow_non_contiguous_dma(reason="a few values of the bias a partition"):
-                queue.dma_start(tile[:], dealt_bias[b, :, t : t + ht1 - ht0])
-            for ht in range(ht0, ht1):
-                row_bias[ht] = tile[:, ht - ht0 : ht - ht0 + 1]
-
-        load_bias(nc.sync, 0, 2, "bias_first")
-        tab_w.append(load_table_words(1))
-        raw[0, 1] = [load_w1(1, 0, LAST), load_w1(1, LAST, QUARTER)]
         p2 = load_list(pos2, "p2")
         p1 = load_list(pos1, "p1")
-        raw[1, 0] = [load_w1(0, PASS, PASS)]
-        load_bias(nc.sync, 2, 3, "w_bf_4_1")
-        raw[1, 1] = [load_w1(1, PASS, PASS)]
-        load_bias(nc.sync, 3, 4, "w_bf_6_0")
-        load_bias(nc.sync, 4, 8, "bias_second")
-        w4_w = keep.tile([P, 2, 2 * N], U8, name="w4_w", align_bytes=256)
-        nc.sync.dma_start(w4_w[:].bitcast(I32), w4_words.rearrange("a p c -> p a c").bitcast(I32))
-        for q in range(QUADS):
-            nc.sync.dma_start(
-                w4_s[32 * q : 32 * q + 4, :, :].bitcast(I32),
-                w4_scales[:, 4 * q : 4 * q + 4, :].rearrange("a r c -> r a c").bitcast(I32),
-            )
+        tab_w = [load_table_words(0)]
         p3 = load_list(pos3, "p3")
         p4 = load_list(pos4, "p4")
-        gain = keep.tile([P, Y_TILES], F32, name="gain")
-        with nc.allow_non_contiguous_dma(reason="one gain a partition"):
-            nc.sync.dma_start(gain[:], gn.rearrange("(i p) -> p i", p=P))
+        tab_w.append(load_table_words(1))
+        raw = {(u, a): new_raw(f"raw{u}_{a}", a, u * P, P) for u, a in ((0, 0), (0, 1), (1, 0))}
 
+        words = {0: [], 1: []}
+
+        def entries(tile, c0, c1):
+            return tile[:, c0 // PER_COLUMN : c1 // PER_COLUMN]
+
+        def gather_words(a, name, c0, c1):
+            tile = sbuf(name, [P, c1 - c0], U32)
+            nc.vector.tensor_copy(tile[:], tab_w[a][:].bitcast(U32).indirect(entries(idx, c0, c1)))
+            words[a].append((tile, c0, c1))
+
+        v_rows = sbuf("v_rows", [P, S], U8)
+        v_s = sbuf("v_s", [P, S], U8)
+        nc.vector.tensor_copy(v_rows[:], tab_s[:].indirect(idx[:]))
+        for q in range(QUADS):
+            nc.scalar.dma_start(v_s[QUAD * q : QUAD * q + 8, :].bitcast(I32), v_rows[q:QUAD:4, :].bitcast(I32))
+        gather_words(0, "v_w0", 0, S)
+        gather_words(1, "v_w1_0", 0, S - HALF)
+
+        turned = [psum.tile([P, PACK, P], F32, name=f"bank{2 + b}") for b in range(2)]
+        bias = sbuf("bias", [P, H_TILES], F32)
+        for t in range(PACK):
+            nc.tensor.transpose(turned[0][:, t, :], bias_rows[:, t * P : (t + 1) * P], identity[:])
+        for t in range(PACK):
+            nc.tensor.transpose(turned[1][:, t, :], bias_rows[:, t:PASS:PACK], identity[:])
+        for b in range(2):
+            nc.scalar.copy(bias[:, PACK * b : PACK * (b + 1)], turned[b][:, :, b])
+        row_bias = {}
         for ht in range(H_TILES):
-            for side in range(PACK):
-                row_bias[ht, side] = row_bias[ht]
-        for ht, side, slot in BIAS_SLOTS:
-            held = keep.tile([P, 1], F32, name=f"bias{ht}{side}", tag=slot, align_bytes=256)
-            copy = nc.scalar.copy if ht >= 2 else nc.gpsimd.tensor_copy
-            copy(held[:], row_bias[ht, side])
-            row_bias[ht, side] = held[:]
+            for side in range(2):
+                row_bias[ht, side] = bias[:, ht : ht + 1]
+                if f"bias{ht}_{side}" in PLACE:
+                    held = sbuf(f"bias{ht}_{side}", [P, 1], F32)
+                    nc.gpsimd.tensor_copy(held[:], bias[:, ht : ht + 1])
+                    row_bias[ht, side] = held[:]
 
-        v_w = [keep.tile([P, S], U32, name=f"v_w{a}", align_bytes=256) for a in range(2)]
-        v_s = keep.tile([P, S], U8, name="v_s", align_bytes=256)
 
-        operand = {}
-
-        def rounded_tile(pair, a):
-            return keep.tile([P, 2, P, PACK], BF16, name=f"w_bf_{2 * pair}_{a}", align_bytes=256)
-
-        def round_w1(pair, a, rounded, part=0):
-            b, u = divmod(pair, 2)
-            source = raw[b, a][part]
-            count = source.shape[2] // PACK
-            first = P - count if part else 0
-            nc.scalar.copy(
-                out=rounded[:, :, first : first + count, :].rearrange("p t m j -> p m j t"),
-                in_=source[:].rearrange("p j (m t) -> p m j t", t=PACK)[:, :, :, 2 * u : 2 * u + 2],
-            )
-
-        def quantize_w1(pair, a, rounded, t0=0, t1=2):
-            name = f"{2 * pair + t0}_{a}"
-            slot = "tab_s" if name == "2_0" else f"w_code_{name}"
-            codes = keep.tile([P, (t1 - t0) * P], U32, name=f"w_code_{name}", tag=slot, align_bytes=256)
-            scales = keep.tile([P, (t1 - t0) * P], U8, name=f"w_scale_{name}", align_bytes=256)
-            values = rounded[:, t0:t1, :, :].rearrange("p t m j -> p (t m j)")
-            nc.vector.quantize_mx(out=codes[:].bitcast(FP8X4), scales=scales[:], in_=values)
-            for t in range(t0, t1):
-                columns = slice((t - t0) * P, (t - t0 + 1) * P)
-                operand[2 * pair + t, a] = (codes[:, columns], scales[:, columns])
-                multiply_w(2 * pair + t, a)
-
-        def prepare_w1(pair, a):
-            rounded = rounded_tile(pair, a)
-            round_w1(pair, a, rounded)
-            quantize_w1(pair, a, rounded)
-
-        h, banks = {}, {}
+        operand, h, banks = {}, {}, {}
 
         def spans(ht):
             if ht == 0:
                 return [(n, i * HALF, (i + 1) * HALF) for i, n in enumerate((4, 5, 6, 7))]
             return [(2 * (ht % PACK), 0, BANK), (2 * (ht % PACK) + 1, BANK, S)]
 
-        def multiply_w(ht, *passes):
-            if passes[0] == 0:
+        def multiply_w(ht, a):
+            opens = ht not in banks
+            if opens:
                 banks[ht] = [psum.tile([P, e1 - e0], F32, name=f"bank{n}") for n, e0, e1 in spans(ht)]
-            for a in passes:
-                for bank, (n, e0, e1) in zip(banks[ht], spans(ht)):
-                    nc.tensor.matmul_mx(
-                        out=bank[:],
-                        lhsT=operand[ht, a][0].bitcast(FP8X4),
-                        lhsT_scale=operand[ht, a][1],
-                        rhs=v_w[a][:, e0:e1].bitcast(FP8X4),
-                        rhs_scale=v_s[4 * a : P, e0:e1],
-                        start=(a == 0),
-                        stop=(a == 1),
-                    )
+            for bank, (n, e0, e1) in zip(banks[ht], spans(ht)):
+                for tile, c0, c1 in words[a]:
+                    f0, f1 = max(e0, c0), min(e1, c1)
+                    if f0 < f1:
+                        nc.tensor.matmul_mx(
+                            out=bank[:, f0 - e0 : f1 - e0],
+                            lhsT=operand[ht, a][0].bitcast(FP8X4),
+                            lhsT_scale=operand[ht, a][1],
+                            rhs=tile[:, f0 - c0 : f1 - c0].bitcast(FP8X4),
+                            rhs_scale=v_s[4 * a : P, f0:f1],
+                            start=(opens and f0 == e0),
+                            stop=(not opens and f1 == e1),
+                        )
+
+        def quantize_w1(name, rounded, parts):
+            codes = sbuf(f"w_code{name}", [P, len(parts) * P], U32)
+            scales = sbuf(f"w_scale{name}", [P, len(parts) * P], U8)
+            values = rounded[:].rearrange("p t m j -> p (t m j)")
+            nc.vector.quantize_mx(out=codes[:].bitcast(FP8X4), scales=scales[:], in_=values)
+            for t, (ht, a) in enumerate(parts):
+                columns = slice(t * P, (t + 1) * P)
+                operand[ht, a] = (codes[:, columns], scales[:, columns])
+                multiply_w(ht, a)
+
+        def round_near(u, a, rounded=None, part=0):
+            if rounded is None:
+                rounded = sbuf(f"rounded{u}_{a}", [P, 1, P, PACK], BF16)
+            nc.scalar.copy(
+                out=rounded[:, part].rearrange("p (c i) j -> p c j i", i=LINE),
+                in_=raw[u, a][:].rearrange("p j (c i) -> p c j i", i=LINE),
+            )
+            return rounded
+
+        def round_wide(ht, a):
+            rounded = sbuf(f"rounded{ht}_{a}", [P, 2, P, PACK], BF16)
+            nc.scalar.copy(
+                out=rounded[:].rearrange("p t m j -> p m j t"),
+                in_=wide[a][:].rearrange("p j (m t) -> p m j t", t=PACK)[:, :, :, ht - PACK : ht - PACK + 2],
+            )
+            return rounded
 
         def empty_h(ht):
-            h[ht] = keep.tile([P, S], F32, name=f"h{ht}")
+            h[ht] = sbuf(f"h{ht}", [P, S], F32)
             for side, (n, e0, e1) in enumerate(spans(ht)):
-                if ht == 0 and side % 2:
-                    nc.vector.tensor_scalar(h[ht][:, e0:e1], banks[ht][side][:], row_bias[ht, side], None, op0=ALU.add)
+                if ht == 0:
+                    nc.vector.tensor_scalar(h[ht][:, e0:e1], banks[ht][side][:], row_bias[ht, 0], None, op0=ALU.add)
                 else:
                     nc.scalar.activation(h[ht][:, e0:e1], banks[ht][side][:], ACT.Identity, bias=row_bias[ht, side])
 
         picked, right, z32, z_bf = {}, {}, {}, {}
-        z32[0, 0] = keep.tile([P, PACK, PAIRS], F32, name="z32_0", align_bytes=256)
+        z32[0, 0] = sbuf("z32_0", [P, PACK, PAIRS], F32)
 
-        def gather_right(ht):
-            picked[ht] = keep.tile([P, PAIRS], F32, name=f"picked{ht}", tag=f"picked{ht % 2}", align_bytes=256)
-            nc.vector.tensor_copy(picked[ht][:], h[ht][:].indirect(p2[:]))
+        def gather_right(ht, c0=0, c1=PAIRS):
+            picked[ht, c0] = sbuf(f"picked{ht}_{c0}", [P, c1 - c0], F32)
+            nc.vector.tensor_copy(picked[ht, c0][:], h[ht][:].indirect(entries(p2, c0, c1)))
 
-        def positive_part(ht, on_scalar=False, c0=0, c1=PAIRS, slot=None):
-            name = f"right{ht}" if c0 == 0 else f"right{ht}_{c0}"
-            right[ht, c0] = keep.tile([P, c1 - c0], F32, name=name, tag=slot or name, align_bytes=256)
+        def positive_part(ht, c0=0, c1=PAIRS, on_scalar=False):
+            right[ht, c0] = sbuf(f"right{ht}_{c0}", [P, c1 - c0], F32)
+            first = c0 if (ht, c0) in picked else 0
+            values = picked[ht, first][:, c0 - first : c1 - first]
             if on_scalar:
-                nc.scalar.activation(right[ht, c0][:], picked[ht][:, c0:c1], ACT.Relu)
+                nc.scalar.activation(right[ht, c0][:], values, ACT.Relu)
             else:
-                nc.gpsimd.tensor_scalar(right[ht, c0][:], picked[ht][:, c0:c1], F32_MAX, 0.0, op0=ALU.min, op1=ALU.max)
+                nc.gpsimd.tensor_scalar(right[ht, c0][:], values, F32_MAX, 0.0, op0=ALU.min, op1=ALU.max)
 
-        def gather_left(ht, c0=0, c1=PAIRS):
-            entries = p1[:, c0 // PER_COLUMN : c1 // PER_COLUMN]
+        def gather_left(ht, c0, c1, target):
             first = HALF if c0 >= HALF and (ht, HALF) in right else 0
             plain = right[ht, first][:, c0 - first : c1 - first]
-            target = z32[ht // PACK, c0][:, ht % PACK, :]
-            nc.vector.tensor_tensor(target, h[ht][:].indirect(entries), plain, ALU.subtract)
+            nc.vector.tensor_tensor(target, h[ht][:].indirect(entries(p1, c0, c1)), plain, ALU.subtract)
 
-        def gather_piece(c0, c1, slot):
-            z32[1, c0] = keep.tile([P, PACK, c1 - c0], F32, name=f"z32_1_{c0}", tag=slot, align_bytes=256)
-            for ht in range(PACK, H_TILES):
-                gather_left(ht, c0, c1)
+        def near_left(u, c0=0, c1=PAIRS):
+            z = sbuf(f"z{u}_{c0}", [P, c1 - c0], F32)
+            gather_left(u, c0, c1, z[:])
+            nc.sync.dma_start(z32[0, 0][QUAD * u : QUAD * (u + 1), :, c0:c1], z[:])
 
-        def round_z(copy, b, c0, values, rounded=None):
+        def wide_left(ht, c0, c1):
+            if (1, c0) not in z32:
+                z32[1, c0] = sbuf(f"z32_1_{c0}", [P, PACK, c1 - c0], F32)
+            gather_left(ht, c0, c1, z32[1, c0][:, ht % PACK, :])
+
+        def round_z(b, c0, values, rounded=None):
             if rounded is None:
-                tile = keep.tile([P, values.shape[2] * PACK], BF16, name=f"z_bf{b}_{c0}", align_bytes=256)
+                tile = sbuf(f"z_bf{b}_{c0}", [P, values.shape[2] * PACK], BF16)
                 rounded = tile[:]
             z_bf[b, c0] = rounded
-            copy(
+            nc.scalar.copy(
                 out=z_bf[b, c0].rearrange("p (c i t) -> p c t i", i=LINE, t=PACK),
                 in_=values.rearrange("p t (c i) -> p c t i", i=LINE),
             )
 
-        y_banks = {}
+        y_banks, z_mx = {}, {}
 
-        z_mx = {}
-
-        def quantize_z(b, c0, slot=None):
+        def quantize_z(b, c0):
             width = z_bf[b, c0].shape[1] // PACK
-            name = f"z_code{b}_{c0}"
-            codes = keep.tile([P, width], U32, name=name, tag=slot or name, align_bytes=256)
-            scales = keep.tile([P, width], U8, name=f"z_scale{b}_{c0}", align_bytes=256)
+            codes = sbuf(f"z_code{b}_{c0}", [P, width], U32)
+            scales = sbuf(f"z_scale{b}_{c0}", [P, width], U8)
             nc.vector.quantize_mx(out=codes[:].bitcast(FP8X4), scales=scales[:], in_=z_bf[b, c0])
             z_mx[b, c0] = (codes, scales, width)
 
@@ -259,79 +313,112 @@ def tile_list_precedent_ladder_kernel(
                     stop=(b == 1 and column + step == span),
                 )
 
-        def multiply_z(b, c0, slot=None):
-            quantize_z(b, c0, slot)
+        def multiply_z(b, c0):
+            quantize_z(b, c0)
             for i in range(Y_TILES):
                 multiply_tile(b, c0, i)
 
-        nc.vector.tensor_copy(v_w[0][:], tab_w[0][:].bitcast(U32).indirect(idx[:]))
-        nc.vector.tensor_copy(v_s[:], tab_s[:].indirect(idx[:]))
-        prepare_w1(0, 0)
-        nc.vector.tensor_copy(v_w[1][:], tab_w[1][:].bitcast(U32).indirect(idx[:]))
-        waiting = rounded_tile(1, 0)
-        round_w1(1, 0, waiting)
-        rounded = [rounded_tile(pair, 1) for pair in range(2)]
-        for part in range(2):
-            round_w1(0, 1, rounded[0], part)
-        quantize_w1(0, 1, rounded[0], 0, 1)
-        quantize_w1(0, 1, rounded[0], 1, 2)
-        quantize_w1(1, 0, waiting)
-        for part in range(2):
-            round_w1(1, 1, rounded[1], part)
-        quantize_w1(1, 1, rounded[1])
-        empty_h(0)
-        gather_right(0)
+        def prepare_near(u, a):
+            quantize_w1(f"{u}_{a}", round_near(u, a), [(u, a)])
+
+        def prepare_wide(ht, a):
+            quantize_w1(f"{ht}_{a}", round_wide(ht, a), [(ht, a), (ht + 1, a)])
 
         def step(ht):
             empty_h(ht)
             gather_right(ht)
             positive_part(ht - 1)
-            gather_left(ht - 1)
 
-        step(1)
-        prepare_w1(2, 0)
+        prepare_near(0, 0)
+        gather_words(1, "v_w1_1", S - HALF, S)
+
+        for u, a in ((1, 1), (2, 0), (2, 1)):
+            raw[u, a] = new_raw(f"raw{u}_{a}", a, u * P, P)
+        raw3 = sbuf("raw3", [P, 2, PACK, P], F32)
+        for a in range(2):
+            load_w1(raw3[:, a], a, 3 * P, P)
+        wide = [new_raw(f"wide{a}", a, PASS, PASS) for a in range(2)]
+        w4_w = sbuf("w4_w", [P, 2, 2 * N], U8)
+        w4_s = sbuf("w4_s", [P, 2, N], U8)
+        nc.sync.dma_start(w4_w[:].bitcast(I32), w4_words.rearrange("a p c -> p a c").bitcast(I32))
+        for q in range(QUADS):
+            nc.sync.dma_start(
+                w4_s[QUAD * q : QUAD * q + 4, :, :].bitcast(I32),
+                w4_scales[:, 4 * q : 4 * q + 4, :].rearrange("a r c -> r a c").bitcast(I32),
+            )
+
+        prepare_near(0, 1)
+        prepare_near(1, 0)
+        empty_h(0)
+        prepare_near(1, 1)
+        gather_right(0, 0, HALF)
+        gather_right(0, HALF, PAIRS)
+        positive_part(0, 0, HALF)
+        rounded2 = sbuf("rounded2", [P, 2, P, PACK], BF16)
+        for a in range(2):
+            round_near(2, a, rounded2, a)
+        quantize_w1("2", rounded2, [(2, 0), (2, 1)])
+        near_left(0, 0, HALF)
+        empty_h(1)
+        gather_right(1)
+        positive_part(0, HALF, PAIRS)
+        rounded3 = sbuf("rounded3", [P, 2, P, PACK], BF16)
+        nc.scalar.copy(
+            out=rounded3[:].rearrange("p a (c i) j -> p a c j i", i=LINE),
+            in_=raw3[:].rearrange("p a j (c i) -> p a c j i", i=LINE),
+        )
+        quantize_w1("3", rounded3, [(3, 0), (3, 1)])
+        near_left(0, HALF, PAIRS)
         step(2)
-        prepare_w1(2, 1)
-        step(3)
-        prepare_w1(3, 0)
+        near_left(1)
+        empty_h(3)
+        prepare_wide(4, 0)
+        gather_right(3)
+        positive_part(2)
+        prepare_wide(4, 1)
+        near_left(2)
+        prepare_wide(6, 1)
+        gain = sbuf("gain", [P, Y_TILES], F32)
+        with nc.allow_non_contiguous_dma(reason="one gain a partition"):
+            nc.sync.dma_start(gain[:], gn.rearrange("(i p) -> p i", p=P))
+        positive_part(3, on_scalar=True)
+        near_left(3)
+
         empty_h(4)
         gather_right(4)
-        prepare_w1(3, 1)
-        positive_part(3, on_scalar=True)
-        gather_left(3)
-        z32[1, 0] = keep.tile([P, PACK, HALF], F32, name="z32_1_0", align_bytes=256)
+        prepare_wide(6, 0)
         for ht in (5, 6, 7):
-            empty_h(ht)
-            gather_right(ht)
-            positive_part(ht - 1)
-            gather_left(ht - 1, 0, HALF)
-        whole = keep.tile([P, PAIRS * PACK], BF16, name="z_bf0_0", align_bytes=256)
+            step(ht)
+            wide_left(ht - 1, 0, HALF)
+        whole = sbuf("z_bf0", [P, PAIRS * PACK], BF16)
         for c0 in (0, HALF):
-            round_z(nc.scalar.copy, 0, c0, z32[0, 0][:, :, c0 : c0 + HALF], whole[:, c0 * PACK : (c0 + HALF) * PACK])
+            round_z(0, c0, z32[0, 0][:, :, c0 : c0 + HALF], whole[:, c0 * PACK : (c0 + HALF) * PACK])
         multiply_z(0, 0)
-        positive_part(7, True, 0, HALF)
-        positive_part(7, True, HALF, PAIRS)
-        gather_left(7, 0, HALF)
-        round_z(nc.scalar.copy, 1, 0, z32[1, 0][:])
-        multiply_z(0, HALF, "right7")
-        gather_piece(HALF, LAST, "picked1")
-        round_z(nc.scalar.copy, 1, HALF, z32[1, HALF][:])
+        positive_part(7, 0, HALF, True)
+        positive_part(7, HALF, PAIRS, True)
+        wide_left(7, 0, HALF)
+        round_z(1, 0, z32[1, 0][:])
+        multiply_z(0, HALF)
+        for ht in range(PACK, H_TILES):
+            wide_left(ht, HALF, LAST)
+        round_z(1, HALF, z32[1, HALF][:])
         multiply_z(1, 0)
-        gather_piece(LAST, PAIRS, "z32_1_0")
-        last_bf = keep.tile([P, QUARTER, PACK], BF16, name="z_bf_last", tag="right6", align_bytes=256)
+        for ht in range(PACK, H_TILES):
+            wide_left(ht, LAST, PAIRS)
+        last_bf = sbuf("z_bf_last", [P, QUARTER, PACK], BF16)
         for t0 in (0, 2):
             nc.vector.tensor_copy(
                 out=last_bf[:, :, t0 : t0 + 2].rearrange("p (c i) t -> p c t i", i=LINE),
                 in_=z32[1, LAST][:, t0 : t0 + 2, :].rearrange("p t (c i) -> p c t i", i=LINE),
             )
         z_bf[1, LAST] = last_bf[:].rearrange("p c t -> p (c t)")
-        quantize_z(1, HALF, "right7_256")
+        quantize_z(1, HALF)
         quantize_z(1, LAST)
         for i in range(Y_TILES):
             for c0 in (HALF, LAST):
                 multiply_tile(1, c0, i)
 
-        y = [keep.tile([P, PAIRS], F32, name=f"y{i}") for i in range(Y_TILES)]
+        y = [sbuf(f"y{i}", [P, PAIRS], F32) for i in range(Y_TILES)]
         nc.scalar.copy(y[0][:, 0:HALF], y_banks[0][:])
         nc.scalar.copy(y[0][:, HALF:LAST], y_banks[4][:])
         for i in range(1, Y_TILES):
@@ -345,14 +432,13 @@ def tile_list_precedent_ladder_kernel(
         first_line = {}
 
         def gather_first_line(i):
-            first_line[i] = keep.tile([P, LINES], F32, name=f"first_line{i}")
+            first_line[i] = sbuf(f"first_line{i}", [P, LINES], F32)
             nc.vector.tensor_copy(first_line[i][:], y[i][:].indirect(p3[:]))
 
         def finish(i, c0, c1):
-            both = keep.tile([P, c1 - c0], F32, name=f"both{i}_{c0}")
-            second_line = y[i][:].indirect(p4[:, c0 // PER_COLUMN : c1 // PER_COLUMN])
-            nc.vector.tensor_tensor(both[:], second_line, first_line[i][:, c0:c1], ALU.mult)
-            result = keep.tile([P, c1 - c0], F32, name=f"result{i}_{c0}")
+            both = sbuf(f"both{i}_{c0}", [P, c1 - c0], F32)
+            nc.vector.tensor_tensor(both[:], y[i][:].indirect(entries(p4, c0, c1)), first_line[i][:, c0:c1], ALU.mult)
+            result = sbuf(f"result{i}_{c0}", [P, c1 - c0], F32)
             nc.scalar.activation(result[:], both[:], ACT.Tanh, scale=gain[:, i : i + 1])
             nc.sync.dma_start(out[i * P : (i + 1) * P, c0:c1], result[:])
 

@@ -33,40 +33,44 @@ LAST = PAIRS - QUARTER
 KB = 1024
 
 PLACE = {
-    "tab_w0": 1 * KB,
-    "raw1_1": 0,
-    "picked0_0": 0,
-    "raw2_0": 2 * KB,
-    "raw2_1": 4 * KB,
-    "h1": 1 * KB,
-    "z0_0": 5 * KB,
-    "raw3": 6 * KB,
-    "z0_256": 6 * KB,
-    "h2": 7 * KB,
+    "tab_w0": 4 * KB + 256,
+    "raw3_0": 9 * KB,
+    "bias1_0": 35 * KB,
+    "rounded3_1": 35 * KB,
+    "bias3_1": 40 * KB,
+    "rounded6_1": 40 * KB,
+    "raw2_1": 3 * KB,
+    "h1": 0,
+    "z0_0": 4 * KB,
+    "raw1_1": 5 * KB,
+    "picked0_0": 5 * KB,
+    "picked0_256": 6 * KB,
+    "raw3_1": 7 * KB,
+    "z0_256": 7 * KB,
+    "h2": 8 * KB,
+    "tab_s": 82 * KB,
+    "near0": 82 * KB,
+    "raw0_1": 80 * KB,
+    "v_w1_2": 80 * KB,
     "tab_w1": 21 * KB,
-    "wide0": 13 * KB + 256,
+    "wide0": 12 * KB,
     "w4_w": 23 * KB + 256,
     "w4_s": 25 * KB + 256,
     "wide1": 26 * KB + 256,
     "gain": 26 * KB + 256,
     "z32_1_0": 70 * KB,
     "z32_1_384": 70 * KB,
-    "picked3_0": 74 * KB,
-    "rounded4_0": 75 * KB,
-    "right2_0": 76 * KB,
+    "bias3_0": 74 * KB,
+    "rounded4": 74 * KB,
     "raw0_0": 78 * KB,
     "v_w1_1": 78 * KB,
-    "bias1_0": 35 * KB,
-    "rounded3": 35 * KB,
     "bias1_1": 37 * KB,
     "right0_256": 37 * KB,
     "bias2_1": 38 * KB,
     "right1_0": 38 * KB,
-    "rounded4_1": 42 * KB,
-    "z2_0": 42 * KB,
     "right3_0": 28 * KB,
-    "bias4_0": 46 * KB,
-    "rounded6_0": 46 * KB,
+    "z2_0": 30 * KB,
+    "rounded6_0": 32 * KB,
     "bias5_1": 50 * KB,
     "right4_0": 50 * KB,
     "bias6_1": 52 * KB,
@@ -127,7 +131,7 @@ def tile_list_precedent_ladder_kernel(
         nc.vector.memset(tab_s[2 * QUAD : P, :].bitcast(I32), 0)
         identity = sbuf("identity", [P, P], F32)
         make_identity(nc, identity[:])
-        nc.gpsimd.dma_start(bias_rows[0:2, :], b1.rearrange("(b c) -> b c", b=2))
+        nc.scalar.dma_start(bias_rows[0:2, :], b1.rearrange("(b c) -> b c", b=2))
 
         for a in range(2):
             nc.sync.dma_start(
@@ -136,12 +140,12 @@ def tile_list_precedent_ladder_kernel(
             )
         idx = load_list(offs, "idx")
         p2 = load_list(pos2, "p2")
-        p1 = load_list(pos1, "p1")
         tab_w = [load_table_words(0)]
+        p1 = load_list(pos1, "p1")
         p3 = load_list(pos3, "p3")
         p4 = load_list(pos4, "p4")
         tab_w.append(load_table_words(1))
-        raw = {(u, a): new_raw(f"raw{u}_{a}", a, u * P, P) for u, a in ((0, 0), (0, 1), (1, 0))}
+        raw = {(0, a): new_raw(f"raw0_{a}", a, 0, P)[:] for a in range(2)}
 
         words = {0: [], 1: []}
 
@@ -157,9 +161,12 @@ def tile_list_precedent_ladder_kernel(
         v_s = sbuf("v_s", [P, S], U8)
         nc.vector.tensor_copy(v_rows[:], tab_s[:].indirect(idx[:]))
         for q in range(QUADS):
-            nc.scalar.dma_start(v_s[QUAD * q : QUAD * q + 8, :].bitcast(I32), v_rows[q:QUAD:4, :].bitcast(I32))
+            nc.sync.dma_start(v_s[QUAD * q : QUAD * q + 8, :].bitcast(I32), v_rows[q:QUAD:4, :].bitcast(I32))
+        near0 = new_raw("near0", 0, P, 2 * P)
+        for u in (1, 2):
+            raw[u, 0] = near0[:, :, (u - 1) * P : u * P]
         gather_words(0, "v_w0", 0, S)
-        gather_words(1, "v_w1_0", 0, S - HALF)
+        gather_words(1, "v_w1_0", 0, BANK)
 
         turned = [psum.tile([P, PACK, P], F32, name=f"bank{2 + b}") for b in range(2)]
         bias = sbuf("bias", [P, H_TILES], F32)
@@ -186,12 +193,13 @@ def tile_list_precedent_ladder_kernel(
                 return [(n, i * HALF, (i + 1) * HALF) for i, n in enumerate((4, 5, 6, 7))]
             return [(2 * (ht % PACK), 0, BANK), (2 * (ht % PACK) + 1, BANK, S)]
 
-        def multiply_w(ht, a):
-            opens = ht not in banks
-            if opens:
+        def multiply_w(ht, *passes):
+            fresh = ht not in banks
+            if fresh:
                 banks[ht] = [psum.tile([P, e1 - e0], F32, name=f"bank{n}") for n, e0, e1 in spans(ht)]
             for bank, (n, e0, e1) in zip(banks[ht], spans(ht)):
-                for tile, c0, c1 in words[a]:
+                for a, (tile, c0, c1) in [(a, piece) for a in passes for piece in words[a]]:
+                    opens = fresh and a == passes[0]
                     f0, f1 = max(e0, c0), min(e1, c1)
                     if f0 < f1:
                         nc.tensor.matmul_mx(
@@ -204,29 +212,34 @@ def tile_list_precedent_ladder_kernel(
                             stop=(not opens and f1 == e1),
                         )
 
-        def quantize_w1(name, rounded, parts):
+        def quantize_only(name, rounded, parts):
             codes = sbuf(f"w_code{name}", [P, len(parts) * P], U32)
             scales = sbuf(f"w_scale{name}", [P, len(parts) * P], U8)
-            values = rounded[:].rearrange("p t m j -> p (t m j)")
+            values = rounded.rearrange("p t m j -> p (t m j)")
             nc.vector.quantize_mx(out=codes[:].bitcast(FP8X4), scales=scales[:], in_=values)
             for t, (ht, a) in enumerate(parts):
                 columns = slice(t * P, (t + 1) * P)
                 operand[ht, a] = (codes[:, columns], scales[:, columns])
-                multiply_w(ht, a)
+
+        def quantize_w1(name, rounded, parts):
+            quantize_only(name, rounded, parts)
+            for ht in sorted({ht for ht, a in parts}):
+                multiply_w(ht, *[a for t, a in parts if t == ht])
 
         def round_near(u, a, rounded=None, part=0):
             if rounded is None:
-                rounded = sbuf(f"rounded{u}_{a}", [P, 1, P, PACK], BF16)
+                rounded = sbuf(f"rounded{u}_{a}", [P, 1, P, PACK], BF16)[:]
             nc.scalar.copy(
                 out=rounded[:, part].rearrange("p (c i) j -> p c j i", i=LINE),
-                in_=raw[u, a][:].rearrange("p j (c i) -> p c j i", i=LINE),
+                in_=raw[u, a].rearrange("p j (c i) -> p c j i", i=LINE),
             )
             return rounded
 
-        def round_wide(ht, a):
-            rounded = sbuf(f"rounded{ht}_{a}", [P, 2, P, PACK], BF16)
+        def round_wide(ht, a, rounded=None):
+            if rounded is None:
+                rounded = sbuf(f"rounded{ht}_{a}", [P, 2, P, PACK], BF16)[:]
             nc.scalar.copy(
-                out=rounded[:].rearrange("p t m j -> p m j t"),
+                out=rounded.rearrange("p t m j -> p m j t"),
                 in_=wide[a][:].rearrange("p j (m t) -> p m j t", t=PACK)[:, :, :, ht - PACK : ht - PACK + 2],
             )
             return rounded
@@ -237,7 +250,7 @@ def tile_list_precedent_ladder_kernel(
                 if ht == 0:
                     nc.vector.tensor_scalar(h[ht][:, e0:e1], banks[ht][side][:], row_bias[ht, 0], None, op0=ALU.add)
                 else:
-                    nc.scalar.activation(h[ht][:, e0:e1], banks[ht][side][:], ACT.Identity, bias=row_bias[ht, side])
+                    nc.scalar.activation(h[ht][:, e0:e1], banks[ht][side][:], ACT.Identity, bias=row_bias[ht, side % 2])
 
         picked, right, z32, z_bf = {}, {}, {}, {}
         z32[0, 0] = sbuf("z32_0", [P, PACK, PAIRS], F32)
@@ -330,13 +343,14 @@ def tile_list_precedent_ladder_kernel(
             positive_part(ht - 1)
 
         prepare_near(0, 0)
-        gather_words(1, "v_w1_1", S - HALF, S)
+        gather_words(1, "v_w1_1", BANK, S - HALF)
+        waiting = round_near(0, 1)
+        quantize_only("0_1", waiting, [(0, 1)])
+        gather_words(1, "v_w1_2", S - HALF, S)
+        multiply_w(0, 1)
 
-        for u, a in ((1, 1), (2, 0), (2, 1)):
-            raw[u, a] = new_raw(f"raw{u}_{a}", a, u * P, P)
-        raw3 = sbuf("raw3", [P, 2, PACK, P], F32)
-        for a in range(2):
-            load_w1(raw3[:, a], a, 3 * P, P)
+        for u, a in ((1, 1), (3, 0), (2, 1), (3, 1)):
+            raw[u, a] = new_raw(f"raw{u}_{a}", a, u * P, P)[:]
         wide = [new_raw(f"wide{a}", a, PASS, PASS) for a in range(2)]
         w4_w = sbuf("w4_w", [P, 2, 2 * N], U8)
         w4_s = sbuf("w4_s", [P, 2, N], U8)
@@ -347,46 +361,43 @@ def tile_list_precedent_ladder_kernel(
                 w4_scales[:, 4 * q : 4 * q + 4, :].rearrange("a r c -> r a c").bitcast(I32),
             )
 
-        prepare_near(0, 1)
-        prepare_near(1, 0)
         empty_h(0)
-        prepare_near(1, 1)
+        rounded1 = sbuf("rounded1", [P, 2, P, PACK], BF16)
+        for a in range(2):
+            round_near(1, a, rounded1, a)
+        quantize_w1("1", rounded1[:], [(1, 0), (1, 1)])
         gather_right(0, 0, HALF)
         gather_right(0, HALF, PAIRS)
         positive_part(0, 0, HALF)
-        rounded2 = sbuf("rounded2", [P, 2, P, PACK], BF16)
-        for a in range(2):
-            round_near(2, a, rounded2, a)
-        quantize_w1("2", rounded2, [(2, 0), (2, 1)])
+        parts = [(2, 0), (3, 0), (2, 1)]
+        rounded2 = sbuf("rounded2", [P, len(parts), P, PACK], BF16)
+        for part, (u, a) in enumerate(parts):
+            round_near(u, a, rounded2, part)
+        quantize_w1("2", rounded2[:], parts)
         near_left(0, 0, HALF)
         empty_h(1)
         gather_right(1)
         positive_part(0, HALF, PAIRS)
-        rounded3 = sbuf("rounded3", [P, 2, P, PACK], BF16)
-        nc.scalar.copy(
-            out=rounded3[:].rearrange("p a (c i) j -> p a c j i", i=LINE),
-            in_=raw3[:].rearrange("p a j (c i) -> p a c j i", i=LINE),
-        )
-        quantize_w1("3", rounded3, [(3, 0), (3, 1)])
+        prepare_near(3, 1)
         near_left(0, HALF, PAIRS)
         step(2)
         near_left(1)
-        empty_h(3)
-        prepare_wide(4, 0)
-        gather_right(3)
-        positive_part(2)
-        prepare_wide(4, 1)
-        near_left(2)
+        step(3)
+        rounded4 = sbuf("rounded4", [P, 2 * 2, P, PACK], BF16)
+        for a in range(2):
+            round_wide(4, a, rounded4[:, 2 * a : 2 * a + 2])
+        quantize_w1("4", rounded4[:], [(4, 0), (5, 0), (4, 1), (5, 1)])
         prepare_wide(6, 1)
+        near_left(2)
         gain = sbuf("gain", [P, Y_TILES], F32)
         with nc.allow_non_contiguous_dma(reason="one gain a partition"):
             nc.sync.dma_start(gain[:], gn.rearrange("(i p) -> p i", p=P))
         positive_part(3, on_scalar=True)
         near_left(3)
+        prepare_wide(6, 0)
 
         empty_h(4)
         gather_right(4)
-        prepare_wide(6, 0)
         for ht in (5, 6, 7):
             step(ht)
             wide_left(ht - 1, 0, HALF)

@@ -60,7 +60,7 @@ PLACE = {
     "gain": 26 * KB + 256,
     "z32_1_0": 70 * KB,
     "z32_1_384": 70 * KB,
-    "bias3_0": 74 * KB,
+    "bias2_0": 74 * KB,
     "rounded4": 74 * KB,
     "raw0_0": 78 * KB,
     "v_w1_1": 78 * KB,
@@ -349,9 +349,11 @@ def tile_list_precedent_ladder_kernel(
         gather_words(1, "v_w1_2", S - HALF, S)
         multiply_w(0, 1)
 
-        for u, a in ((1, 1), (3, 0), (2, 1), (3, 1)):
+        for u, a in ((1, 1), (3, 0), (2, 1)):
             raw[u, a] = new_raw(f"raw{u}_{a}", a, u * P, P)[:]
-        wide = [new_raw(f"wide{a}", a, PASS, PASS) for a in range(2)]
+        wide = [new_raw("wide0", 0, PASS, PASS)]
+        raw[3, 1] = new_raw("raw3_1", 1, 3 * P, P)[:]
+        wide.append(new_raw("wide1", 1, PASS, PASS))
         w4_w = sbuf("w4_w", [P, 2, 2 * N], U8)
         w4_s = sbuf("w4_s", [P, 2, N], U8)
         nc.sync.dma_start(w4_w[:].bitcast(I32), w4_words.rearrange("a p c -> p a c").bitcast(I32))
@@ -382,10 +384,10 @@ def tile_list_precedent_ladder_kernel(
         near_left(0, HALF, PAIRS)
         step(2)
         near_left(1)
-        step(3)
         rounded4 = sbuf("rounded4", [P, 2 * 2, P, PACK], BF16)
-        for a in range(2):
-            round_wide(4, a, rounded4[:, 2 * a : 2 * a + 2])
+        round_wide(4, 0, rounded4[:, 0:2])
+        step(3)
+        round_wide(4, 1, rounded4[:, 2:4])
         quantize_w1("4", rounded4[:], [(4, 0), (5, 0), (4, 1), (5, 1)])
         prepare_wide(6, 1)
         near_left(2)

@@ -68,8 +68,8 @@ PLACE = {
     "right0_256": 37 * KB,
     "bias2_1": 38 * KB,
     "right1_0": 38 * KB,
-    "right3_0": 28 * KB,
-    "z2_0": 30 * KB,
+    "right3_0": 74 * KB,
+    "z2_0": 76 * KB,
     "rounded6_0": 32 * KB,
     "bias5_1": 50 * KB,
     "right4_0": 50 * KB,
@@ -259,14 +259,14 @@ def tile_list_precedent_ladder_kernel(
             picked[ht, c0] = sbuf(f"picked{ht}_{c0}", [P, c1 - c0], F32)
             nc.vector.tensor_copy(picked[ht, c0][:], h[ht][:].indirect(entries(p2, c0, c1)))
 
-        def positive_part(ht, c0=0, c1=PAIRS, on_scalar=False):
+        def positive_part(ht, c0=0, c1=PAIRS, on_scalar=False, engine=nc.gpsimd):
             right[ht, c0] = sbuf(f"right{ht}_{c0}", [P, c1 - c0], F32)
             first = c0 if (ht, c0) in picked else 0
             values = picked[ht, first][:, c0 - first : c1 - first]
             if on_scalar:
                 nc.scalar.activation(right[ht, c0][:], values, ACT.Relu)
             else:
-                nc.gpsimd.tensor_scalar(right[ht, c0][:], values, F32_MAX, 0.0, op0=ALU.min, op1=ALU.max)
+                engine.tensor_scalar(right[ht, c0][:], values, F32_MAX, 0.0, op0=ALU.min, op1=ALU.max)
 
         def gather_left(ht, c0, c1, target):
             first = HALF if c0 >= HALF and (ht, HALF) in right else 0
@@ -389,13 +389,13 @@ def tile_list_precedent_ladder_kernel(
         step(3)
         round_wide(4, 1, rounded4[:, 2:4])
         quantize_w1("4", rounded4[:], [(4, 0), (5, 0), (4, 1), (5, 1)])
-        prepare_wide(6, 1)
+        positive_part(3, engine=nc.vector)
         near_left(2)
+        near_left(3)
+        prepare_wide(6, 1)
         gain = sbuf("gain", [P, Y_TILES], F32)
         with nc.allow_non_contiguous_dma(reason="one gain a partition"):
             nc.sync.dma_start(gain[:], gn.rearrange("(i p) -> p i", p=P))
-        positive_part(3, on_scalar=True)
-        near_left(3)
         prepare_wide(6, 0)
 
         empty_h(4)

@@ -42,16 +42,18 @@ PLACE = {
     "raw2_1": 3 * KB,
     "h1": 0,
     "z0_0": 4 * KB,
-    "raw1_1": 5 * KB,
-    "picked0_0": 5 * KB,
-    "picked0_256": 6 * KB,
+    "raw2_0": 5 * KB,
+    "raw1_0": 81 * KB,
+    "h0": 78 * KB,
+    "raw1_1": 83 * KB,
+    "picked0_0": 83 * KB,
+    "picked0_256": 84 * KB,
     "raw3_1": 7 * KB,
     "z0_256": 7 * KB,
     "h2": 8 * KB,
     "tab_s": 82 * KB,
-    "near0": 82 * KB,
-    "raw0_1": 80 * KB,
-    "v_w1_2": 80 * KB,
+    "raw0_1": 104 * KB,
+    "v_w1_2": 104 * KB,
     "tab_w1": 21 * KB,
     "wide0": 12 * KB,
     "w4_w": 23 * KB + 256,
@@ -62,8 +64,8 @@ PLACE = {
     "z32_1_384": 70 * KB,
     "bias2_0": 74 * KB,
     "rounded4": 74 * KB,
-    "raw0_0": 78 * KB,
-    "v_w1_1": 78 * KB,
+    "raw0_0": 102 * KB,
+    "v_w1_1": 102 * KB,
     "bias1_1": 37 * KB,
     "right0_256": 37 * KB,
     "bias2_1": 38 * KB,
@@ -162,9 +164,8 @@ def tile_list_precedent_ladder_kernel(
         nc.vector.tensor_copy(v_rows[:], tab_s[:].indirect(idx[:]))
         for q in range(QUADS):
             nc.sync.dma_start(v_s[QUAD * q : QUAD * q + 8, :].bitcast(I32), v_rows[q:QUAD:4, :].bitcast(I32))
-        near0 = new_raw("near0", 0, P, 2 * P)
-        for u in (1, 2):
-            raw[u, 0] = near0[:, :, (u - 1) * P : u * P]
+        for a in range(2):
+            raw[1, a] = new_raw(f"raw1_{a}", a, P, P)[:]
         gather_words(0, "v_w0", 0, S)
         gather_words(1, "v_w1_0", 0, BANK)
 
@@ -349,7 +350,7 @@ def tile_list_precedent_ladder_kernel(
         gather_words(1, "v_w1_2", S - HALF, S)
         multiply_w(0, 1)
 
-        for u, a in ((1, 1), (3, 0), (2, 1)):
+        for u, a in ((2, 0), (3, 0), (2, 1)):
             raw[u, a] = new_raw(f"raw{u}_{a}", a, u * P, P)[:]
         wide = [new_raw("wide0", 0, PASS, PASS)]
         raw[3, 1] = new_raw("raw3_1", 1, 3 * P, P)[:]
@@ -363,11 +364,9 @@ def tile_list_precedent_ladder_kernel(
                 w4_scales[:, 4 * q : 4 * q + 4, :].rearrange("a r c -> r a c").bitcast(I32),
             )
 
+        prepare_near(1, 0)
         empty_h(0)
-        rounded1 = sbuf("rounded1", [P, 2, P, PACK], BF16)
-        for a in range(2):
-            round_near(1, a, rounded1, a)
-        quantize_w1("1", rounded1[:], [(1, 0), (1, 1)])
+        prepare_near(1, 1)
         gather_right(0, 0, HALF)
         gather_right(0, HALF, PAIRS)
         positive_part(0, 0, HALF)

@@ -33,45 +33,47 @@ LAST = PAIRS - QUARTER
 KB = 1024
 
 PLACE = {
-    "tab_w0": 4 * KB + 256,
-    "raw3_0": 9 * KB,
-    "bias1_0": 35 * KB,
-    "rounded3_1": 35 * KB,
-    "bias3_1": 40 * KB,
-    "rounded6_1": 40 * KB,
+    "tab_w0": 4 * KB + 512,
+    "raw3_0": 9 * KB + 256,
+    "bias1_0": 106 * KB,
+    "rounded3_1": 106 * KB,
+    "bias3": 22 * KB,
+    "rounded6_1": 20 * KB + 256,
+    "right2_0": 22 * KB + 256,
     "raw2_1": 3 * KB,
     "h1": 0,
     "z0_0": 4 * KB,
-    "raw2_0": 5 * KB,
+    "raw2_0": 5 * KB + 256,
     "raw1_0": 81 * KB,
     "h0": 78 * KB,
     "raw1_1": 83 * KB,
     "picked0_0": 83 * KB,
     "picked0_256": 84 * KB,
-    "raw3_1": 7 * KB,
-    "z0_256": 7 * KB,
-    "h2": 8 * KB,
+    "raw3_1": 7 * KB + 256,
+    "z0_256": 7 * KB + 256,
+    "h2": 8 * KB + 256,
     "tab_s": 82 * KB,
     "raw0_1": 104 * KB,
     "v_w1_2": 104 * KB,
     "tab_w1": 21 * KB,
-    "wide0": 12 * KB,
-    "w4_w": 23 * KB + 256,
-    "w4_s": 25 * KB + 256,
-    "wide1": 26 * KB + 256,
-    "gain": 26 * KB + 256,
+    "wide0": 12 * KB + 256,
+    "h4": 12 * KB + 256,
+    "h5": 16 * KB + 256,
+    "w4_w": 24 * KB + 256,
+    "w4_s": 26 * KB + 256,
+    "wide1": 27 * KB + 256,
+    "gain": 27 * KB + 256,
     "z32_1_0": 70 * KB,
     "z32_1_384": 70 * KB,
     "bias2_0": 74 * KB,
-    "rounded4": 74 * KB,
+    "rounded4_0": 74 * KB,
     "raw0_0": 102 * KB,
     "v_w1_1": 102 * KB,
     "bias1_1": 37 * KB,
     "right0_256": 37 * KB,
     "bias2_1": 38 * KB,
     "right1_0": 38 * KB,
-    "right3_0": 74 * KB,
-    "z2_0": 76 * KB,
+    "right3_0": 29 * KB,
     "rounded6_0": 32 * KB,
     "bias5_1": 50 * KB,
     "right4_0": 50 * KB,
@@ -171,12 +173,12 @@ def tile_list_precedent_ladder_kernel(
 
         turned = [psum.tile([P, PACK, P], F32, name=f"bank{2 + b}") for b in range(2)]
         bias = sbuf("bias", [P, H_TILES], F32)
-        for t in range(PACK):
+        for t in range(PACK - 1):
             nc.tensor.transpose(turned[0][:, t, :], bias_rows[:, t * P : (t + 1) * P], identity[:])
         for t in range(PACK):
             nc.tensor.transpose(turned[1][:, t, :], bias_rows[:, t:PASS:PACK], identity[:])
-        for b in range(2):
-            nc.scalar.copy(bias[:, PACK * b : PACK * (b + 1)], turned[b][:, :, b])
+        nc.scalar.copy(bias[:, 0 : PACK - 1], turned[0][:, 0 : PACK - 1, 0])
+        nc.scalar.copy(bias[:, PACK:H_TILES], turned[1][:, :, 1])
         row_bias = {}
         for ht in range(H_TILES):
             for side in range(2):
@@ -352,8 +354,11 @@ def tile_list_precedent_ladder_kernel(
 
         for u, a in ((2, 0), (3, 0), (2, 1)):
             raw[u, a] = new_raw(f"raw{u}_{a}", a, u * P, P)[:]
-        wide = [new_raw("wide0", 0, PASS, PASS)]
         raw[3, 1] = new_raw("raw3_1", 1, 3 * P, P)[:]
+        wide = [new_raw("wide0", 0, PASS, PASS)]
+        row_bias[3, 0] = row_bias[3, 1] = sbuf("bias3", [P, P], F32)[:, 0:1]
+        with nc.allow_non_contiguous_dma(reason="one value of the bias a partition"):
+            nc.sync.dma_start(row_bias[3, 0], b1[3 * P : PASS].rearrange("(p one) -> p one", one=1))
         wide.append(new_raw("wide1", 1, PASS, PASS))
         w4_w = sbuf("w4_w", [P, 2, 2 * N], U8)
         w4_s = sbuf("w4_s", [P, 2, N], U8)
@@ -383,15 +388,14 @@ def tile_list_precedent_ladder_kernel(
         near_left(0, HALF, PAIRS)
         step(2)
         near_left(1)
-        rounded4 = sbuf("rounded4", [P, 2 * 2, P, PACK], BF16)
-        round_wide(4, 0, rounded4[:, 0:2])
+        prepare_wide(4, 0)
         step(3)
-        round_wide(4, 1, rounded4[:, 2:4])
-        quantize_w1("4", rounded4[:], [(4, 0), (5, 0), (4, 1), (5, 1)])
-        positive_part(3, engine=nc.vector)
         near_left(2)
+        prepare_wide(4, 1)
+        waiting = round_wide(6, 1)
+        positive_part(3, engine=nc.vector)
+        quantize_w1("6_1", waiting, [(6, 1), (7, 1)])
         near_left(3)
-        prepare_wide(6, 1)
         gain = sbuf("gain", [P, Y_TILES], F32)
         with nc.allow_non_contiguous_dma(reason="one gain a partition"):
             nc.sync.dma_start(gain[:], gn.rearrange("(i p) -> p i", p=P))

@@ -35,11 +35,16 @@ KB = 1024
 PLACE = {
     "tab_w0": 4 * KB + 512,
     "raw3_0": 9 * KB + 256,
-    "bias1_0": 106 * KB,
-    "rounded3_1": 106 * KB,
-    "bias3": 22 * KB,
-    "rounded6_1": 20 * KB + 256,
-    "right2_0": 22 * KB + 256,
+    "bias1_0": 21 * KB + 256,
+    "rounded3_1": 21 * KB + 256,
+    "bias2_1": 22 * KB + 256,
+    "right1_0": 21 * KB + 256,
+    "right2_0": 23 * KB,
+    "bias3": 24 * KB + 768,
+    "rounded6_1": 25 * KB,
+    "rounded2": 108 * KB,
+    "bias1_1": 111 * KB,
+    "right0_256": 110 * KB + 512,
     "raw2_1": 3 * KB,
     "h1": 0,
     "z0_0": 4 * KB,
@@ -55,26 +60,22 @@ PLACE = {
     "tab_s": 82 * KB,
     "raw0_1": 104 * KB,
     "v_w1_2": 104 * KB,
-    "tab_w1": 21 * KB,
+    "tab_w1": 25 * KB,
     "wide0": 12 * KB + 256,
     "h4": 12 * KB + 256,
     "h5": 16 * KB + 256,
-    "w4_w": 24 * KB + 256,
-    "w4_s": 26 * KB + 256,
-    "wide1": 27 * KB + 256,
-    "gain": 27 * KB + 256,
+    "w4_w": 27 * KB,
+    "w4_s": 29 * KB,
+    "wide1": 30 * KB,
+    "gain": 30 * KB,
     "z32_1_0": 70 * KB,
     "z32_1_384": 70 * KB,
     "bias2_0": 74 * KB,
     "rounded4_0": 74 * KB,
     "raw0_0": 102 * KB,
     "v_w1_1": 102 * KB,
-    "bias1_1": 37 * KB,
-    "right0_256": 37 * KB,
-    "bias2_1": 38 * KB,
-    "right1_0": 38 * KB,
-    "right3_0": 29 * KB,
-    "rounded6_0": 32 * KB,
+    "right3_0": 32 * KB,
+    "rounded6_0": 35 * KB,
     "bias5_1": 50 * KB,
     "right4_0": 50 * KB,
     "bias6_1": 52 * KB,

@@ -39,9 +39,9 @@ PLACE = {
     "rounded3_1": 21 * KB + 256,
     "bias2_1": 22 * KB + 256,
     "right1_0": 21 * KB + 256,
-    "right2_0": 23 * KB,
-    "bias3": 24 * KB + 768,
-    "rounded6_1": 25 * KB,
+    "right2_0": 22 * KB + 768,
+    "bias3_1": 24 * KB + 512,
+    "rounded6_1": 24 * KB + 768,
     "rounded2": 108 * KB,
     "bias1_1": 111 * KB,
     "right0_256": 110 * KB + 512,
@@ -174,20 +174,20 @@ def tile_list_precedent_ladder_kernel(
 
         turned = [psum.tile([P, PACK, P], F32, name=f"bank{2 + b}") for b in range(2)]
         bias = sbuf("bias", [P, H_TILES], F32)
-        for t in range(PACK - 1):
+        for t in range(PACK):
             nc.tensor.transpose(turned[0][:, t, :], bias_rows[:, t * P : (t + 1) * P], identity[:])
         for t in range(PACK):
             nc.tensor.transpose(turned[1][:, t, :], bias_rows[:, t:PASS:PACK], identity[:])
-        nc.scalar.copy(bias[:, 0 : PACK - 1], turned[0][:, 0 : PACK - 1, 0])
-        nc.scalar.copy(bias[:, PACK:H_TILES], turned[1][:, :, 1])
+        for b in range(2):
+            nc.scalar.copy(bias[:, PACK * b : PACK * (b + 1)], turned[b][:, :, b])
         row_bias = {}
         for ht in range(H_TILES):
             for side in range(2):
                 row_bias[ht, side] = bias[:, ht : ht + 1]
                 if f"bias{ht}_{side}" in PLACE:
-                    held = sbuf(f"bias{ht}_{side}", [P, 1], F32)
-                    nc.gpsimd.tensor_copy(held[:], bias[:, ht : ht + 1])
-                    row_bias[ht, side] = held[:]
+                    held = sbuf(f"bias{ht}_{side}", [P, P if ht == 3 else 1], F32)[:, 0:1]
+                    nc.gpsimd.tensor_copy(held, bias[:, ht : ht + 1])
+                    row_bias[ht, side] = held
 
 
         operand, h, banks = {}, {}, {}
@@ -355,11 +355,8 @@ def tile_list_precedent_ladder_kernel(
 
         for u, a in ((2, 0), (3, 0), (2, 1)):
             raw[u, a] = new_raw(f"raw{u}_{a}", a, u * P, P)[:]
-        raw[3, 1] = new_raw("raw3_1", 1, 3 * P, P)[:]
         wide = [new_raw("wide0", 0, PASS, PASS)]
-        row_bias[3, 0] = row_bias[3, 1] = sbuf("bias3", [P, P], F32)[:, 0:1]
-        with nc.allow_non_contiguous_dma(reason="one value of the bias a partition"):
-            nc.sync.dma_start(row_bias[3, 0], b1[3 * P : PASS].rearrange("(p one) -> p one", one=1))
+        raw[3, 1] = new_raw("raw3_1", 1, 3 * P, P)[:]
         wide.append(new_raw("wide1", 1, PASS, PASS))
         w4_w = sbuf("w4_w", [P, 2, 2 * N], U8)
         w4_s = sbuf("w4_s", [P, 2, N], U8)

@@ -34,7 +34,6 @@ KB = 1024
 
 PLACE = {
     "tab_w0": 4 * KB + 512,
-    "raw3_0": 9 * KB + 256,
     "bias1_0": 21 * KB + 256,
     "rounded3_1": 21 * KB + 256,
     "bias2_1": 22 * KB + 256,
@@ -48,15 +47,15 @@ PLACE = {
     "raw2_1": 3 * KB,
     "h1": 0,
     "z0_0": 4 * KB,
-    "raw2_0": 5 * KB + 256,
+    "near0": 5 * KB,
     "raw1_0": 81 * KB,
     "h0": 78 * KB,
     "raw1_1": 83 * KB,
     "picked0_0": 83 * KB,
     "picked0_256": 84 * KB,
-    "raw3_1": 7 * KB + 256,
-    "z0_256": 7 * KB + 256,
-    "h2": 8 * KB + 256,
+    "raw3_1": 9 * KB,
+    "z0_256": 10 * KB,
+    "h2": 6 * KB,
     "tab_s": 82 * KB,
     "raw0_1": 104 * KB,
     "v_w1_2": 104 * KB,
@@ -353,8 +352,9 @@ def tile_list_precedent_ladder_kernel(
         gather_words(1, "v_w1_2", S - HALF, S)
         multiply_w(0, 1)
 
-        for u, a in ((2, 0), (3, 0), (2, 1)):
-            raw[u, a] = new_raw(f"raw{u}_{a}", a, u * P, P)[:]
+        near0 = new_raw("near0", 0, 2 * P, 2 * P)
+        raw[2, 0], raw[3, 0] = near0[:, :, 0:P], near0[:, :, P : 2 * P]
+        raw[2, 1] = new_raw("raw2_1", 1, 2 * P, P)[:]
         wide = [new_raw("wide0", 0, PASS, PASS)]
         raw[3, 1] = new_raw("raw3_1", 1, 3 * P, P)[:]
         wide.append(new_raw("wide1", 1, PASS, PASS))

@@ -67,8 +67,6 @@ PLACE = {
     "w4_s": 29 * KB,
     "wide1": 30 * KB,
     "gain": 30 * KB,
-    "z32_1_0": 70 * KB,
-    "z32_1_384": 70 * KB,
     "bias2_0": 74 * KB,
     "rounded4_0": 74 * KB,
     "raw0_0": 102 * KB,
@@ -81,16 +79,18 @@ PLACE = {
     "right5_0": 52 * KB,
     "bias7_1": 54 * KB,
     "right6_0": 54 * KB,
-    "z_bf_last": 54 * KB,
     "bias7_0": 56 * KB,
     "z_bf0": 56 * KB,
-    "picked7_0": 60 * KB,
-    "z32_1_256": 60 * KB,
     "z32_0": 62 * KB,
     "right7_0": 62 * KB,
     "z_code0_256": 62 * KB,
     "right7_256": 63 * KB,
-    "z_code1_256": 63 * KB,
+    "z_bf1_0": 64 * KB,
+    "z_bf1_256": 66 * KB,
+    "picked7_0": 60 * KB,
+    "z_high256": 60 * KB,
+    "z_high0": 70 * KB,
+    "z_code1_256": 71 * KB,
 }
 
 
@@ -281,11 +281,6 @@ def tile_list_precedent_ladder_kernel(
             gather_left(u, c0, c1, z[:])
             nc.sync.dma_start(z32[0, 0][QUAD * u : QUAD * (u + 1), :, c0:c1], z[:])
 
-        def wide_left(ht, c0, c1):
-            if (1, c0) not in z32:
-                z32[1, c0] = sbuf(f"z32_1_{c0}", [P, PACK, c1 - c0], F32)
-            gather_left(ht, c0, c1, z32[1, c0][:, ht % PACK, :])
-
         def round_z(b, c0, values, rounded=None):
             if rounded is None:
                 tile = sbuf(f"z_bf{b}_{c0}", [P, values.shape[2] * PACK], BF16)
@@ -314,7 +309,7 @@ def tile_list_precedent_ladder_kernel(
 
         def multiply_tile(b, c0, i):
             codes, scales, width = z_mx[b, c0]
-            step = HALF if c0 == 0 else QUARTER
+            step = QUARTER if i < Y_TILES - 1 and c0 == HALF else HALF
             for c in range(0, width, step):
                 n, span, column = y_place(i, c0 + c)
                 if n not in y_banks:
@@ -399,38 +394,45 @@ def tile_list_precedent_ladder_kernel(
             nc.sync.dma_start(gain[:], gn.rearrange("(i p) -> p i", p=P))
         prepare_wide(6, 0)
 
+        z_low = sbuf("z_low", [P, 2, PAIRS], F32)
+        z_high = [sbuf(f"z_high{c0}", [P, 2, HALF], F32) for c0 in (0, HALF)]
+        z_pairs = [sbuf(f"z_bf1_{c0}", [P, HALF, PACK], BF16) for c0 in (0, HALF)]
+
+        def wide_left(ht, c0, c1):
+            target = z_low[:, ht % 2, c0:c1] if ht < 6 else z_high[c0 // HALF][:, ht % 2, :]
+            gather_left(ht, c0, c1, target)
+
+        def round_pair(side, t0, copy):
+            values = z_high[side][:] if t0 else z_low[:, :, side * HALF : (side + 1) * HALF]
+            copy(
+                out=z_pairs[side][:, :, t0 : t0 + 2].rearrange("p (c i) t -> p c t i", i=LINE),
+                in_=values.rearrange("p t (c i) -> p c t i", i=LINE),
+            )
+            z_bf[1, side * HALF] = z_pairs[side][:].rearrange("p c t -> p (c t)")
+
         empty_h(4)
         gather_right(4)
-        for ht in (5, 6, 7):
+        for ht in (5, 6):
             step(ht)
-            wide_left(ht - 1, 0, HALF)
+            wide_left(ht - 1, 0, PAIRS)
+        step(7)
         whole = sbuf("z_bf0", [P, PAIRS * PACK], BF16)
         for c0 in (0, HALF):
             round_z(0, c0, z32[0, 0][:, :, c0 : c0 + HALF], whole[:, c0 * PACK : (c0 + HALF) * PACK])
-        multiply_z(0, 0)
+        round_pair(0, 0, nc.scalar.copy)
         positive_part(7, 0, HALF, True)
         positive_part(7, HALF, PAIRS, True)
+        round_pair(1, 0, nc.scalar.copy)
+        wide_left(6, 0, HALF)
+        multiply_z(0, 0)
         wide_left(7, 0, HALF)
-        round_z(1, 0, z32[1, 0][:])
+        round_pair(0, 2, nc.scalar.copy)
+        wide_left(6, HALF, PAIRS)
         multiply_z(0, HALF)
-        for ht in range(PACK, H_TILES):
-            wide_left(ht, HALF, LAST)
-        round_z(1, HALF, z32[1, HALF][:])
+        wide_left(7, HALF, PAIRS)
         multiply_z(1, 0)
-        for ht in range(PACK, H_TILES):
-            wide_left(ht, LAST, PAIRS)
-        last_bf = sbuf("z_bf_last", [P, QUARTER, PACK], BF16)
-        for t0 in (0, 2):
-            nc.vector.tensor_copy(
-                out=last_bf[:, :, t0 : t0 + 2].rearrange("p (c i) t -> p c t i", i=LINE),
-                in_=z32[1, LAST][:, t0 : t0 + 2, :].rearrange("p t (c i) -> p c t i", i=LINE),
-            )
-        z_bf[1, LAST] = last_bf[:].rearrange("p c t -> p (c t)")
-        quantize_z(1, HALF)
-        quantize_z(1, LAST)
-        for i in range(Y_TILES):
-            for c0 in (HALF, LAST):
-                multiply_tile(1, c0, i)
+        round_pair(1, 2, nc.vector.tensor_copy)
+        multiply_z(1, HALF)
 
         y = [sbuf(f"y{i}", [P, PAIRS], F32) for i in range(Y_TILES)]
         nc.scalar.copy(y[0][:, 0:HALF], y_banks[0][:])

@@ -31,31 +31,33 @@ F32_MAX = 3.4028234663852886e38
 HALF, QUARTER = PAIRS // 2, PAIRS // 4
 LAST = PAIRS - QUARTER
 KB = 1024
+FIRST = 192
+WARM_UPS = 3
 
 PLACE = {
     "tab_w0": 4 * KB + 512,
-    "bias1_0": 21 * KB + 256,
-    "rounded3_1": 21 * KB + 256,
-    "bias2_1": 22 * KB + 256,
-    "right1_0": 21 * KB + 256,
-    "right2_0": 22 * KB + 768,
-    "bias3_1": 24 * KB + 512,
-    "rounded6_1": 24 * KB + 768,
-    "rounded2": 108 * KB,
-    "bias1_1": 111 * KB,
-    "right0_256": 110 * KB + 512,
-    "raw2_1": 3 * KB,
     "h1": 0,
-    "z0_0": 4 * KB,
-    "near0": 5 * KB,
+    "late_bias2": 105 * KB + 256,
+    "right1_0": 105 * KB + 512,
+    "rounded3_1": 107 * KB + 256,
+    "bias1_0": 108 * KB,
+    "rounded4_0": 108 * KB,
+    "right2_0": 109 * KB + 256,
+    "bias3_1": 111 * KB,
+    "rounded6_1": 111 * KB + 256,
+    "rounded2": 114 * KB,
+    "right0_192": 116 * KB + 512,
+    "bias1_1": 117 * KB,
+    "near0": 1 * KB,
+    "raw2_1": 5 * KB,
+    "z0_0": 5 * KB,
+    "raw3_1": 7 * KB,
+    "z0_192": 7 * KB,
     "raw1_0": 81 * KB,
     "h0": 78 * KB,
     "raw1_1": 83 * KB,
     "picked0_0": 83 * KB,
-    "picked0_256": 84 * KB,
-    "raw3_1": 9 * KB,
-    "z0_256": 10 * KB,
-    "h2": 6 * KB,
+    "picked0_192": 84 * KB,
     "tab_s": 82 * KB,
     "raw0_1": 104 * KB,
     "v_w1_2": 104 * KB,
@@ -67,8 +69,6 @@ PLACE = {
     "w4_s": 29 * KB,
     "wide1": 30 * KB,
     "gain": 30 * KB,
-    "bias2_0": 74 * KB,
-    "rounded4_0": 74 * KB,
     "raw0_0": 102 * KB,
     "v_w1_1": 102 * KB,
     "right3_0": 32 * KB,
@@ -188,6 +188,17 @@ def tile_list_precedent_ladder_kernel(
                     nc.gpsimd.tensor_copy(held, bias[:, ht : ht + 1])
                     row_bias[ht, side] = held
 
+        idle = psum.tile([P, BANK], F32, name="bank3")
+        for warm_up in range(WARM_UPS):
+            nc.tensor.matmul_mx(
+                out=idle[:],
+                lhsT=words[0][0][0][:, 0:P].bitcast(FP8X4),
+                lhsT_scale=v_rows[:, 0:P],
+                rhs=words[0][0][0][:, 0:BANK].bitcast(FP8X4),
+                rhs_scale=v_rows[:, 0:BANK],
+                start=True,
+                stop=True,
+            )
 
         operand, h, banks = {}, {}, {}
 
@@ -272,7 +283,7 @@ def tile_list_precedent_ladder_kernel(
                 engine.tensor_scalar(right[ht, c0][:], values, F32_MAX, 0.0, op0=ALU.min, op1=ALU.max)
 
         def gather_left(ht, c0, c1, target):
-            first = HALF if c0 >= HALF and (ht, HALF) in right else 0
+            first = max(c for t, c in right if t == ht and c <= c0)
             plain = right[ht, first][:, c0 - first : c1 - first]
             nc.vector.tensor_tensor(target, h[ht][:].indirect(entries(p1, c0, c1)), plain, ALU.subtract)
 
@@ -352,6 +363,10 @@ def tile_list_precedent_ladder_kernel(
         raw[2, 1] = new_raw("raw2_1", 1, 2 * P, P)[:]
         wide = [new_raw("wide0", 0, PASS, PASS)]
         raw[3, 1] = new_raw("raw3_1", 1, 3 * P, P)[:]
+        late = sbuf("late_bias2", [P, P], F32)[:, 0:1]
+        with nc.allow_non_contiguous_dma(reason="one bias a partition"):
+            nc.sync.dma_start(late, b1[2 * P : 3 * P].rearrange("(p o) -> p o", o=1))
+        row_bias[2, 0] = row_bias[2, 1] = late
         wide.append(new_raw("wide1", 1, PASS, PASS))
         w4_w = sbuf("w4_w", [P, 2, 2 * N], U8)
         w4_s = sbuf("w4_s", [P, 2, N], U8)
@@ -365,20 +380,20 @@ def tile_list_precedent_ladder_kernel(
         prepare_near(1, 0)
         empty_h(0)
         prepare_near(1, 1)
-        gather_right(0, 0, HALF)
-        gather_right(0, HALF, PAIRS)
-        positive_part(0, 0, HALF)
+        gather_right(0, 0, FIRST)
+        gather_right(0, FIRST, PAIRS)
+        positive_part(0, 0, FIRST)
         parts = [(2, 0), (3, 0), (2, 1)]
         rounded2 = sbuf("rounded2", [P, len(parts), P, PACK], BF16)
         for part, (u, a) in enumerate(parts):
             round_near(u, a, rounded2, part)
         quantize_w1("2", rounded2[:], parts)
-        near_left(0, 0, HALF)
+        near_left(0, 0, FIRST)
         empty_h(1)
         gather_right(1)
-        positive_part(0, HALF, PAIRS)
+        positive_part(0, FIRST, PAIRS)
         prepare_near(3, 1)
-        near_left(0, HALF, PAIRS)
+        near_left(0, FIRST, PAIRS)
         step(2)
         near_left(1)
         prepare_wide(4, 0)

@@ -349,7 +349,7 @@ def tile_list_precedent_ladder_kernel(
         def step(ht):
             empty_h(ht)
             gather_right(ht)
-            positive_part(ht - 1)
+            positive_part(ht - 1, on_scalar=ht == 5)
 
         prepare_near(0, 0)
         gather_words(1, "v_w1_1", BANK, S - HALF)

@@ -23,6 +23,7 @@ PASS = P * PACK
 BANK = 512
 QUADS = 4
 QUAD = P // QUADS
+SCALE_ROWS = 4
 PER_COLUMN = 16
 LINE = 4
 Y_TILES = N // P
@@ -30,47 +31,29 @@ H_TILES = H // P
 F32_MAX = 3.4028234663852886e38
 HALF, QUARTER = PAIRS // 2, PAIRS // 4
 LAST = PAIRS - QUARTER
-KB = 1024
 FIRST = 192
 WARM_UPS = 3
+LATE_TILE = 2
+TURNED = [u for u in range(PACK) if u != LATE_TILE]
+TWICE_REUSED = 3
+KB = 1024
 
 PLACE = {
     "tab_w0": 4 * KB + 512,
-    "h1": 0,
-    "late_bias2": 105 * KB + 256,
-    "right1_0": 105 * KB + 512,
-    "rounded3_1": 107 * KB + 256,
-    "bias1_0": 108 * KB,
-    "rounded4_0": 108 * KB,
-    "right2_0": 109 * KB + 256,
-    "bias3_1": 111 * KB,
-    "rounded6_1": 111 * KB + 256,
-    "rounded2": 114 * KB,
-    "right0_192": 116 * KB + 512,
-    "bias1_1": 117 * KB,
     "near0": 1 * KB,
     "raw2_1": 5 * KB,
-    "z0_0": 5 * KB,
     "raw3_1": 7 * KB,
-    "z0_192": 7 * KB,
-    "raw1_0": 81 * KB,
-    "h0": 78 * KB,
-    "raw1_1": 83 * KB,
-    "picked0_0": 83 * KB,
-    "picked0_192": 84 * KB,
-    "tab_s": 82 * KB,
-    "raw0_1": 104 * KB,
-    "v_w1_2": 104 * KB,
-    "tab_w1": 25 * KB,
     "wide0": 12 * KB + 256,
+    "h1": 0,
+    "z0_0": 5 * KB,
+    f"z0_{FIRST}": 7 * KB,
     "h4": 12 * KB + 256,
     "h5": 16 * KB + 256,
+    "tab_w1": 25 * KB,
     "w4_w": 27 * KB,
     "w4_s": 29 * KB,
     "wide1": 30 * KB,
     "gain": 30 * KB,
-    "raw0_0": 102 * KB,
-    "v_w1_1": 102 * KB,
     "right3_0": 32 * KB,
     "rounded6_0": 35 * KB,
     "bias5_1": 50 * KB,
@@ -81,16 +64,37 @@ PLACE = {
     "right6_0": 54 * KB,
     "bias7_0": 56 * KB,
     "z_bf0": 56 * KB,
+    "picked7_0": 60 * KB,
+    f"z_high{HALF}": 60 * KB,
     "z32_0": 62 * KB,
     "right7_0": 62 * KB,
-    "z_code0_256": 62 * KB,
-    "right7_256": 63 * KB,
+    f"right7_{HALF}": 63 * KB,
     "z_bf1_0": 64 * KB,
-    "z_bf1_256": 66 * KB,
-    "picked7_0": 60 * KB,
-    "z_high256": 60 * KB,
+    f"z_bf1_{HALF}": 66 * KB,
+    f"z_code0_{HALF}": 62 * KB,
     "z_high0": 70 * KB,
-    "z_code1_256": 71 * KB,
+    f"z_code1_{HALF}": 71 * KB,
+    "tab_s": 82 * KB,
+    "raw1_0": 81 * KB,
+    "raw1_1": 83 * KB,
+    "h0": 78 * KB,
+    "picked0_0": 83 * KB,
+    f"picked0_{FIRST}": 84 * KB,
+    "raw0_0": 102 * KB,
+    "v_w1_1": 102 * KB,
+    "raw0_1": 104 * KB,
+    "v_w1_2": 104 * KB,
+    "late_bias": 105 * KB + 256,
+    "right1_0": 105 * KB + 512,
+    "rounded3_1": 107 * KB + 256,
+    "bias1_0": 108 * KB,
+    "rounded4_0": 108 * KB,
+    "right2_0": 109 * KB + 256,
+    "bias3_1": 111 * KB,
+    "rounded6_1": 111 * KB + 256,
+    "rounded2": 114 * KB,
+    f"right0_{FIRST}": 116 * KB + 512,
+    "bias1_1": 117 * KB,
 }
 
 
@@ -119,14 +123,11 @@ def tile_list_precedent_ladder_kernel(
             nc.sync.dma_start(tile[:], tab_words[a].rearrange("p t i -> p (t i)").bitcast(I32))
             return tile
 
-        def load_w1(target, a, c0, width):
+        def load_w1(name, a, c0, width):
+            tile = sbuf(name, [P, PACK, width], F32)
             rows = w1[a * PASS : (a + 1) * PASS, c0 : c0 + width]
-            nc.sync.dma_start(target, rows.rearrange("(p j) c -> p j c", j=PACK))
-
-        def new_raw(name, a, c0, width):
-            raw = sbuf(name, [P, PACK, width], F32)
-            load_w1(raw[:], a, c0, width)
-            return raw
+            nc.sync.dma_start(tile[:], rows.rearrange("(p j) c -> p j c", j=PACK))
+            return tile
 
         bias_rows = sbuf("bias_rows", [P, PASS], F32)
         tab_s = sbuf("tab_s", [P, T], U8)
@@ -137,10 +138,11 @@ def tile_list_precedent_ladder_kernel(
         make_identity(nc, identity[:])
         nc.scalar.dma_start(bias_rows[0:2, :], b1.rearrange("(b c) -> b c", b=2))
 
+        rows_of_pass = QUADS * SCALE_ROWS
         for a in range(2):
             nc.sync.dma_start(
-                tab_s[16 * a : 16 * (a + 1), :].bitcast(I32),
-                tab_scales[a].rearrange("(q r) c -> r q c", r=4).bitcast(I32),
+                tab_s[rows_of_pass * a : rows_of_pass * (a + 1), :].bitcast(I32),
+                tab_scales[a].rearrange("(q r) c -> r q c", r=SCALE_ROWS).bitcast(I32),
             )
         idx = load_list(offs, "idx")
         p2 = load_list(pos2, "p2")
@@ -149,7 +151,7 @@ def tile_list_precedent_ladder_kernel(
         p3 = load_list(pos3, "p3")
         p4 = load_list(pos4, "p4")
         tab_w.append(load_table_words(1))
-        raw = {(0, a): new_raw(f"raw0_{a}", a, 0, P)[:] for a in range(2)}
+        raw = {(0, a): load_w1(f"raw0_{a}", a, 0, P)[:] for a in range(2)}
 
         words = {0: [], 1: []}
 
@@ -165,36 +167,40 @@ def tile_list_precedent_ladder_kernel(
         v_s = sbuf("v_s", [P, S], U8)
         nc.vector.tensor_copy(v_rows[:], tab_s[:].indirect(idx[:]))
         for q in range(QUADS):
-            nc.sync.dma_start(v_s[QUAD * q : QUAD * q + 8, :].bitcast(I32), v_rows[q:QUAD:4, :].bitcast(I32))
+            nc.sync.dma_start(
+                v_s[QUAD * q : QUAD * q + 2 * SCALE_ROWS, :].bitcast(I32), v_rows[q:QUAD:QUADS, :].bitcast(I32)
+            )
         for a in range(2):
-            raw[1, a] = new_raw(f"raw1_{a}", a, P, P)[:]
+            raw[1, a] = load_w1(f"raw1_{a}", a, P, P)[:]
         gather_words(0, "v_w0", 0, S)
         gather_words(1, "v_w1_0", 0, BANK)
 
-        turned = [psum.tile([P, PACK, P], F32, name=f"bank{2 + b}") for b in range(2)]
-        bias = sbuf("bias", [P, H_TILES], F32)
+        turned_near = psum.tile([P, len(TURNED), P], F32, name="bank2")
+        turned_wide = psum.tile([P, PACK, P], F32, name="bank3")
+        bias = sbuf("bias", [P, len(TURNED) + PACK], F32)
+        for n, u in enumerate(TURNED):
+            nc.tensor.transpose(turned_near[:, n, :], bias_rows[:, u * P : (u + 1) * P], identity[:])
         for t in range(PACK):
-            nc.tensor.transpose(turned[0][:, t, :], bias_rows[:, t * P : (t + 1) * P], identity[:])
-        for t in range(PACK):
-            nc.tensor.transpose(turned[1][:, t, :], bias_rows[:, t:PASS:PACK], identity[:])
-        for b in range(2):
-            nc.scalar.copy(bias[:, PACK * b : PACK * (b + 1)], turned[b][:, :, b])
+            nc.tensor.transpose(turned_wide[:, t, :], bias_rows[:, t:PASS:PACK], identity[:])
+        nc.scalar.copy(bias[:, 0 : len(TURNED)], turned_near[:, :, 0])
+        nc.scalar.copy(bias[:, len(TURNED) :], turned_wide[:, :, 1])
         row_bias = {}
-        for ht in range(H_TILES):
+        for n, ht in enumerate(TURNED + list(range(PACK, H_TILES))):
             for side in range(2):
-                row_bias[ht, side] = bias[:, ht : ht + 1]
+                row_bias[ht, side] = bias[:, n : n + 1]
                 if f"bias{ht}_{side}" in PLACE:
-                    held = sbuf(f"bias{ht}_{side}", [P, P if ht == 3 else 1], F32)[:, 0:1]
-                    nc.gpsimd.tensor_copy(held, bias[:, ht : ht + 1])
+                    held = sbuf(f"bias{ht}_{side}", [P, P if ht == TWICE_REUSED else 1], F32)[:, 0:1]
+                    nc.gpsimd.tensor_copy(held, bias[:, n : n + 1])
                     row_bias[ht, side] = held
 
+        first_words = words[0][0][0]
         idle = psum.tile([P, BANK], F32, name="bank3")
         for warm_up in range(WARM_UPS):
             nc.tensor.matmul_mx(
                 out=idle[:],
-                lhsT=words[0][0][0][:, 0:P].bitcast(FP8X4),
+                lhsT=first_words[:, 0:P].bitcast(FP8X4),
                 lhsT_scale=v_rows[:, 0:P],
-                rhs=words[0][0][0][:, 0:BANK].bitcast(FP8X4),
+                rhs=first_words[:, 0:BANK].bitcast(FP8X4),
                 rhs_scale=v_rows[:, 0:BANK],
                 start=True,
                 stop=True,
@@ -221,7 +227,7 @@ def tile_list_precedent_ladder_kernel(
                             lhsT=operand[ht, a][0].bitcast(FP8X4),
                             lhsT_scale=operand[ht, a][1],
                             rhs=tile[:, f0 - c0 : f1 - c0].bitcast(FP8X4),
-                            rhs_scale=v_s[4 * a : P, f0:f1],
+                            rhs_scale=v_s[SCALE_ROWS * a : P, f0:f1],
                             start=(opens and f0 == e0),
                             stop=(not opens and f1 == e1),
                         )
@@ -249,9 +255,8 @@ def tile_list_precedent_ladder_kernel(
             )
             return rounded
 
-        def round_wide(ht, a, rounded=None):
-            if rounded is None:
-                rounded = sbuf(f"rounded{ht}_{a}", [P, 2, P, PACK], BF16)[:]
+        def round_wide(ht, a):
+            rounded = sbuf(f"rounded{ht}_{a}", [P, 2, P, PACK], BF16)[:]
             nc.scalar.copy(
                 out=rounded.rearrange("p t m j -> p m j t"),
                 in_=wide[a][:].rearrange("p j (m t) -> p m j t", t=PACK)[:, :, :, ht - PACK : ht - PACK + 2],
@@ -264,10 +269,10 @@ def tile_list_precedent_ladder_kernel(
                 if ht == 0:
                     nc.vector.tensor_scalar(h[ht][:, e0:e1], banks[ht][side][:], row_bias[ht, 0], None, op0=ALU.add)
                 else:
-                    nc.scalar.activation(h[ht][:, e0:e1], banks[ht][side][:], ACT.Identity, bias=row_bias[ht, side % 2])
+                    nc.scalar.activation(h[ht][:, e0:e1], banks[ht][side][:], ACT.Identity, bias=row_bias[ht, side])
 
-        picked, right, z32, z_bf = {}, {}, {}, {}
-        z32[0, 0] = sbuf("z32_0", [P, PACK, PAIRS], F32)
+        picked, right, z_bf = {}, {}, {}
+        z_near = sbuf("z32_0", [P, PACK, PAIRS], F32)
 
         def gather_right(ht, c0=0, c1=PAIRS):
             picked[ht, c0] = sbuf(f"picked{ht}_{c0}", [P, c1 - c0], F32)
@@ -290,17 +295,7 @@ def tile_list_precedent_ladder_kernel(
         def near_left(u, c0=0, c1=PAIRS):
             z = sbuf(f"z{u}_{c0}", [P, c1 - c0], F32)
             gather_left(u, c0, c1, z[:])
-            nc.sync.dma_start(z32[0, 0][QUAD * u : QUAD * (u + 1), :, c0:c1], z[:])
-
-        def round_z(b, c0, values, rounded=None):
-            if rounded is None:
-                tile = sbuf(f"z_bf{b}_{c0}", [P, values.shape[2] * PACK], BF16)
-                rounded = tile[:]
-            z_bf[b, c0] = rounded
-            nc.scalar.copy(
-                out=z_bf[b, c0].rearrange("p (c i t) -> p c t i", i=LINE, t=PACK),
-                in_=values.rearrange("p t (c i) -> p c t i", i=LINE),
-            )
+            nc.sync.dma_start(z_near[QUAD * u : QUAD * (u + 1), :, c0:c1], z[:])
 
         y_banks, z_mx = {}, {}
 
@@ -346,10 +341,10 @@ def tile_list_precedent_ladder_kernel(
         def prepare_wide(ht, a):
             quantize_w1(f"{ht}_{a}", round_wide(ht, a), [(ht, a), (ht + 1, a)])
 
-        def step(ht):
+        def next_tile(ht, on_scalar=False):
             empty_h(ht)
             gather_right(ht)
-            positive_part(ht - 1, on_scalar=ht == 5)
+            positive_part(ht - 1, on_scalar=on_scalar)
 
         prepare_near(0, 0)
         gather_words(1, "v_w1_1", BANK, S - HALF)
@@ -358,23 +353,23 @@ def tile_list_precedent_ladder_kernel(
         gather_words(1, "v_w1_2", S - HALF, S)
         multiply_w(0, 1)
 
-        near0 = new_raw("near0", 0, 2 * P, 2 * P)
+        near0 = load_w1("near0", 0, 2 * P, 2 * P)
         raw[2, 0], raw[3, 0] = near0[:, :, 0:P], near0[:, :, P : 2 * P]
-        raw[2, 1] = new_raw("raw2_1", 1, 2 * P, P)[:]
-        wide = [new_raw("wide0", 0, PASS, PASS)]
-        raw[3, 1] = new_raw("raw3_1", 1, 3 * P, P)[:]
-        late = sbuf("late_bias2", [P, P], F32)[:, 0:1]
+        raw[2, 1] = load_w1("raw2_1", 1, 2 * P, P)[:]
+        wide = [load_w1("wide0", 0, PASS, PASS)]
+        raw[3, 1] = load_w1("raw3_1", 1, 3 * P, P)[:]
+        late_bias = sbuf("late_bias", [P, P], F32)[:, 0:1]
         with nc.allow_non_contiguous_dma(reason="one bias a partition"):
-            nc.sync.dma_start(late, b1[2 * P : 3 * P].rearrange("(p o) -> p o", o=1))
-        row_bias[2, 0] = row_bias[2, 1] = late
-        wide.append(new_raw("wide1", 1, PASS, PASS))
+            nc.sync.dma_start(late_bias, b1[LATE_TILE * P : (LATE_TILE + 1) * P].rearrange("(p o) -> p o", o=1))
+        row_bias[LATE_TILE, 0] = row_bias[LATE_TILE, 1] = late_bias
+        wide.append(load_w1("wide1", 1, PASS, PASS))
         w4_w = sbuf("w4_w", [P, 2, 2 * N], U8)
         w4_s = sbuf("w4_s", [P, 2, N], U8)
         nc.sync.dma_start(w4_w[:].bitcast(I32), w4_words.rearrange("a p c -> p a c").bitcast(I32))
         for q in range(QUADS):
             nc.sync.dma_start(
-                w4_s[QUAD * q : QUAD * q + 4, :, :].bitcast(I32),
-                w4_scales[:, 4 * q : 4 * q + 4, :].rearrange("a r c -> r a c").bitcast(I32),
+                w4_s[QUAD * q : QUAD * q + SCALE_ROWS, :, :].bitcast(I32),
+                w4_scales[:, SCALE_ROWS * q : SCALE_ROWS * (q + 1), :].rearrange("a r c -> r a c").bitcast(I32),
             )
 
         prepare_near(1, 0)
@@ -394,10 +389,10 @@ def tile_list_precedent_ladder_kernel(
         positive_part(0, FIRST, PAIRS)
         prepare_near(3, 1)
         near_left(0, FIRST, PAIRS)
-        step(2)
+        next_tile(2)
         near_left(1)
         prepare_wide(4, 0)
-        step(3)
+        next_tile(3)
         near_left(2)
         prepare_wide(4, 1)
         waiting = round_wide(6, 1)
@@ -414,7 +409,7 @@ def tile_list_precedent_ladder_kernel(
         z_pairs = [sbuf(f"z_bf1_{c0}", [P, HALF, PACK], BF16) for c0 in (0, HALF)]
 
         def wide_left(ht, c0, c1):
-            target = z_low[:, ht % 2, c0:c1] if ht < 6 else z_high[c0 // HALF][:, ht % 2, :]
+            target = z_low[:, ht % 2, c0:c1] if ht < PACK + 2 else z_high[c0 // HALF][:, ht % 2, :]
             gather_left(ht, c0, c1, target)
 
         def round_pair(side, t0, copy):
@@ -427,16 +422,21 @@ def tile_list_precedent_ladder_kernel(
 
         empty_h(4)
         gather_right(4)
-        for ht in (5, 6):
-            step(ht)
-            wide_left(ht - 1, 0, PAIRS)
-        step(7)
-        whole = sbuf("z_bf0", [P, PAIRS * PACK], BF16)
+        next_tile(5, on_scalar=True)
+        wide_left(4, 0, PAIRS)
+        next_tile(6)
+        wide_left(5, 0, PAIRS)
+        next_tile(7)
+        near_bf = sbuf("z_bf0", [P, PAIRS * PACK], BF16)
         for c0 in (0, HALF):
-            round_z(0, c0, z32[0, 0][:, :, c0 : c0 + HALF], whole[:, c0 * PACK : (c0 + HALF) * PACK])
+            z_bf[0, c0] = near_bf[:, c0 * PACK : (c0 + HALF) * PACK]
+            nc.scalar.copy(
+                out=z_bf[0, c0].rearrange("p (c i t) -> p c t i", i=LINE, t=PACK),
+                in_=z_near[:, :, c0 : c0 + HALF].rearrange("p t (c i) -> p c t i", i=LINE),
+            )
         round_pair(0, 0, nc.scalar.copy)
-        positive_part(7, 0, HALF, True)
-        positive_part(7, HALF, PAIRS, True)
+        positive_part(7, 0, HALF, on_scalar=True)
+        positive_part(7, HALF, PAIRS, on_scalar=True)
         round_pair(1, 0, nc.scalar.copy)
         wide_left(6, 0, HALF)
         multiply_z(0, 0)

from contextlib import ExitStack

import concourse.mybir as mybir
from concourse.masks import make_identity

K, T, S, H, PAIRS, N, LINES = 1024, 2048, 1024, 1024, 512, 512, 256
FLOPS = 2 * K * H * S + 2 * H * N * PAIRS

F32 = mybir.dt.float32
BF16 = mybir.dt.bfloat16
I32 = mybir.dt.int32
U32 = mybir.dt.uint32
U16 = mybir.dt.uint16
U8 = mybir.dt.uint8
FP8X4 = mybir.dt.float8_e4m3fn_x4
FP4X4 = mybir.dt.float4_e2m1fn_x4
ACT = mybir.ActivationFunctionType
ALU = mybir.AluOpType

P = 128
PACK = 4
PASS = P * PACK
BANK = 512
QUADS = 4
QUAD = P // QUADS
SCALE_ROWS = 4
PER_COLUMN = 16
LINE = 4
Y_TILES = N // P
H_TILES = H // P
F32_MAX = 3.4028234663852886e38
HALF, QUARTER = PAIRS // 2, PAIRS // 4
LAST = PAIRS - QUARTER
FIRST = 192
WARM_UPS = 3
LATE_TILE = 2
TURNED = [u for u in range(PACK) if u != LATE_TILE]
TWICE_REUSED = 3
KB = 1024

PLACE = {
    "tab_w0": 4 * KB + 512,
    "near0": 1 * KB,
    "raw2_1": 5 * KB,
    "raw3_1": 7 * KB,
    "wide0": 12 * KB + 256,
    "h1": 0,
    "z0_0": 5 * KB,
    f"z0_{FIRST}": 7 * KB,
    "h4": 12 * KB + 256,
    "h5": 16 * KB + 256,
    "tab_w1": 25 * KB,
    "w4_w": 27 * KB,
    "w4_s": 29 * KB,
    "wide1": 30 * KB,
    "gain": 30 * KB,
    "right3_0": 32 * KB,
    "rounded6_0": 35 * KB,
    "bias5_1": 50 * KB,
    "right4_0": 50 * KB,
    "bias6_1": 52 * KB,
    "right5_0": 52 * KB,
    "bias7_1": 54 * KB,
    "right6_0": 54 * KB,
    "bias7_0": 56 * KB,
    "z_bf0": 56 * KB,
    "picked7_0": 60 * KB,
    f"z_high{HALF}": 60 * KB,
    "z32_0": 62 * KB,
    "right7_0": 62 * KB,
    f"right7_{HALF}": 63 * KB,
    "z_bf1_0": 64 * KB,
    f"z_bf1_{HALF}": 66 * KB,
    f"z_code0_{HALF}": 62 * KB,
    "z_high0": 70 * KB,
    f"z_code1_{HALF}": 71 * KB,
    "tab_s": 82 * KB,
    "raw1_0": 81 * KB,
    "raw1_1": 83 * KB,
    "h0": 78 * KB,
    "picked0_0": 83 * KB,
    f"picked0_{FIRST}": 84 * KB,
    "raw0_0": 102 * KB,
    "v_w1_1": 102 * KB,
    "raw0_1": 104 * KB,
    "v_w1_2": 104 * KB,
    "late_bias": 105 * KB + 256,
    "right1_0": 105 * KB + 512,
    "rounded3_1": 107 * KB + 256,
    "bias1_0": 108 * KB,
    "rounded4_0": 108 * KB,
    "right2_0": 109 * KB + 256,
    "bias3_1": 111 * KB,
    "rounded6_1": 111 * KB + 256,
    "rounded2": 114 * KB,
    f"right0_{FIRST}": 116 * KB + 512,
    "bias1_1": 117 * KB,
}


def tile_list_precedent_ladder_kernel(
    tc, tab_words, tab_scales, offs, w1, b1, pos1, pos2, w4_words, w4_scales, pos3, pos4, gn, out
):
    nc = tc.nc
    with ExitStack() as ctx:
        lists = ctx.enter_context(tc.tile_pool(name="lists", bufs=1))
        keep = ctx.enter_context(tc.tile_pool(name="keep", bufs=1))
        reused = ctx.enter_context(tc.tile_pool(name="reused", bufs=1))
        psum = ctx.enter_context(tc.psum_pool(name="psum", bufs=1))

        def sbuf(name, shape, dtype):
            if name in PLACE:
                return reused.tile(shape, dtype, name=name, align_bytes=256, offset=PLACE[name])
            return keep.tile(shape, dtype, name=name, align_bytes=256)

        def load_list(src, name):
            tile = lists.tile(list(src.shape), U16, name=name)
            nc.sync.dma_start(tile[:], src)
            return tile

        def load_table_words(a):
            tile = sbuf(f"tab_w{a}", [P, T], I32)
            nc.sync.dma_start(tile[:], tab_words[a].rearrange("p t i -> p (t i)").bitcast(I32))
            return tile

        def load_w1(name, a, c0, width):
            tile = sbuf(name, [P, PACK, width], F32)
            rows = w1[a * PASS : (a + 1) * PASS, c0 : c0 + width]
            nc.sync.dma_start(tile[:], rows.rearrange("(p j) c -> p j c", j=PACK))
            return tile

        bias_rows = sbuf("bias_rows", [P, PASS], F32)
        tab_s = sbuf("tab_s", [P, T], U8)
        nc.vector.memset(bias_rows[:], 0.0)
        nc.vector.memset(tab_s[QUAD : 2 * QUAD, :].bitcast(I32), 0)
        nc.vector.memset(tab_s[2 * QUAD : P, :].bitcast(I32), 0)
        identity = sbuf("identity", [P, P], F32)
        make_identity(nc, identity[:])
        nc.scalar.dma_start(bias_rows[0:2, :], b1.rearrange("(b c) -> b c", b=2))

        rows_of_pass = QUADS * SCALE_ROWS
        for a in range(2):
            nc.sync.dma_start(
                tab_s[rows_of_pass * a : rows_of_pass * (a + 1), :].bitcast(I32),
                tab_scales[a].rearrange("(q r) c -> r q c", r=SCALE_ROWS).bitcast(I32),
            )
        idx = load_list(offs, "idx")
        p2 = load_list(pos2, "p2")
        tab_w = [load_table_words(0)]
        p1 = load_list(pos1, "p1")
        p3 = load_list(pos3, "p3")
        p4 = load_list(pos4, "p4")
        tab_w.append(load_table_words(1))
        raw = {(0, a): load_w1(f"raw0_{a}", a, 0, P)[:] for a in range(2)}

        words = {0: [], 1: []}

        def entries(tile, c0, c1):
            return tile[:, c0 // PER_COLUMN : c1 // PER_COLUMN]

        def gather_words(a, name, c0, c1):
            tile = sbuf(name, [P, c1 - c0], U32)
            nc.vector.tensor_copy(tile[:], tab_w[a][:].bitcast(U32).indirect(entries(idx, c0, c1)))
            words[a].append((tile, c0, c1))

        v_rows = sbuf("v_rows", [P, S], U8)
        v_s = sbuf("v_s", [P, S], U8)
        nc.vector.tensor_copy(v_rows[:], tab_s[:].indirect(idx[:]))
        for q in range(QUADS):
            nc.sync.dma_start(
                v_s[QUAD * q : QUAD * q + 2 * SCALE_ROWS, :].bitcast(I32), v_rows[q:QUAD:QUADS, :].bitcast(I32)
            )
        for a in range(2):
            raw[1, a] = load_w1(f"raw1_{a}", a, P, P)[:]
        gather_words(0, "v_w0", 0, S)
        gather_words(1, "v_w1_0", 0, BANK)

        turned_near = psum.tile([P, len(TURNED), P], F32, name="bank2")
        turned_wide = psum.tile([P, PACK, P], F32, name="bank3")
        bias = sbuf("bias", [P, len(TURNED) + PACK], F32)
        for n, u in enumerate(TURNED):
            nc.tensor.transpose(turned_near[:, n, :], bias_rows[:, u * P : (u + 1) * P], identity[:])
        for t in range(PACK):
            nc.tensor.transpose(turned_wide[:, t, :], bias_rows[:, t:PASS:PACK], identity[:])
        nc.scalar.copy(bias[:, 0 : len(TURNED)], turned_near[:, :, 0])
        nc.scalar.copy(bias[:, len(TURNED) :], turned_wide[:, :, 1])
        row_bias = {}
        for n, ht in enumerate(TURNED + list(range(PACK, H_TILES))):
            for side in range(2):
                row_bias[ht, side] = bias[:, n : n + 1]
                if f"bias{ht}_{side}" in PLACE:
                    held = sbuf(f"bias{ht}_{side}", [P, P if ht == TWICE_REUSED else 1], F32)[:, 0:1]
                    nc.gpsimd.tensor_copy(held, bias[:, n : n + 1])
                    row_bias[ht, side] = held

        first_words = words[0][0][0]
        idle = psum.tile([P, BANK], F32, name="bank3")
        for warm_up in range(WARM_UPS):
            nc.tensor.matmul_mx(
                out=idle[:],
                lhsT=first_words[:, 0:P].bitcast(FP8X4),
                lhsT_scale=v_rows[:, 0:P],
                rhs=first_words[:, 0:BANK].bitcast(FP8X4),
                rhs_scale=v_rows[:, 0:BANK],
                start=True,
                stop=True,
            )

        operand, h, banks = {}, {}, {}

        def spans(ht):
            if ht == 0:
                return [(n, i * HALF, (i + 1) * HALF) for i, n in enumerate((4, 5, 6, 7))]
            return [(2 * (ht % PACK), 0, BANK), (2 * (ht % PACK) + 1, BANK, S)]

        def multiply_w(ht, *passes):
            fresh = ht not in banks
            if fresh:
                banks[ht] = [psum.tile([P, e1 - e0], F32, name=f"bank{n}") for n, e0, e1 in spans(ht)]
            for bank, (n, e0, e1) in zip(banks[ht], spans(ht)):
                for a, (tile, c0, c1) in [(a, piece) for a in passes for piece in words[a]]:
                    opens = fresh and a == passes[0]
                    f0, f1 = max(e0, c0), min(e1, c1)
                    if f0 < f1:
                        nc.tensor.matmul_mx(
                            out=bank[:, f0 - e0 : f1 - e0],
                            lhsT=operand[ht, a][0].bitcast(FP8X4),
                            lhsT_scale=operand[ht, a][1],
                            rhs=tile[:, f0 - c0 : f1 - c0].bitcast(FP8X4),
                            rhs_scale=v_s[SCALE_ROWS * a : P, f0:f1],
                            start=(opens and f0 == e0),
                            stop=(not opens and f1 == e1),
                        )

        def quantize_only(name, rounded, parts):
            codes = sbuf(f"w_code{name}", [P, len(parts) * P], U32)
            scales = sbuf(f"w_scale{name}", [P, len(parts) * P], U8)
            values = rounded.rearrange("p t m j -> p (t m j)")
            nc.vector.quantize_mx(out=codes[:].bitcast(FP8X4), scales=scales[:], in_=values)
            for t, (ht, a) in enumerate(parts):
                columns = slice(t * P, (t + 1) * P)
                operand[ht, a] = (codes[:, columns], scales[:, columns])

        def quantize_w1(name, rounded, parts):
            quantize_only(name, rounded, parts)
            for ht in sorted({ht for ht, a in parts}):
                multiply_w(ht, *[a for t, a in parts if t == ht])

        def round_near(u, a, rounded=None, part=0):
            if rounded is None:
                rounded = sbuf(f"rounded{u}_{a}", [P, 1, P, PACK], BF16)[:]
            nc.scalar.copy(
                out=rounded[:, part].rearrange("p (c i) j -> p c j i", i=LINE),
                in_=raw[u, a].rearrange("p j (c i) -> p c j i", i=LINE),
            )
            return rounded

        def round_wide(ht, a):
            rounded = sbuf(f"rounded{ht}_{a}", [P, 2, P, PACK], BF16)[:]
            nc.scalar.copy(
                out=rounded.rearrange("p t m j -> p m j t"),
                in_=wide[a][:].rearrange("p j (m t) -> p m j t", t=PACK)[:, :, :, ht - PACK : ht - PACK + 2],
            )
            return rounded

        def empty_h(ht):
            h[ht] = sbuf(f"h{ht}", [P, S], F32)
            for side, (n, e0, e1) in enumerate(spans(ht)):
                if ht == 0:
                    nc.vector.tensor_scalar(h[ht][:, e0:e1], banks[ht][side][:], row_bias[ht, 0], None, op0=ALU.add)
                else:
                    nc.scalar.activation(h[ht][:, e0:e1], banks[ht][side][:], ACT.Identity, bias=row_bias[ht, side])

        picked, right, z_bf = {}, {}, {}
        z_near = sbuf("z32_0", [P, PACK, PAIRS], F32)

        def gather_right(ht, c0=0, c1=PAIRS):
            picked[ht, c0] = sbuf(f"picked{ht}_{c0}", [P, c1 - c0], F32)
            nc.vector.tensor_copy(picked[ht, c0][:], h[ht][:].indirect(entries(p2, c0, c1)))

        def positive_part(ht, c0=0, c1=PAIRS, on_scalar=False, engine=nc.gpsimd):
            right[ht, c0] = sbuf(f"right{ht}_{c0}", [P, c1 - c0], F32)
            first = c0 if (ht, c0) in picked else 0
            values = picked[ht, first][:, c0 - first : c1 - first]
            if on_scalar:
                nc.scalar.activation(right[ht, c0][:], values, ACT.Relu)
            else:
                engine.tensor_scalar(right[ht, c0][:], values, F32_MAX, 0.0, op0=ALU.min, op1=ALU.max)

        def gather_left(ht, c0, c1, target):
            first = max(c for t, c in right if t == ht and c <= c0)
            plain = right[ht, first][:, c0 - first : c1 - first]
            nc.vector.tensor_tensor(target, h[ht][:].indirect(entries(p1, c0, c1)), plain, ALU.subtract)

        def near_left(u, c0=0, c1=PAIRS):
            z = sbuf(f"z{u}_{c0}", [P, c1 - c0], F32)
            gather_left(u, c0, c1, z[:])
            nc.sync.dma_start(z_near[QUAD * u : QUAD * (u + 1), :, c0:c1], z[:])

        y_banks, z_mx = {}, {}

        def quantize_z(b, c0):
            width = z_bf[b, c0].shape[1] // PACK
            codes = sbuf(f"z_code{b}_{c0}", [P, width], U32)
            scales = sbuf(f"z_scale{b}_{c0}", [P, width], U8)
            nc.vector.quantize_mx(out=codes[:].bitcast(FP8X4), scales=scales[:], in_=z_bf[b, c0])
            z_mx[b, c0] = (codes, scales, width)

        def y_place(i, c):
            if i == 0:
                return {0: (0, HALF, 0), HALF: (4, QUARTER, 0), LAST: (5, QUARTER, 0)}[c]
            if i == Y_TILES - 1:
                return (i, PAIRS, c)
            return (i, LAST, c) if c < LAST else (5 + i, QUARTER, 0)

        def multiply_tile(b, c0, i):
            codes, scales, width = z_mx[b, c0]
            step = QUARTER if i < Y_TILES - 1 and c0 == HALF else HALF
            for c in range(0, width, step):
                n, span, column = y_place(i, c0 + c)
                if n not in y_banks:
                    y_banks[n] = psum.tile([P, span], F32, name=f"bank{n}")
                nc.tensor.matmul_mx(
                    out=y_banks[n][:, column : column + step],
                    lhsT=w4_w[:, b, 2 * P * i : 2 * P * (i + 1)].bitcast(FP4X4),
                    lhsT_scale=w4_s[:, b, P * i : P * (i + 1)],
                    rhs=codes[:, c : c + step].bitcast(FP8X4),
                    rhs_scale=scales[:, c : c + step],
                    start=(b == 0 and column == 0),
                    stop=(b == 1 and column + step == span),
                )

        def multiply_z(b, c0):
            quantize_z(b, c0)
            for i in range(Y_TILES):
                multiply_tile(b, c0, i)

        def prepare_near(u, a):
            quantize_w1(f"{u}_{a}", round_near(u, a), [(u, a)])

        def prepare_wide(ht, a):
            quantize_w1(f"{ht}_{a}", round_wide(ht, a), [(ht, a), (ht + 1, a)])

        def next_tile(ht, on_scalar=False):
            empty_h(ht)
            gather_right(ht)
            positive_part(ht - 1, on_scalar=on_scalar)

        prepare_near(0, 0)
        gather_words(1, "v_w1_1", BANK, S - HALF)
        waiting = round_near(0, 1)
        quantize_only("0_1", waiting, [(0, 1)])
        gather_words(1, "v_w1_2", S - HALF, S)
        multiply_w(0, 1)

        near0 = load_w1("near0", 0, 2 * P, 2 * P)
        raw[2, 0], raw[3, 0] = near0[:, :, 0:P], near0[:, :, P : 2 * P]
        raw[2, 1] = load_w1("raw2_1", 1, 2 * P, P)[:]
        wide = [load_w1("wide0", 0, PASS, PASS)]
        raw[3, 1] = load_w1("raw3_1", 1, 3 * P, P)[:]
        late_bias = sbuf("late_bias", [P, P], F32)[:, 0:1]
        with nc.allow_non_contiguous_dma(reason="one bias a partition"):
            nc.sync.dma_start(late_bias, b1[LATE_TILE * P : (LATE_TILE + 1) * P].rearrange("(p o) -> p o", o=1))
        row_bias[LATE_TILE, 0] = row_bias[LATE_TILE, 1] = late_bias
        wide.append(load_w1("wide1", 1, PASS, PASS))
        w4_w = sbuf("w4_w", [P, 2, 2 * N], U8)
        w4_s = sbuf("w4_s", [P, 2, N], U8)
        nc.sync.dma_start(w4_w[:].bitcast(I32), w4_words.rearrange("a p c -> p a c").bitcast(I32))
        for q in range(QUADS):
            nc.sync.dma_start(
                w4_s[QUAD * q : QUAD * q + SCALE_ROWS, :, :].bitcast(I32),
                w4_scales[:, SCALE_ROWS * q : SCALE_ROWS * (q + 1), :].rearrange("a r c -> r a c").bitcast(I32),
            )

        prepare_near(1, 0)
        empty_h(0)
        prepare_near(1, 1)
        gather_right(0, 0, FIRST)
        gather_right(0, FIRST, PAIRS)
        positive_part(0, 0, FIRST)
        parts = [(2, 0), (3, 0), (2, 1)]
        rounded2 = sbuf("rounded2", [P, len(parts), P, PACK], BF16)
        for part, (u, a) in enumerate(parts):
            round_near(u, a, rounded2, part)
        quantize_w1("2", rounded2[:], parts)
        near_left(0, 0, FIRST)
        empty_h(1)
        gather_right(1)
        positive_part(0, FIRST, PAIRS)
        prepare_near(3, 1)
        near_left(0, FIRST, PAIRS)
        next_tile(2)
        near_left(1)
        prepare_wide(4, 0)
        next_tile(3)
        near_left(2)
        prepare_wide(4, 1)
        waiting = round_wide(6, 1)
        positive_part(3, engine=nc.vector)
        quantize_w1("6_1", waiting, [(6, 1), (7, 1)])
        near_left(3)
        gain = sbuf("gain", [P, Y_TILES], F32)
        with nc.allow_non_contiguous_dma(reason="one gain a partition"):
            nc.sync.dma_start(gain[:], gn.rearrange("(i p) -> p i", p=P))
        prepare_wide(6, 0)

        z_low = sbuf("z_low", [P, 2, PAIRS], F32)
        z_high = [sbuf(f"z_high{c0}", [P, 2, HALF], F32) for c0 in (0, HALF)]
        z_pairs = [sbuf(f"z_bf1_{c0}", [P, HALF, PACK], BF16) for c0 in (0, HALF)]

        def wide_left(ht, c0, c1):
            target = z_low[:, ht % 2, c0:c1] if ht < PACK + 2 else z_high[c0 // HALF][:, ht % 2, :]
            gather_left(ht, c0, c1, target)

        def round_pair(side, t0, copy):
            values = z_high[side][:] if t0 else z_low[:, :, side * HALF : (side + 1) * HALF]
            copy(
                out=z_pairs[side][:, :, t0 : t0 + 2].rearrange("p (c i) t -> p c t i", i=LINE),
                in_=values.rearrange("p t (c i) -> p c t i", i=LINE),
            )
            z_bf[1, side * HALF] = z_pairs[side][:].rearrange("p c t -> p (c t)")

        empty_h(4)
        gather_right(4)
        next_tile(5, on_scalar=True)
        wide_left(4, 0, PAIRS)
        next_tile(6)
        wide_left(5, 0, PAIRS)
        next_tile(7)
        near_bf = sbuf("z_bf0", [P, PAIRS * PACK], BF16)
        for c0 in (0, HALF):
            z_bf[0, c0] = near_bf[:, c0 * PACK : (c0 + HALF) * PACK]
            nc.scalar.copy(
                out=z_bf[0, c0].rearrange("p (c i t) -> p c t i", i=LINE, t=PACK),
                in_=z_near[:, :, c0 : c0 + HALF].rearrange("p t (c i) -> p c t i", i=LINE),
            )
        round_pair(0, 0, nc.scalar.copy)
        positive_part(7, 0, HALF, on_scalar=True)
        positive_part(7, HALF, PAIRS, on_scalar=True)
        round_pair(1, 0, nc.scalar.copy)
        wide_left(6, 0, HALF)
        multiply_z(0, 0)
        wide_left(7, 0, HALF)
        round_pair(0, 2, nc.scalar.copy)
        wide_left(6, HALF, PAIRS)
        multiply_z(0, HALF)
        wide_left(7, HALF, PAIRS)
        multiply_z(1, 0)
        round_pair(1, 2, nc.vector.tensor_copy)
        multiply_z(1, HALF)

        y = [sbuf(f"y{i}", [P, PAIRS], F32) for i in range(Y_TILES)]
        nc.scalar.copy(y[0][:, 0:HALF], y_banks[0][:])
        nc.scalar.copy(y[0][:, HALF:LAST], y_banks[4][:])
        for i in range(1, Y_TILES):
            nc.scalar.copy(y[i][:, 0 : y_place(i, 0)[1]], y_banks[i][:])

        def empty_last(i):
            nc.vector.tensor_copy(y[i][:, LAST:PAIRS], y_banks[5 + i][:])

        empty_last(0)
        empty_last(1)
        first_line = {}

        def gather_first_line(i):
            first_line[i] = sbuf(f"first_line{i}", [P, LINES], F32)
            nc.vector.tensor_copy(first_line[i][:], y[i][:].indirect(p3[:]))

        def finish(i, c0, c1):
            both = sbuf(f"both{i}_{c0}", [P, c1 - c0], F32)
            nc.vector.tensor_tensor(both[:], y[i][:].indirect(entries(p4, c0, c1)), first_line[i][:, c0:c1], ALU.mult)
            result = sbuf(f"result{i}_{c0}", [P, c1 - c0], F32)
            nc.scalar.activation(result[:], both[:], ACT.Tanh, scale=gain[:, i : i + 1])
            nc.sync.dma_start(out[i * P : (i + 1) * P, c0:c1], result[:])

        gather_first_line(0)
        empty_last(2)
        for i in range(1, Y_TILES):
            gather_first_line(i)
            finish(i - 1, 0, LINES)
        finish(Y_TILES - 1, 0, LINES // 2)
        finish(Y_TILES - 1, LINES // 2, LINES)
